import numpy as np
import ml_dtypes


def mxq(x, axis, fmt="e4m3"):
    dtype, down = {"e4m3": (ml_dtypes.float8_e4m3fn, 7), "e5m2": (ml_dtypes.float8_e5m2, 14)}[fmt]
    v = np.moveaxis(np.asarray(x, np.float32).astype(ml_dtypes.bfloat16).astype(np.float64), axis, -1)
    blocks = v.reshape(v.shape[:-1] + (-1, 32))
    amax = np.abs(blocks).max(-1, keepdims=True)
    byte = np.maximum(np.where(amax > 0, np.frexp(amax)[1] - 1 + 127, 0) - down, 1)
    scale = np.exp2(byte - 127.0)
    codes = (blocks / scale).astype(np.float32).astype(dtype).astype(np.float64)
    return np.moveaxis((codes * scale).reshape(v.shape), -1, axis)


WIDE = False


def mx_kscale(k):
    if not WIDE:
        return np.ones(k)
    levels = np.array([10, -10, 5, -5, 0])
    if k % 512:
        return np.exp2(np.random.permutation(np.resize(levels, k // 32))).repeat(32)
    a = np.empty((k // 512, 16))
    for p in range(k // 512):
        a[p, :8] = np.random.permutation(np.resize(levels, 8))
        for g in range(8):
            far = levels[np.abs(levels - a[p, g]) >= 10]
            a[p, g + 8] = far[np.random.randint(len(far))]
    return np.exp2(a.ravel()).repeat(32)


def f64(x):
    return np.asarray(x).astype(np.float64)


def striped(idx):
    return np.tile(idx.reshape(-1, 16).T, (8, 1)).astype(np.uint16)


def unstriped(offs):
    return offs[:16].T.reshape(-1).astype(np.int64)


E2M1 = np.array([0.0, 0.5, 1.0, 1.5, 2.0, 3.0, 4.0, 6.0, -0.0, -0.5, -1.0, -1.5, -2.0, -3.0, -4.0, -6.0])


def pack_weight(w, fmt):
    k, n = w.shape
    w = f64(np.asarray(w, np.float32).astype(ml_dtypes.bfloat16)).reshape(k // 32, 32, n)
    amax = np.abs(w).max(1)
    if fmt == "e4m3":
        byte = np.frexp(amax)[1] - 1 + 127 - 7
    else:
        mant, ex = np.frexp(amax / 6.0)
        byte = np.where(mant > 0.5, ex, ex - 1) + 127
    byte = np.clip(np.where(amax > 0, byte, 1), 1, 254)
    scaled = (w * np.exp2(127.0 - byte)[:, None, :]).reshape(k, n).astype(np.float32)
    by_word = np.ascontiguousarray(scaled.reshape(k // 512, 128, 4, n).transpose(0, 1, 3, 2))
    if fmt == "e4m3":
        words = by_word.astype(ml_dtypes.float8_e4m3fn).view(np.uint8)
    else:
        c = by_word.astype(ml_dtypes.float4_e2m1fn).view(np.uint8) & 0xF
        words = (c[..., 0::2] | (c[..., 1::2] << 4)).reshape(k // 512, 128, 2 * n)
    return np.ascontiguousarray(words), np.ascontiguousarray(byte.astype(np.uint8).reshape(k // 512, 16, n))


def unpack_weight(words, scales, fmt):
    g, _, n = scales.shape
    words = np.ascontiguousarray(words).reshape(g, 128, n, -1)
    if fmt == "e4m3":
        vals = words.view(ml_dtypes.float8_e4m3fn).astype(np.float64)
    else:
        nib = np.empty((g, 128, n, 4), np.uint8)
        nib[..., 0::2] = words & 0xF
        nib[..., 1::2] = words >> 4
        vals = E2M1[nib]
    vals = vals * np.repeat(np.exp2(scales.astype(np.float64) - 127.0), 8, axis=1)[..., None]
    return vals.transpose(0, 1, 3, 2).reshape(g * 512, n)


def gelu(v):
    return 0.5 * v * (1.0 + np.tanh(np.sqrt(2.0 / np.pi) * (v + 0.044715 * v**3)))


def bf(x):
    return np.asarray(x, np.float32).astype(ml_dtypes.bfloat16)

def planes(Y):
    n, m = Y.shape
    b = f64(bf(Y)).reshape(n // 32, 32, m)
    amax = np.abs(b).max(1)
    byte = np.clip(np.where(amax > 0, np.frexp(amax)[1] - 1 + 127 - 7, 1), 1, 254)
    codes = (b * np.exp2(127.0 - byte)[:, None, :]).reshape(n, m).astype(np.float32).astype(ml_dtypes.float8_e4m3fn).view(np.uint8)
    words = codes.reshape(n // 512, 128, 4, m).transpose(0, 1, 3, 2)
    return np.ascontiguousarray(words), np.ascontiguousarray(byte.astype(np.uint8).reshape(n // 512, 16, m))


K, H, T, S, T2, S2 = 512, 1024, 2048, 1024, 4096, 1536


def setup_inputs():
    n = np.random.standard_normal
    s = mx_kscale(K)[:, None]
    u = mx_kscale(H)[:, None]
    tab_words, tab_scales = pack_weight(n((K, T)) * s, "e4m3")
    tab2_words, tab2_scales = pack_weight(n((H, T2)) * np.sqrt(2.0 / H) / u, "e4m3")
    w1 = 0.24 * n((K, H)) / np.sqrt(K) / s
    w4_words, w4_scales = pack_weight(n((K, H)) / np.sqrt(K) / s * u.T, "e2m1")
    b = 0.5 * np.pi * (2.0 * np.random.random_sample(H) - 1.0)
    return {
        "tab_words": tab_words, "tab_scales": tab_scales,
        "tab2_words": tab2_words, "tab2_scales": tab2_scales,
        "offs": striped(np.random.permutation(T)[:S]),
        "offs2": striped(np.random.permutation(T2)[:S2]),
        "w1": w1.astype(np.float32),
        "w4_words": w4_words, "w4_scales": w4_scales,
        "b": b.astype(np.float32),
        "mu": (0.5 * n(S2)).astype(np.float32),
        "wh": np.exp(0.8 * n(S2)).astype(np.float32),
    }


def reference(tab_words, tab_scales, tab2_words, tab2_scales, offs, offs2, w1, w4_words, w4_scales, b, mu, wh):
    v = unpack_weight(tab_words, tab_scales, "e4m3")[:, unstriped(offs)]
    v2 = unpack_weight(tab2_words, tab2_scales, "e4m3")[:, unstriped(offs2)]
    w4 = unpack_weight(w4_words, w4_scales, "e2m1")
    p = mxq(f64(w1), 0, "e4m3").T @ v
    q = w4.T @ v
    h = np.cos(p + f64(b)[:, None]) * q
    c = v2.T @ mxq(h, 0, "e4m3")
    y = (c - f64(mu)[:, None]) * f64(wh)[:, None]
    words, scales = planes(y)
    return y, words, scales

@@ -1,0 +1,333 @@
+import math
+from contextlib import ExitStack
+
+import concourse.mybir as mybir
+
+K, H, T, S, T2, S2 = 512, 1024, 2048, 1024, 4096, 1536
+FLOPS = 2 * (2 * K * H * S + H * S2 * S)
+
+F32 = mybir.dt.float32
+BF16 = mybir.dt.bfloat16
+I32 = mybir.dt.int32
+U32 = mybir.dt.uint32
+U16 = mybir.dt.uint16
+U8 = mybir.dt.uint8
+E4 = mybir.dt.float8_e4m3fn_x4
+E2 = mybir.dt.float4_e2m1fn_x4
+ACT = mybir.ActivationFunctionType
+ALU = mybir.AluOpType
+
+P = 128
+PACK = 4
+PASS = P * PACK
+NA = H // PASS
+NG = S2 // PASS
+QUADS = 4
+LIST_ROWS = 16
+CHUNKS = [(0, 512), (512, 256), (768, 256)]
+
+
+def tile_list_fourier_landmark_block_kernel(
+    tc, tab_words, tab_scales, tab2_words, tab2_scales, offs, offs2, w1, w4_words, w4_scales, b, mu, wh,
+    out_0, out_1, out_2,
+):
+    nc = tc.nc
+    with ExitStack() as ctx:
+        lists = ctx.enter_context(tc.tile_pool(name="lists", bufs=1))
+        keep = ctx.enter_context(tc.tile_pool(name="keep", bufs=1))
+        work = ctx.enter_context(tc.tile_pool(name="work", bufs=2))
+        reuse = ctx.enter_context(tc.tile_pool(name="reuse", bufs=1))
+        psum = ctx.enter_context(tc.psum_pool(name="psum", bufs=1))
+
+        def kept(shape, dtype, name):
+            return keep.tile(shape, dtype, name=name, align_bytes=64)
+
+        idx = lists.tile([P, S // LIST_ROWS], U16, name="idx")
+        idx2 = lists.tile([P, S2 // LIST_ROWS], U16, name="idx2")
+
+        def shared(shape, dtype, name, offset):
+            return reuse.tile(shape, dtype, name=name, align_bytes=64, offset=offset)
+
+        s_banks = [psum.tile([P, PASS], F32, name=f"s_bank{i}") for i in range(5)]
+        q_banks = [psum.tile([P, PASS], F32, name=f"q_bank{i}") for i in range(3)]
+        s_used = []
+        q_used = []
+
+        def take(banks, used):
+            bank = banks[len(used) % len(banks)]
+            used.append(bank)
+            return bank
+
+        warm = kept([P, 2], F32, "warm")
+        tab_s = kept([P, T], U8, "tab_s")
+        w4_s_raw = kept([P, H], U8, "w4_s_raw")
+        tab2_s = kept([P, T2], U8, "tab2_s")
+        for plane in (tab_s, w4_s_raw, tab2_s):
+            nc.vector.memset(plane[:].bitcast(I32), 0)
+        nc.gpsimd.memset(warm[:, 0:1], 0.0)
+        nc.scalar.activation(warm[:, 1:2], warm[:, 0:1], ACT.Sin)
+
+        tab_w = shared([P, T], I32, "tab_w", 0)
+        w4_w_raw = kept([P, 2 * H], U8, "w4_w_raw")
+        tab2_w = [kept([P, T2], I32, f"tab2_w{a}") for a in range(NA)]
+        pieces = [2, 1]
+        w1_raw = [
+            [kept([P, PACK, PASS // pieces[a]], F32, f"w1_raw{a}{u}") for u in range(pieces[a])] for a in range(NA)
+        ]
+        b_sb = kept([P, NA, PACK], F32, "b_sb")
+        mu_sb = kept([P, NG, PACK], F32, "mu_sb")
+        wh_sb = kept([P, NG, PACK], F32, "wh_sb")
+
+        def load_w1(a, u):
+            width = PASS // pieces[a]
+            c0 = a * PASS + u * width
+            nc.sync.dma_start(w1_raw[a][u][:], w1[:, c0 : c0 + width].rearrange("(p j) c -> p j c", j=PACK))
+
+        def load_rows(plane, scales):
+            for quad in range(QUADS):
+                nc.sync.dma_start(
+                    plane[32 * quad : 32 * quad + 4, :].bitcast(I32),
+                    scales[0, 4 * quad : 4 * quad + 4, :].bitcast(I32),
+                )
+
+        def load_words(tile, words):
+            nc.sync.dma_start(tile[:], words.rearrange("p n i -> p (n i)").bitcast(I32))
+
+        nc.sync.dma_start(w4_w_raw[:].bitcast(I32), w4_words[0].bitcast(I32))
+        nc.sync.dma_start(idx[:], offs)
+        load_rows(tab_s, tab_scales)
+        load_w1(0, 0)
+        load_w1(0, 1)
+        load_w1(1, 0)
+        load_rows(w4_s_raw, w4_scales)
+        load_words(tab_w, tab_words[0])
+        nc.sync.dma_start(idx2[:], offs2)
+        load_words(tab2_w[0], tab2_words[0])
+        load_words(tab2_w[1], tab2_words[1])
+        nc.gpsimd.dma_start(b_sb[:], b.rearrange("(a p t) -> p a t", p=P, t=PACK))
+        nc.gpsimd.dma_start(
+            tab2_s[0 : 16 * NA, :].bitcast(I32), tab2_scales.rearrange("a q t -> (a q) t").bitcast(I32)
+        )
+        nc.gpsimd.dma_start(mu_sb[:], mu.rearrange("(g p t) -> p g t", p=P, t=PACK))
+        nc.gpsimd.dma_start(wh_sb[:], wh.rearrange("(g p t) -> p g t", p=P, t=PACK))
+
+        w4_w = kept([P, 2 * H], U8, "w4_w")
+        w4_s = kept([P, H], U8, "w4_s")
+        v_w = [kept([P, n], U32, f"v_w{c}") for c, (j0, n) in enumerate(CHUNKS)]
+        v_s = [kept([P, n], U8, f"v_s{c}") for c, (j0, n) in enumerate(CHUNKS)]
+        w1_bf = [kept([P, PACK, P, PACK], BF16, f"w1_bf{a}") for a in range(NA)]
+        w1_w = [kept([P, PASS], U32, f"w1_w{a}") for a in range(NA)]
+        w1_s = [kept([P, PASS], U8, "w1_s0"), shared([P, PASS], U8, "w1_s1", S2)]
+        v2_w = [
+            [
+                shared([P, PACK, P], U32, f"v2_w{g}{a}", 4 * T)
+                if (g, a) == (2, 0)
+                else kept([P, PACK, P], U32, f"v2_w{g}{a}")
+                for a in range(NA)
+            ]
+            for g in range(NG)
+        ]
+        v2_s_list = shared([P, S2], U8, "v2_s_list", 0)
+        v2_s_dealt = kept([P, S2], U8, "v2_s_dealt")
+        v2_s = kept([P, S2], U8, "v2_s")
+        nc.gpsimd.memset(v2_s[:].bitcast(I32), 0)
+        h_w = [[kept([P, n], U32, f"h_w{c}{a}") for a in range(NA)] for c, (j0, n) in enumerate(CHUNKS)]
+        h_s = [[kept([P, n], U8, f"h_s{c}{a}") for a in range(NA)] for c, (j0, n) in enumerate(CHUNKS)]
+        shift = kept([P, NG, PACK], F32, "shift")
+        mu_wh = kept([P, NG, PACK], F32, "mu_wh")
+        y_s = [kept([P, NG, n], U8, f"y_s{c}") for c, (j0, n) in enumerate(CHUNKS)]
+
+        def entries(lst, j0, n):
+            return lst[:, j0 // LIST_ROWS : (j0 + n) // LIST_ROWS]
+
+        def deal(out, in_):
+            nc.vector.tensor_copy(
+                out.rearrange("p (g t m) -> p g t m", t=PACK, m=P),
+                in_.rearrange("p (g m t) -> p g t m", t=PACK, m=P),
+            )
+
+        def gather_v_scales(c):
+            j0, n = CHUNKS[c]
+            nc.vector.tensor_copy(v_s[c][:], tab_s[:].indirect(entries(idx, j0, n)))
+
+        def gather_v_words(c):
+            j0, n = CHUNKS[c]
+            nc.vector.tensor_copy(v_w[c][:], tab_w[:].bitcast(U32).indirect(entries(idx, j0, n)))
+
+        def round_w1(a):
+            for u in range(pieces[a]):
+                m0 = u * (P // pieces[a])
+                nc.scalar.copy(
+                    w1_bf[a][:, :, m0 : m0 + P // pieces[a], :].rearrange("p t m j -> p m j t"),
+                    w1_raw[a][u][:].rearrange("p j (m t) -> p m j t", t=PACK),
+                )
+
+        def quantize_w1(a):
+            nc.vector.quantize_mx(
+                out=w1_w[a][:].bitcast(E4),
+                scales=w1_s[a][:],
+                in_=w1_bf[a][:].rearrange("p t m j -> p (t m j)"),
+            )
+
+        def gather_v2_words(g, a):
+            nc.vector.tensor_copy(
+                v2_w[g][a][:].rearrange("p t m -> p m t"),
+                tab2_w[a][:].bitcast(U32).indirect(entries(idx2, g * PASS, PASS)),
+            )
+
+        def gather_v2_scales():
+            nc.vector.tensor_copy(v2_s_list[:], tab2_s[:].indirect(idx2[:]))
+            deal(v2_s_dealt[:], v2_s_list[:])
+
+        def place_v2_scales():
+            for a in range(NA):
+                for quad in range(QUADS):
+                    src = 16 * a + 4 * quad
+                    dst = 32 * quad + 4 * a
+                    nc.sync.dma_start(v2_s[dst : dst + 4, :].bitcast(I32), v2_s_dealt[src : src + 4, :].bitcast(I32))
+
+        def gather_v2(g):
+            for a in range(NA):
+                gather_v2_words(g, a)
+
+        def gather_v(c):
+            gather_v_scales(c)
+            gather_v_words(c)
+
+        def features(c, a):
+            j0, n = CHUNKS[c]
+            dist = work.tile([P, PACK, n], F32, name="dist", tag="dist")
+            cosv = work.tile([P, PACK, n], F32, name="cosv", tag="cosv", bufs=3)
+            per_bank = PASS // n
+            for t in range(PACK):
+                if t % per_bank == 0:
+                    p_bank = take(s_banks, s_used)[:].rearrange("p (t n) -> p t n", n=n)
+                nc.tensor.matmul_mx(
+                    out=p_bank[:, t % per_bank, :],
+                    lhsT=w1_w[a][:, t * P : (t + 1) * P].bitcast(E4),
+                    lhsT_scale=w1_s[a][:, t * P : (t + 1) * P],
+                    rhs=v_w[c][:].bitcast(E4),
+                    rhs_scale=v_s[c][:],
+                    start=True,
+                    stop=True,
+                )
+                if t % per_bank == per_bank - 1:
+                    for tt in range(t - per_bank + 1, t + 1):
+                        nc.scalar.activation(
+                            dist[:, tt, :], p_bank[:, tt % per_bank, :], ACT.Abs, bias=b_sb[:, a, tt : tt + 1]
+                        )
+                if t % 2 == 1:
+                    nc.scalar.activation(
+                        cosv[:, t - 1 : t + 1, :], dist[:, t - 1 : t + 1, :], ACT.Sin, bias=math.pi / 2, scale=-1.0
+                    )
+            if (c, a) == (0, 1):
+                h_bf = shared([P, n, PACK], BF16, "h_bf01", 4 * T)
+            else:
+                h_bf = work.tile([P, n, PACK], BF16, name="h_bf", tag="h_bf", align_bytes=64)
+            for j in range(0, n, P):
+                q_bank = take(q_banks, q_used)[:].rearrange("p (t n) -> p t n", n=P)
+                for t in range(PACK):
+                    col = a * PASS + t * P
+                    nc.tensor.matmul_mx(
+                        out=q_bank[:, t, :],
+                        lhsT=w4_w[:, 2 * col : 2 * (col + P)].bitcast(E2),
+                        lhsT_scale=w4_s[:, col : col + P],
+                        rhs=v_w[c][:, j : j + P].bitcast(E4),
+                        rhs_scale=v_s[c][:, j : j + P],
+                        start=True,
+                        stop=True,
+                    )
+                nc.vector.tensor_tensor(
+                    h_bf[:, j : j + P, :].rearrange("p (c i) t -> p c t i", i=2),
+                    q_bank.rearrange("p t (c i) -> p c t i", i=2),
+                    cosv[:, :, j : j + P].rearrange("p t (c i) -> p c t i", i=2),
+                    ALU.mult,
+                )
+            nc.vector.quantize_mx(
+                out=h_w[c][a][:].bitcast(E4),
+                scales=h_s[c][a][:],
+                in_=h_bf[:].rearrange("p n t -> p (n t)"),
+            )
+
+        def block(c, g):
+            j0, n = CHUNKS[c]
+            y = work.tile([P, PACK, n], F32, name="y", tag="y", bufs=3)
+            per_bank = PASS // n
+            for t in range(PACK):
+                if t % per_bank == 0:
+                    c_bank = take(s_banks, s_used)[:].rearrange("p (t n) -> p t n", n=n)
+                for a in range(NA):
+                    nc.tensor.matmul_mx(
+                        out=c_bank[:, t % per_bank, :],
+                        lhsT=v2_w[g][a][:, t, :].bitcast(E4),
+                        lhsT_scale=v2_s[4 * a : P, g * PASS + t * P : g * PASS + (t + 1) * P],
+                        rhs=h_w[c][a][:].bitcast(E4),
+                        rhs_scale=h_s[c][a][:],
+                        start=(a == 0),
+                        stop=(a == NA - 1),
+                    )
+                if t % per_bank == per_bank - 1:
+                    for tt in range(t - per_bank + 1, t + 1):
+                        nc.scalar.activation(
+                            y[:, tt, :], c_bank[:, tt % per_bank, :], ACT.Identity,
+                            bias=shift[:, g, tt : tt + 1], scale=wh_sb[:, g, tt : tt + 1],
+                        )
+            rows = out_0[g * PASS : (g + 1) * PASS, j0 : j0 + n]
+            nc.sync.dma_start(rows.rearrange("(p t) j -> p t j", t=PACK), y[:])
+            y_bf = work.tile([P, n, PACK], BF16, name="y_bf", tag="y_bf", align_bytes=64)
+            nc.vector.tensor_copy(
+                y_bf[:].rearrange("p (c i) t -> p c t i", i=2),
+                y[:].rearrange("p t (c i) -> p c t i", i=2),
+            )
+            y_w = work.tile([P, n], U32, name="y_w", tag="y_w", bufs=3, align_bytes=64)
+            nc.vector.quantize_mx(
+                out=y_w[:].bitcast(E4),
+                scales=y_s[c][:, g, :],
+                in_=y_bf[:].rearrange("p n t -> p (n t)"),
+            )
+            nc.sync.dma_start(
+                out_1[g, :, j0 : j0 + n, :].rearrange("p n t -> p (n t)").bitcast(I32), y_w[:].bitcast(I32)
+            )
+
+        def store_scales(c):
+            j0, n = CHUNKS[c]
+            for quad in range(QUADS):
+                nc.sync.dma_start(
+                    out_2[:, 4 * quad : 4 * quad + 4, j0 : j0 + n].bitcast(I32).rearrange("g r n -> r g n"),
+                    y_s[c][32 * quad : 32 * quad + 4, :, :].bitcast(I32),
+                )
+
+        deal(w4_w[:].bitcast(U16), w4_w_raw[:].bitcast(U16))
+        gather_v_scales(0)
+        round_w1(0)
+        quantize_w1(0)
+        round_w1(1)
+        gather_v_words(0)
+        deal(w4_s[:], w4_s_raw[:])
+        gather_v(1)
+        gather_v(2)
+        quantize_w1(1)
+        gather_v2_scales()
+        place_v2_scales()
+        features(0, 0)
+        gather_v2(0)
+        features(0, 1)
+        nc.gpsimd.tensor_tensor(mu_wh[:], mu_sb[:], wh_sb[:], ALU.mult)
+        nc.gpsimd.tensor_scalar(shift[:], mu_wh[:], -1.0, 0.0, ALU.mult, ALU.add)
+        features(1, 0)
+        gather_v2(1)
+        features(1, 1)
+        block(0, 0)
+        gather_v2(2)
+        block(0, 1)
+        features(2, 0)
+        block(0, 2)
+        store_scales(0)
+        block(1, 0)
+        features(2, 1)
+        block(1, 1)
+        block(1, 2)
+        store_scales(1)
+        for g in range(NG):
+            block(2, g)
+        store_scales(2)

@@ -24,6 +24,7 @@ NA = H // PASS
 NG = S2 // PASS
 QUADS = 4
 LIST_ROWS = 16
+NS = 4
 CHUNKS = [(0, 512), (512, 256), (768, 256)]
 
 
@@ -48,8 +49,9 @@ def tile_list_fourier_landmark_block_kernel(
         def shared(shape, dtype, name, offset):
             return reuse.tile(shape, dtype, name=name, align_bytes=64, offset=offset)
 
-        s_banks = [psum.tile([P, PASS], F32, name=f"s_bank{i}") for i in range(5)]
-        q_banks = [psum.tile([P, PASS], F32, name=f"q_bank{i}") for i in range(3)]
+        s_banks = [psum.tile([P, PASS], F32, name=f"bank{i}") for i in range(8)]
+        q_banks = s_banks[NS:]
+        s_banks = s_banks[:NS]
         s_used = []
         q_used = []
 
@@ -62,17 +64,19 @@ def tile_list_fourier_landmark_block_kernel(
         tab_s = kept([P, T], U8, "tab_s")
         w4_s_raw = kept([P, H], U8, "w4_s_raw")
         tab2_s = kept([P, T2], U8, "tab2_s")
-        for plane in (tab_s, w4_s_raw, tab2_s):
+        for plane in (tab_s, w4_s_raw):
             nc.vector.memset(plane[:].bitcast(I32), 0)
         nc.gpsimd.memset(warm[:, 0:1], 0.0)
+        nc.gpsimd.memset(tab2_s[:].bitcast(I32), 0)
         nc.scalar.activation(warm[:, 1:2], warm[:, 0:1], ACT.Sin)
 
-        tab_w = shared([P, T], I32, "tab_w", 0)
+        tab_w = kept([P, T], I32, "tab_w")
         w4_w_raw = kept([P, 2 * H], U8, "w4_w_raw")
-        tab2_w = [kept([P, T2], I32, f"tab2_w{a}") for a in range(NA)]
+        tab2_w = [kept([P, T2], I32, "tab2_w0"), shared([P, T2], I32, "tab2_w1", 0)]
         pieces = [2, 1]
         w1_raw = [
-            [kept([P, PACK, PASS // pieces[a]], F32, f"w1_raw{a}{u}") for u in range(pieces[a])] for a in range(NA)
+            [kept([P, PACK, PASS // 2], F32, f"w1_raw0{u}") for u in range(2)],
+            [shared([P, PACK, PASS], F32, "w1_raw1", 0)],
         ]
         b_sb = kept([P, NA, PACK], F32, "b_sb")
         mu_sb = kept([P, NG, PACK], F32, "mu_sb")
@@ -90,44 +94,48 @@ def tile_list_fourier_landmark_block_kernel(
                     scales[0, 4 * quad : 4 * quad + 4, :].bitcast(I32),
                 )
 
-        def load_words(tile, words):
-            nc.sync.dma_start(tile[:], words.rearrange("p n i -> p (n i)").bitcast(I32))
+        def load_words(tile, words, queue=nc.sync):
+            queue.dma_start(tile[:], words.rearrange("p n i -> p (n i)").bitcast(I32))
 
-        nc.sync.dma_start(w4_w_raw[:].bitcast(I32), w4_words[0].bitcast(I32))
         nc.sync.dma_start(idx[:], offs)
-        load_rows(tab_s, tab_scales)
         load_w1(0, 0)
-        load_w1(0, 1)
-        load_w1(1, 0)
-        load_rows(w4_s_raw, w4_scales)
-        load_words(tab_w, tab_words[0])
-        nc.sync.dma_start(idx2[:], offs2)
-        load_words(tab2_w[0], tab2_words[0])
-        load_words(tab2_w[1], tab2_words[1])
-        nc.gpsimd.dma_start(b_sb[:], b.rearrange("(a p t) -> p a t", p=P, t=PACK))
-        nc.gpsimd.dma_start(
+        load_rows(tab_s, tab_scales)
+        nc.sync.dma_start(
             tab2_s[0 : 16 * NA, :].bitcast(I32), tab2_scales.rearrange("a q t -> (a q) t").bitcast(I32)
         )
+        load_w1(0, 1)
+        nc.sync.dma_start(idx2[:], offs2)
+        load_words(tab_w, tab_words[0])
+        nc.sync.dma_start(w4_w_raw[:].bitcast(I32), w4_words[0].bitcast(I32))
+        load_rows(w4_s_raw, w4_scales)
+        load_w1(1, 0)
+        load_words(tab2_w[0], tab2_words[0])
+        nc.gpsimd.dma_start(b_sb[:], b.rearrange("(a p t) -> p a t", p=P, t=PACK))
         nc.gpsimd.dma_start(mu_sb[:], mu.rearrange("(g p t) -> p g t", p=P, t=PACK))
         nc.gpsimd.dma_start(wh_sb[:], wh.rearrange("(g p t) -> p g t", p=P, t=PACK))
 
         w4_w = kept([P, 2 * H], U8, "w4_w")
         w4_s = kept([P, H], U8, "w4_s")
-        v_w = [kept([P, n], U32, f"v_w{c}") for c, (j0, n) in enumerate(CHUNKS)]
-        v_s = [kept([P, n], U8, f"v_s{c}") for c, (j0, n) in enumerate(CHUNKS)]
-        w1_bf = [kept([P, PACK, P, PACK], BF16, f"w1_bf{a}") for a in range(NA)]
+        KB = 1024
+        v_w = [kept([P, 512], U32, "v_w0"), kept([P, 256], U32, "v_w1"), kept([P, 256], U32, "v_w2")]
+        v_s = [kept([P, 512], U8, "v_s0"), kept([P, 256], U8, "v_s1"), kept([P, 256], U8, "v_s2")]
+        w1_bf = [kept([P, PACK, P, PACK], BF16, "w1_bf0"), shared([P, PACK, P, PACK], BF16, "w1_bf1", 28 * KB)]
         w1_w = [kept([P, PASS], U32, f"w1_w{a}") for a in range(NA)]
-        w1_s = [kept([P, PASS], U8, "w1_s0"), shared([P, PASS], U8, "w1_s1", S2)]
+        w1_s = [kept([P, PASS], U8, f"w1_s{a}") for a in range(NA)]
+        h_at = {(0, 0): 28 * KB, (0, 1): 20 * KB, (1, 0): 25 * KB}
         v2_w = [
             [
-                shared([P, PACK, P], U32, f"v2_w{g}{a}", 4 * T)
-                if (g, a) == (2, 0)
+                shared([P, PACK, P], U32, f"v2_w{g}{a}", 19 * KB + (2 * g + a - 2) * 2 * KB)
+                if g > 0
                 else kept([P, PACK, P], U32, f"v2_w{g}{a}")
                 for a in range(NA)
             ]
             for g in range(NG)
         ]
-        v2_s_list = shared([P, S2], U8, "v2_s_list", 0)
+        v2_s_list = [
+            shared([P, PASS], U8, f"v2_s_list{g}", 28 * KB + g * PASS) if g > 0 else kept([P, PASS], U8, f"v2_s_list{g}")
+            for g in range(NG)
+        ]
         v2_s_dealt = kept([P, S2], U8, "v2_s_dealt")
         v2_s = kept([P, S2], U8, "v2_s")
         nc.gpsimd.memset(v2_s[:].bitcast(I32), 0)
@@ -135,7 +143,8 @@ def tile_list_fourier_landmark_block_kernel(
         h_s = [[kept([P, n], U8, f"h_s{c}{a}") for a in range(NA)] for c, (j0, n) in enumerate(CHUNKS)]
         shift = kept([P, NG, PACK], F32, "shift")
         mu_wh = kept([P, NG, PACK], F32, "mu_wh")
-        y_s = [kept([P, NG, n], U8, f"y_s{c}") for c, (j0, n) in enumerate(CHUNKS)]
+        y_s = kept([P, NG, S], U8, "y_s")
+        y_w = [kept([P, NG, n], U32, f"y_w{c}") for c, (j0, n) in enumerate(CHUNKS)]
 
         def entries(lst, j0, n):
             return lst[:, j0 // LIST_ROWS : (j0 + n) // LIST_ROWS]
@@ -157,7 +166,8 @@ def tile_list_fourier_landmark_block_kernel(
         def round_w1(a):
             for u in range(pieces[a]):
                 m0 = u * (P // pieces[a])
-                nc.scalar.copy(
+                cast = nc.scalar.copy if a == 0 else nc.vector.tensor_copy
+                cast(
                     w1_bf[a][:, :, m0 : m0 + P // pieces[a], :].rearrange("p t m j -> p m j t"),
                     w1_raw[a][u][:].rearrange("p j (m t) -> p m j t", t=PACK),
                 )
@@ -175,9 +185,9 @@ def tile_list_fourier_landmark_block_kernel(
                 tab2_w[a][:].bitcast(U32).indirect(entries(idx2, g * PASS, PASS)),
             )
 
-        def gather_v2_scales():
-            nc.vector.tensor_copy(v2_s_list[:], tab2_s[:].indirect(idx2[:]))
-            deal(v2_s_dealt[:], v2_s_list[:])
+        def gather_v2_scales(g):
+            nc.vector.tensor_copy(v2_s_list[g][:], tab2_s[:].indirect(entries(idx2, g * PASS, PASS)))
+            deal(v2_s_dealt[:, g * PASS : (g + 1) * PASS], v2_s_list[g][:])
 
         def place_v2_scales():
             for a in range(NA):
@@ -194,7 +204,9 @@ def tile_list_fourier_landmark_block_kernel(
             gather_v_scales(c)
             gather_v_words(c)
 
-        def features(c, a):
+        cos_of = {}
+
+        def cosines(c, a):
             j0, n = CHUNKS[c]
             dist = work.tile([P, PACK, n], F32, name="dist", tag="dist")
             cosv = work.tile([P, PACK, n], F32, name="cosv", tag="cosv", bufs=3)
@@ -220,8 +232,13 @@ def tile_list_fourier_landmark_block_kernel(
                     nc.scalar.activation(
                         cosv[:, t - 1 : t + 1, :], dist[:, t - 1 : t + 1, :], ACT.Sin, bias=math.pi / 2, scale=-1.0
                     )
-            if (c, a) == (0, 1):
-                h_bf = shared([P, n, PACK], BF16, "h_bf01", 4 * T)
+            cos_of[(c, a)] = cosv
+
+        def features(c, a):
+            j0, n = CHUNKS[c]
+            cosv = cos_of[(c, a)]
+            if (c, a) in h_at:
+                h_bf = shared([P, n, PACK], BF16, f"h_bf{c}{a}", h_at[(c, a)])
             else:
                 h_bf = work.tile([P, n, PACK], BF16, name="h_bf", tag="h_bf", align_bytes=64)
             for j in range(0, n, P):
@@ -249,9 +266,11 @@ def tile_list_fourier_landmark_block_kernel(
                 in_=h_bf[:].rearrange("p n t -> p (n t)"),
             )
 
+        y_of = {}
+
         def block(c, g):
             j0, n = CHUNKS[c]
-            y = work.tile([P, PACK, n], F32, name="y", tag="y", bufs=3)
+            y = work.tile([P, PACK, n], F32, name="y", tag="y", bufs=4)
             per_bank = PASS // n
             for t in range(PACK):
                 if t % per_bank == 0:
@@ -272,62 +291,93 @@ def tile_list_fourier_landmark_block_kernel(
                             y[:, tt, :], c_bank[:, tt % per_bank, :], ACT.Identity,
                             bias=shift[:, g, tt : tt + 1], scale=wh_sb[:, g, tt : tt + 1],
                         )
-            rows = out_0[g * PASS : (g + 1) * PASS, j0 : j0 + n]
-            nc.sync.dma_start(rows.rearrange("(p t) j -> p t j", t=PACK), y[:])
+                if (t + 1) % (2 * per_bank) == 0:
+                    rows = out_0[g * PASS : (g + 1) * PASS, j0 : j0 + n].rearrange("(p t) j -> p t j", t=PACK)
+                    t0 = t + 1 - 2 * per_bank
+                    nc.sync.dma_start(rows[:, t0 : t + 1, :], y[:, t0 : t + 1, :])
+            y_of[(c, g)] = y
+
+        def planes(c, g):
+            j0, n = CHUNKS[c]
+            y = y_of[(c, g)]
             y_bf = work.tile([P, n, PACK], BF16, name="y_bf", tag="y_bf", align_bytes=64)
             nc.vector.tensor_copy(
                 y_bf[:].rearrange("p (c i) t -> p c t i", i=2),
                 y[:].rearrange("p t (c i) -> p c t i", i=2),
             )
-            y_w = work.tile([P, n], U32, name="y_w", tag="y_w", bufs=3, align_bytes=64)
             nc.vector.quantize_mx(
-                out=y_w[:].bitcast(E4),
-                scales=y_s[c][:, g, :],
+                out=y_w[c][:, g, :].bitcast(E4),
+                scales=y_s[:, g, j0 : j0 + n],
                 in_=y_bf[:].rearrange("p n t -> p (n t)"),
             )
+
+        def store_words(c, g0, g1):
+            j0, n = CHUNKS[c]
             nc.sync.dma_start(
-                out_1[g, :, j0 : j0 + n, :].rearrange("p n t -> p (n t)").bitcast(I32), y_w[:].bitcast(I32)
+                out_1[g0:g1, :, j0 : j0 + n, :].rearrange("g p n t -> p g (n t)").bitcast(I32),
+                y_w[c][:, g0:g1, :].bitcast(I32),
             )
 
-        def store_scales(c):
-            j0, n = CHUNKS[c]
+        def store_scales():
             for quad in range(QUADS):
                 nc.sync.dma_start(
-                    out_2[:, 4 * quad : 4 * quad + 4, j0 : j0 + n].bitcast(I32).rearrange("g r n -> r g n"),
-                    y_s[c][32 * quad : 32 * quad + 4, :, :].bitcast(I32),
+                    out_2[:, 4 * quad : 4 * quad + 4, :].bitcast(I32).rearrange("g r n -> r g n"),
+                    y_s[32 * quad : 32 * quad + 4, :, :].bitcast(I32),
                 )
 
-        deal(w4_w[:].bitcast(U16), w4_w_raw[:].bitcast(U16))
         gather_v_scales(0)
         round_w1(0)
         quantize_w1(0)
-        round_w1(1)
         gather_v_words(0)
-        deal(w4_s[:], w4_s_raw[:])
         gather_v(1)
-        gather_v(2)
+        gather_v_scales(2)
+        gather_v2_scales(0)
+        deal(w4_w[:].bitcast(U16), w4_w_raw[:].bitcast(U16))
+        deal(w4_s[:], w4_s_raw[:])
+        round_w1(1)
+        load_words(tab2_w[1], tab2_words[1], nc.scalar)
         quantize_w1(1)
-        gather_v2_scales()
-        place_v2_scales()
-        features(0, 0)
-        gather_v2(0)
-        features(0, 1)
+        gather_v2_scales(1)
         nc.gpsimd.tensor_tensor(mu_wh[:], mu_sb[:], wh_sb[:], ALU.mult)
         nc.gpsimd.tensor_scalar(shift[:], mu_wh[:], -1.0, 0.0, ALU.mult, ALU.add)
-        features(1, 0)
-        gather_v2(1)
-        features(1, 1)
+        cosines(0, 0)
+        features(0, 0)
+        gather_v2_scales(2)
+        place_v2_scales()
+        gather_v2(0)
+        cosines(0, 1)
+        features(0, 1)
+        gather_v_words(2)
+        cosines(1, 0)
+        cosines(1, 1)
         block(0, 0)
-        gather_v2(2)
+        gather_v2(1)
+        features(1, 0)
         block(0, 1)
-        features(2, 0)
+        gather_v2(2)
+        features(1, 1)
         block(0, 2)
-        store_scales(0)
-        block(1, 0)
+        planes(0, 0)
+        cosines(2, 0)
+        cosines(2, 1)
+        features(2, 0)
         features(2, 1)
+        block(1, 0)
+        planes(0, 1)
         block(1, 1)
+        planes(0, 2)
         block(1, 2)
-        store_scales(1)
-        for g in range(NG):
-            block(2, g)
-        store_scales(2)
+        store_words(0, 0, 3)
+        planes(1, 0)
+        planes(1, 1)
+        block(2, 0)
+        planes(1, 2)
+        block(2, 1)
+        store_words(1, 0, 3)
+        planes(2, 0)
+        block(2, 2)
+        planes(2, 1)
+        store_words(2, 0, 2)
+        planes(2, 2)
+        store_words(2, 2, 3)
+        store_scales()

@@ -12,20 +12,29 @@ I32 = mybir.dt.int32
 U32 = mybir.dt.uint32
 U16 = mybir.dt.uint16
 U8 = mybir.dt.uint8
-E4 = mybir.dt.float8_e4m3fn_x4
-E2 = mybir.dt.float4_e2m1fn_x4
+E4M3 = mybir.dt.float8_e4m3fn_x4
+E2M1 = mybir.dt.float4_e2m1fn_x4
 ACT = mybir.ActivationFunctionType
 ALU = mybir.AluOpType
 
 P = 128
 PACK = 4
 PASS = P * PACK
-NA = H // PASS
-NG = S2 // PASS
-QUADS = 4
+PASSES = H // PASS
+GROUPS = S2 // PASS
+HALF = S // 2
+QUADRANTS = 4
+QUADRANT = P // QUADRANTS
+SCALE_ROWS = 4
+BLOCKS = QUADRANTS * SCALE_ROWS
 LIST_ROWS = 16
-NS = 4
-CHUNKS = [(0, 512), (512, 256), (768, 256)]
+
+KB = 1024
+AT_W1_BF = 0
+AT_H01 = 4 * KB
+AT_COS10 = 8 * KB
+AT_Y_BF = 16 * KB
+AT_W1_RAW = 24 * KB
 
 
 def tile_list_fourier_landmark_block_kernel(
@@ -43,22 +52,15 @@ def tile_list_fourier_landmark_block_kernel(
         def kept(shape, dtype, name):
             return keep.tile(shape, dtype, name=name, align_bytes=64)
 
-        idx = lists.tile([P, S // LIST_ROWS], U16, name="idx")
-        idx2 = lists.tile([P, S2 // LIST_ROWS], U16, name="idx2")
-
         def shared(shape, dtype, name, offset):
             return reuse.tile(shape, dtype, name=name, align_bytes=64, offset=offset)
 
-        s_banks = [psum.tile([P, PASS], F32, name=f"bank{i}") for i in range(8)]
-        q_banks = s_banks[NS:]
-        s_banks = s_banks[:NS]
-        s_used = []
-        q_used = []
+        idx = lists.tile([P, S // LIST_ROWS], U16, name="idx")
+        idx2 = lists.tile([P, S2 // LIST_ROWS], U16, name="idx2")
 
-        def take(banks, used):
-            bank = banks[len(used) % len(banks)]
-            used.append(bank)
-            return bank
+        banks = [psum.tile([P, PASS], F32, name=f"bank{i}") for i in range(2 * PACK)]
+        low, high = banks[:PACK], banks[PACK:]
+        unit_banks = {(0, 0): (low, high), (0, 1): (low, low), (1, 0): (high, high), (1, 1): (low, low)}
 
         warm = kept([P, 2], F32, "warm")
         tab_s = kept([P, T], U8, "tab_s")
@@ -72,82 +74,75 @@ def tile_list_fourier_landmark_block_kernel(
 
         tab_w = kept([P, T], I32, "tab_w")
         w4_w_raw = kept([P, 2 * H], U8, "w4_w_raw")
-        tab2_w = [kept([P, T2], I32, "tab2_w0"), shared([P, T2], I32, "tab2_w1", 0)]
-        pieces = [2, 1]
+        tab2_w = [kept([P, T2], I32, "tab2_w0"), shared([P, T2], I32, "tab2_w1", AT_W1_RAW + 2 * KB)]
         w1_raw = [
             [kept([P, PACK, PASS // 2], F32, f"w1_raw0{u}") for u in range(2)],
-            [shared([P, PACK, PASS], F32, "w1_raw1", 0)],
+            [shared([P, PACK, PASS], F32, "w1_raw1", AT_W1_RAW)],
         ]
-        b_sb = kept([P, NA, PACK], F32, "b_sb")
-        mu_sb = kept([P, NG, PACK], F32, "mu_sb")
-        wh_sb = kept([P, NG, PACK], F32, "wh_sb")
+        b_sb = kept([P, PASSES, PACK], F32, "b_sb")
+        mu_sb = kept([P, GROUPS, PACK], F32, "mu_sb")
+        wh_sb = kept([P, GROUPS, PACK], F32, "wh_sb")
 
         def load_w1(a, u):
-            width = PASS // pieces[a]
+            width = PASS // len(w1_raw[a])
             c0 = a * PASS + u * width
             nc.sync.dma_start(w1_raw[a][u][:], w1[:, c0 : c0 + width].rearrange("(p j) c -> p j c", j=PACK))
 
-        def load_rows(plane, scales):
-            for quad in range(QUADS):
+        def load_scale_rows(plane, scales):
+            for quad in range(QUADRANTS):
                 nc.sync.dma_start(
-                    plane[32 * quad : 32 * quad + 4, :].bitcast(I32),
-                    scales[0, 4 * quad : 4 * quad + 4, :].bitcast(I32),
+                    plane[QUADRANT * quad : QUADRANT * quad + SCALE_ROWS, :].bitcast(I32),
+                    scales[0, SCALE_ROWS * quad : SCALE_ROWS * (quad + 1), :].bitcast(I32),
                 )
 
-        def load_words(tile, words, queue=nc.sync):
+        def load_words(queue, tile, words):
             queue.dma_start(tile[:], words.rearrange("p n i -> p (n i)").bitcast(I32))
 
         nc.sync.dma_start(idx[:], offs)
         load_w1(0, 0)
-        load_rows(tab_s, tab_scales)
+        load_scale_rows(tab_s, tab_scales)
         nc.sync.dma_start(
-            tab2_s[0 : 16 * NA, :].bitcast(I32), tab2_scales.rearrange("a q t -> (a q) t").bitcast(I32)
+            tab2_s[0 : BLOCKS * PASSES, :].bitcast(I32), tab2_scales.rearrange("a q t -> (a q) t").bitcast(I32)
         )
         load_w1(0, 1)
         nc.sync.dma_start(idx2[:], offs2)
-        load_words(tab_w, tab_words[0])
+        load_words(nc.sync, tab_w, tab_words[0])
         nc.sync.dma_start(w4_w_raw[:].bitcast(I32), w4_words[0].bitcast(I32))
-        load_rows(w4_s_raw, w4_scales)
+        load_scale_rows(w4_s_raw, w4_scales)
         load_w1(1, 0)
-        load_words(tab2_w[0], tab2_words[0])
+        load_words(nc.sync, tab2_w[0], tab2_words[0])
         nc.gpsimd.dma_start(b_sb[:], b.rearrange("(a p t) -> p a t", p=P, t=PACK))
         nc.gpsimd.dma_start(mu_sb[:], mu.rearrange("(g p t) -> p g t", p=P, t=PACK))
         nc.gpsimd.dma_start(wh_sb[:], wh.rearrange("(g p t) -> p g t", p=P, t=PACK))
 
         w4_w = kept([P, 2 * H], U8, "w4_w")
         w4_s = kept([P, H], U8, "w4_s")
-        KB = 1024
-        v_w = [kept([P, 512], U32, "v_w0"), kept([P, 256], U32, "v_w1"), kept([P, 256], U32, "v_w2")]
-        v_s = [kept([P, 512], U8, "v_s0"), kept([P, 256], U8, "v_s1"), kept([P, 256], U8, "v_s2")]
-        w1_bf = [kept([P, PACK, P, PACK], BF16, "w1_bf0"), shared([P, PACK, P, PACK], BF16, "w1_bf1", 28 * KB)]
-        w1_w = [kept([P, PASS], U32, f"w1_w{a}") for a in range(NA)]
-        w1_s = [kept([P, PASS], U8, f"w1_s{a}") for a in range(NA)]
-        h_at = {(0, 0): 28 * KB, (0, 1): 20 * KB, (1, 0): 25 * KB}
-        v2_w = [
-            [
-                shared([P, PACK, P], U32, f"v2_w{g}{a}", 19 * KB + (2 * g + a - 2) * 2 * KB)
-                if g > 0
-                else kept([P, PACK, P], U32, f"v2_w{g}{a}")
-                for a in range(NA)
-            ]
-            for g in range(NG)
-        ]
-        v2_s_list = [
-            shared([P, PASS], U8, f"v2_s_list{g}", 28 * KB + g * PASS) if g > 0 else kept([P, PASS], U8, f"v2_s_list{g}")
-            for g in range(NG)
+        v_w = [kept([P, HALF], U32, f"v_w{c}") for c in range(2)]
+        v_s = [kept([P, HALF], U8, f"v_s{c}") for c in range(2)]
+        w1_bf = [kept([P, PACK, P, PACK], BF16, "w1_bf0"), shared([P, PACK, P, PACK], BF16, "w1_bf1", AT_W1_BF)]
+        w1_w = [kept([P, PASS], U32, f"w1_w{a}") for a in range(PASSES)]
+        w1_s = [kept([P, PASS], U8, f"w1_s{a}") for a in range(PASSES)]
+        v2_w = {(0, 0): kept([P, PACK, P], U32, "v2_w00"), (0, 1): shared([P, PACK, P], U32, "v2_w01", AT_H01)}
+        for g in range(1, GROUPS):
+            for a in range(PASSES):
+                v2_w[(g, a)] = shared([P, PACK, P], U32, f"v2_w{g}{a}", AT_COS10 + (PASSES * (g - 1) + a) * 2 * KB)
+        v2_s_picked = [kept([P, PASS], U8, "v2_s_picked0")] + [
+            shared([P, PASS], U8, f"v2_s_picked{g}", AT_W1_RAW + g * PASS) for g in range(1, GROUPS)
         ]
         v2_s_dealt = kept([P, S2], U8, "v2_s_dealt")
         v2_s = kept([P, S2], U8, "v2_s")
         nc.gpsimd.memset(v2_s[:].bitcast(I32), 0)
-        h_w = [[kept([P, n], U32, f"h_w{c}{a}") for a in range(NA)] for c, (j0, n) in enumerate(CHUNKS)]
-        h_s = [[kept([P, n], U8, f"h_s{c}{a}") for a in range(NA)] for c, (j0, n) in enumerate(CHUNKS)]
-        shift = kept([P, NG, PACK], F32, "shift")
-        mu_wh = kept([P, NG, PACK], F32, "mu_wh")
-        y_s = kept([P, NG, S], U8, "y_s")
-        y_w = [kept([P, NG, n], U32, f"y_w{c}") for c, (j0, n) in enumerate(CHUNKS)]
+        h_bf_at = {(0, 0): AT_W1_BF, (0, 1): AT_H01, (1, 1): AT_Y_BF + 2 * KB}
+        h_w = [[kept([P, HALF], U32, f"h_w{c}{a}") for a in range(PASSES)] for c in range(2)]
+        h_s = [[kept([P, HALF], U8, f"h_s{c}{a}") for a in range(PASSES)] for c in range(2)]
+        mu_wh = kept([P, GROUPS, PACK], F32, "mu_wh")
+        shift = kept([P, GROUPS, PACK], F32, "shift")
+        y_s = kept([P, GROUPS, S], U8, "y_s")
+        y_w = [kept([P, GROUPS, HALF], U32, f"y_w{c}") for c in range(2)]
+        cos_of, h_bf_of, y_of, rounded = {}, {}, {}, []
 
-        def entries(lst, j0, n):
-            return lst[:, j0 // LIST_ROWS : (j0 + n) // LIST_ROWS]
+        def entries(lst, part):
+            return lst[:, part * PASS // LIST_ROWS : (part + 1) * PASS // LIST_ROWS]
 
         def deal(out, in_):
             nc.vector.tensor_copy(
@@ -156,228 +151,192 @@ def tile_list_fourier_landmark_block_kernel(
             )
 
         def gather_v_scales(c):
-            j0, n = CHUNKS[c]
-            nc.vector.tensor_copy(v_s[c][:], tab_s[:].indirect(entries(idx, j0, n)))
+            nc.vector.tensor_copy(v_s[c][:], tab_s[:].indirect(entries(idx, c)))
 
         def gather_v_words(c):
-            j0, n = CHUNKS[c]
-            nc.vector.tensor_copy(v_w[c][:], tab_w[:].bitcast(U32).indirect(entries(idx, j0, n)))
+            nc.vector.tensor_copy(v_w[c][:], tab_w[:].bitcast(U32).indirect(entries(idx, c)))
 
-        def round_w1(a):
-            for u in range(pieces[a]):
-                m0 = u * (P // pieces[a])
-                cast = nc.scalar.copy if a == 0 else nc.vector.tensor_copy
+        def round_w1(a, cast):
+            for u, raw in enumerate(w1_raw[a]):
+                count = P // len(w1_raw[a])
                 cast(
-                    w1_bf[a][:, :, m0 : m0 + P // pieces[a], :].rearrange("p t m j -> p m j t"),
-                    w1_raw[a][u][:].rearrange("p j (m t) -> p m j t", t=PACK),
+                    w1_bf[a][:, :, u * count : (u + 1) * count, :].rearrange("p t m j -> p m t j"),
+                    raw[:].rearrange("p j (m t) -> p m t j", t=PACK),
                 )
 
         def quantize_w1(a):
             nc.vector.quantize_mx(
-                out=w1_w[a][:].bitcast(E4),
+                out=w1_w[a][:].bitcast(E4M3),
                 scales=w1_s[a][:],
                 in_=w1_bf[a][:].rearrange("p t m j -> p (t m j)"),
             )
 
         def gather_v2_words(g, a):
             nc.vector.tensor_copy(
-                v2_w[g][a][:].rearrange("p t m -> p m t"),
-                tab2_w[a][:].bitcast(U32).indirect(entries(idx2, g * PASS, PASS)),
+                v2_w[(g, a)][:].rearrange("p t m -> p m t"), tab2_w[a][:].bitcast(U32).indirect(entries(idx2, g))
             )
 
         def gather_v2_scales(g):
-            nc.vector.tensor_copy(v2_s_list[g][:], tab2_s[:].indirect(entries(idx2, g * PASS, PASS)))
-            deal(v2_s_dealt[:, g * PASS : (g + 1) * PASS], v2_s_list[g][:])
+            nc.vector.tensor_copy(v2_s_picked[g][:], tab2_s[:].indirect(entries(idx2, g)))
+            deal(v2_s_dealt[:, g * PASS : (g + 1) * PASS], v2_s_picked[g][:])
 
         def place_v2_scales():
-            for a in range(NA):
-                for quad in range(QUADS):
-                    src = 16 * a + 4 * quad
-                    dst = 32 * quad + 4 * a
-                    nc.sync.dma_start(v2_s[dst : dst + 4, :].bitcast(I32), v2_s_dealt[src : src + 4, :].bitcast(I32))
-
-        def gather_v2(g):
-            for a in range(NA):
-                gather_v2_words(g, a)
-
-        def gather_v(c):
-            gather_v_scales(c)
-            gather_v_words(c)
-
-        cos_of = {}
+            for a in range(PASSES):
+                for quad in range(QUADRANTS):
+                    src = BLOCKS * a + SCALE_ROWS * quad
+                    dst = QUADRANT * quad + SCALE_ROWS * a
+                    nc.sync.dma_start(
+                        v2_s[dst : dst + SCALE_ROWS, :].bitcast(I32), v2_s_dealt[src : src + SCALE_ROWS, :].bitcast(I32)
+                    )
 
         def cosines(c, a):
-            j0, n = CHUNKS[c]
-            dist = work.tile([P, PACK, n], F32, name="dist", tag="dist")
-            cosv = work.tile([P, PACK, n], F32, name="cosv", tag="cosv", bufs=3)
-            per_bank = PASS // n
+            dist = work.tile([P, PACK, HALF], F32, name="dist", tag="dist")
+            if (c, a) == (1, 0):
+                cos = shared([P, PACK, HALF], F32, "cos10", AT_COS10)
+            else:
+                cos = work.tile([P, PACK, HALF], F32, name="cos", tag="cos")
+            cos_of[(c, a)] = cos
             for t in range(PACK):
-                if t % per_bank == 0:
-                    p_bank = take(s_banks, s_used)[:].rearrange("p (t n) -> p t n", n=n)
+                p_bank = unit_banks[(c, a)][0][t]
                 nc.tensor.matmul_mx(
-                    out=p_bank[:, t % per_bank, :],
-                    lhsT=w1_w[a][:, t * P : (t + 1) * P].bitcast(E4),
+                    out=p_bank[:],
+                    lhsT=w1_w[a][:, t * P : (t + 1) * P].bitcast(E4M3),
                     lhsT_scale=w1_s[a][:, t * P : (t + 1) * P],
-                    rhs=v_w[c][:].bitcast(E4),
+                    rhs=v_w[c][:].bitcast(E4M3),
                     rhs_scale=v_s[c][:],
                     start=True,
                     stop=True,
                 )
-                if t % per_bank == per_bank - 1:
-                    for tt in range(t - per_bank + 1, t + 1):
-                        nc.scalar.activation(
-                            dist[:, tt, :], p_bank[:, tt % per_bank, :], ACT.Abs, bias=b_sb[:, a, tt : tt + 1]
-                        )
+                nc.scalar.activation(dist[:, t, :], p_bank[:], ACT.Abs, bias=b_sb[:, a, t : t + 1])
                 if t % 2 == 1:
                     nc.scalar.activation(
-                        cosv[:, t - 1 : t + 1, :], dist[:, t - 1 : t + 1, :], ACT.Sin, bias=math.pi / 2, scale=-1.0
+                        cos[:, t - 1 : t + 1, :], dist[:, t - 1 : t + 1, :], ACT.Sin, bias=math.pi / 2, scale=-1.0
                     )
-            cos_of[(c, a)] = cosv
 
         def features(c, a):
-            j0, n = CHUNKS[c]
-            cosv = cos_of[(c, a)]
-            if (c, a) in h_at:
-                h_bf = shared([P, n, PACK], BF16, f"h_bf{c}{a}", h_at[(c, a)])
+            if (c, a) in h_bf_at:
+                h_bf = shared([P, HALF, PACK], BF16, f"h_bf{c}{a}", h_bf_at[(c, a)])
             else:
-                h_bf = work.tile([P, n, PACK], BF16, name="h_bf", tag="h_bf", align_bytes=64)
-            for j in range(0, n, P):
-                q_bank = take(q_banks, q_used)[:].rearrange("p (t n) -> p t n", n=P)
+                h_bf = kept([P, HALF, PACK], BF16, f"h_bf{c}{a}")
+            h_bf_of[(c, a)] = h_bf
+            for j in range(0, HALF, P):
+                q_bank = unit_banks[(c, a)][1][j // P][:].rearrange("p (t n) -> p t n", n=P)
                 for t in range(PACK):
                     col = a * PASS + t * P
                     nc.tensor.matmul_mx(
                         out=q_bank[:, t, :],
-                        lhsT=w4_w[:, 2 * col : 2 * (col + P)].bitcast(E2),
+                        lhsT=w4_w[:, 2 * col : 2 * (col + P)].bitcast(E2M1),
                         lhsT_scale=w4_s[:, col : col + P],
-                        rhs=v_w[c][:, j : j + P].bitcast(E4),
+                        rhs=v_w[c][:, j : j + P].bitcast(E4M3),
                         rhs_scale=v_s[c][:, j : j + P],
                         start=True,
                         stop=True,
                     )
                 nc.vector.tensor_tensor(
-                    h_bf[:, j : j + P, :].rearrange("p (c i) t -> p c t i", i=2),
-                    q_bank.rearrange("p t (c i) -> p c t i", i=2),
-                    cosv[:, :, j : j + P].rearrange("p t (c i) -> p c t i", i=2),
+                    h_bf[:, j : j + P, :].rearrange("p (n i) t -> p n t i", i=2),
+                    q_bank.rearrange("p t (n i) -> p n t i", i=2),
+                    cos_of[(c, a)][:, :, j : j + P].rearrange("p t (n i) -> p n t i", i=2),
                     ALU.mult,
                 )
-            nc.vector.quantize_mx(
-                out=h_w[c][a][:].bitcast(E4),
-                scales=h_s[c][a][:],
-                in_=h_bf[:].rearrange("p n t -> p (n t)"),
-            )
 
-        y_of = {}
+        def quantize_h(c, a):
+            nc.vector.quantize_mx(
+                out=h_w[c][a][:].bitcast(E4M3),
+                scales=h_s[c][a][:],
+                in_=h_bf_of[(c, a)][:].rearrange("p n t -> p (n t)"),
+            )
 
         def block(c, g):
-            j0, n = CHUNKS[c]
-            y = work.tile([P, PACK, n], F32, name="y", tag="y", bufs=4)
-            per_bank = PASS // n
-            for t in range(PACK):
-                if t % per_bank == 0:
-                    c_bank = take(s_banks, s_used)[:].rearrange("p (t n) -> p t n", n=n)
-                for a in range(NA):
-                    nc.tensor.matmul_mx(
-                        out=c_bank[:, t % per_bank, :],
-                        lhsT=v2_w[g][a][:, t, :].bitcast(E4),
-                        lhsT_scale=v2_s[4 * a : P, g * PASS + t * P : g * PASS + (t + 1) * P],
-                        rhs=h_w[c][a][:].bitcast(E4),
-                        rhs_scale=h_s[c][a][:],
-                        start=(a == 0),
-                        stop=(a == NA - 1),
-                    )
-                if t % per_bank == per_bank - 1:
-                    for tt in range(t - per_bank + 1, t + 1):
-                        nc.scalar.activation(
-                            y[:, tt, :], c_bank[:, tt % per_bank, :], ACT.Identity,
-                            bias=shift[:, g, tt : tt + 1], scale=wh_sb[:, g, tt : tt + 1],
-                        )
-                if (t + 1) % (2 * per_bank) == 0:
-                    rows = out_0[g * PASS : (g + 1) * PASS, j0 : j0 + n].rearrange("(p t) j -> p t j", t=PACK)
-                    t0 = t + 1 - 2 * per_bank
-                    nc.sync.dma_start(rows[:, t0 : t + 1, :], y[:, t0 : t + 1, :])
+            y = kept([P, PACK, HALF], F32, f"y{c}{g}")
             y_of[(c, g)] = y
+            rows = out_0[g * PASS : (g + 1) * PASS, c * HALF : (c + 1) * HALF].rearrange("(p t) j -> p t j", t=PACK)
+            for t in range(PACK):
+                col = g * PASS + t * P
+                for a in reversed(range(PASSES)):
+                    nc.tensor.matmul_mx(
+                        out=high[t][:],
+                        lhsT=v2_w[(g, a)][:, t, :].bitcast(E4M3),
+                        lhsT_scale=v2_s[SCALE_ROWS * a : P, col : col + P],
+                        rhs=h_w[c][a][:].bitcast(E4M3),
+                        rhs_scale=h_s[c][a][:],
+                        start=(a == PASSES - 1),
+                        stop=(a == 0),
+                    )
+                nc.scalar.activation(
+                    y[:, t, :], high[t][:], ACT.Identity, bias=shift[:, g, t : t + 1], scale=wh_sb[:, g, t : t + 1]
+                )
+                if t % 2 == 1:
+                    nc.sync.dma_start(rows[:, t - 1 : t + 1, :], y[:, t - 1 : t + 1, :])
 
-        def planes(c, g):
-            j0, n = CHUNKS[c]
-            y = y_of[(c, g)]
-            y_bf = work.tile([P, n, PACK], BF16, name="y_bf", tag="y_bf", align_bytes=64)
-            nc.vector.tensor_copy(
-                y_bf[:].rearrange("p (c i) t -> p c t i", i=2),
-                y[:].rearrange("p t (c i) -> p c t i", i=2),
+        def planes(c, g, j0, n, cast):
+            y_bf = shared([P, n, PACK], BF16, f"y_bf{len(rounded)}", AT_Y_BF + (len(rounded) + 1) % 2 * 4 * KB)
+            rounded.append(y_bf)
+            cast(
+                y_bf[:].rearrange("p (n i) t -> p n t i", i=2),
+                y_of[(c, g)][:, :, j0 : j0 + n].rearrange("p t (n i) -> p n t i", i=2),
             )
             nc.vector.quantize_mx(
-                out=y_w[c][:, g, :].bitcast(E4),
-                scales=y_s[:, g, j0 : j0 + n],
+                out=y_w[c][:, g, j0 : j0 + n].bitcast(E4M3),
+                scales=y_s[:, g, c * HALF + j0 : c * HALF + j0 + n],
                 in_=y_bf[:].rearrange("p n t -> p (n t)"),
             )
 
-        def store_words(c, g0, g1):
-            j0, n = CHUNKS[c]
+        def store_words(c, g):
             nc.sync.dma_start(
-                out_1[g0:g1, :, j0 : j0 + n, :].rearrange("g p n t -> p g (n t)").bitcast(I32),
-                y_w[c][:, g0:g1, :].bitcast(I32),
+                out_1[g, :, c * HALF : (c + 1) * HALF, :].rearrange("p n t -> p (n t)").bitcast(I32),
+                y_w[c][:, g, :].bitcast(I32),
             )
 
         def store_scales():
-            for quad in range(QUADS):
+            for quad in range(QUADRANTS):
                 nc.sync.dma_start(
-                    out_2[:, 4 * quad : 4 * quad + 4, :].bitcast(I32).rearrange("g r n -> r g n"),
-                    y_s[32 * quad : 32 * quad + 4, :, :].bitcast(I32),
+                    out_2[:, SCALE_ROWS * quad : SCALE_ROWS * (quad + 1), :].bitcast(I32).rearrange("g r n -> r g n"),
+                    y_s[QUADRANT * quad : QUADRANT * quad + SCALE_ROWS, :, :].bitcast(I32),
                 )
 
         gather_v_scales(0)
-        round_w1(0)
+        round_w1(0, nc.scalar.copy)
         quantize_w1(0)
         gather_v_words(0)
-        gather_v(1)
-        gather_v_scales(2)
+        gather_v_scales(1)
+        gather_v_words(1)
         gather_v2_scales(0)
         deal(w4_w[:].bitcast(U16), w4_w_raw[:].bitcast(U16))
         deal(w4_s[:], w4_s_raw[:])
-        round_w1(1)
-        load_words(tab2_w[1], tab2_words[1], nc.scalar)
+        round_w1(1, nc.vector.tensor_copy)
+        load_words(nc.scalar, tab2_w[1], tab2_words[1])
         quantize_w1(1)
-        gather_v2_scales(1)
+        for g in range(1, GROUPS):
+            gather_v2_scales(g)
+        place_v2_scales()
         nc.gpsimd.tensor_tensor(mu_wh[:], mu_sb[:], wh_sb[:], ALU.mult)
         nc.gpsimd.tensor_scalar(shift[:], mu_wh[:], -1.0, 0.0, ALU.mult, ALU.add)
-        cosines(0, 0)
-        features(0, 0)
-        gather_v2_scales(2)
-        place_v2_scales()
-        gather_v2(0)
-        cosines(0, 1)
-        features(0, 1)
-        gather_v_words(2)
+
+        for a in range(PASSES):
+            cosines(0, a)
+            features(0, a)
+            quantize_h(0, a)
+            gather_v2_words(0, a)
         cosines(1, 0)
+        features(1, 0)
+        for g in range(1, GROUPS):
+            for a in reversed(range(PASSES)):
+                gather_v2_words(g, a)
+        quantize_h(1, 0)
         cosines(1, 1)
         block(0, 0)
-        gather_v2(1)
-        features(1, 0)
-        block(0, 1)
-        gather_v2(2)
         features(1, 1)
-        block(0, 2)
-        planes(0, 0)
-        cosines(2, 0)
-        cosines(2, 1)
-        features(2, 0)
-        features(2, 1)
-        block(1, 0)
-        planes(0, 1)
-        block(1, 1)
-        planes(0, 2)
-        block(1, 2)
-        store_words(0, 0, 3)
-        planes(1, 0)
-        planes(1, 1)
-        block(2, 0)
-        planes(1, 2)
-        block(2, 1)
-        store_words(1, 0, 3)
-        planes(2, 0)
-        block(2, 2)
-        planes(2, 1)
-        store_words(2, 0, 2)
-        planes(2, 2)
-        store_words(2, 2, 3)
+        quantize_h(1, 1)
+        for g in range(1, GROUPS):
+            block(0, g)
+        for g in range(GROUPS):
+            planes(0, g, 0, HALF, nc.vector.tensor_copy)
+            block(1, g)
+            store_words(0, g)
+        for g in range(GROUPS - 1):
+            planes(1, g, 0, HALF, nc.vector.tensor_copy)
+            store_words(1, g)
+        planes(1, GROUPS - 1, 0, HALF // 2, nc.scalar.copy)
+        planes(1, GROUPS - 1, HALF // 2, HALF // 2, nc.vector.tensor_copy)
+        store_words(1, GROUPS - 1)
         store_scales()

@@ -23,6 +23,7 @@ PASS = P * PACK
 PASSES = H // PASS
 GROUPS = S2 // PASS
 HALF = S // 2
+QUARTER = HALF // 2
 QUADRANTS = 4
 QUADRANT = P // QUADRANTS
 SCALE_ROWS = 4
@@ -66,10 +67,10 @@ def tile_list_fourier_landmark_block_kernel(
         tab_s = kept([P, T], U8, "tab_s")
         w4_s_raw = kept([P, H], U8, "w4_s_raw")
         tab2_s = kept([P, T2], U8, "tab2_s")
-        for plane in (tab_s, w4_s_raw):
-            nc.vector.memset(plane[:].bitcast(I32), 0)
+        nc.gpsimd.memset(tab_s[:].bitcast(I32), 0)
         nc.gpsimd.memset(warm[:, 0:1], 0.0)
-        nc.gpsimd.memset(tab2_s[:].bitcast(I32), 0)
+        for plane in (tab2_s, w4_s_raw):
+            nc.vector.memset(plane[:].bitcast(I32), 0)
         nc.scalar.activation(warm[:, 1:2], warm[:, 0:1], ACT.Sin)
 
         tab_w = kept([P, T], I32, "tab_w")
@@ -99,13 +100,13 @@ def tile_list_fourier_landmark_block_kernel(
             queue.dma_start(tile[:], words.rearrange("p n i -> p (n i)").bitcast(I32))
 
         nc.sync.dma_start(idx[:], offs)
-        load_w1(0, 0)
+        nc.sync.dma_start(idx2[:], offs2)
         load_scale_rows(tab_s, tab_scales)
+        load_w1(0, 0)
         nc.sync.dma_start(
             tab2_s[0 : BLOCKS * PASSES, :].bitcast(I32), tab2_scales.rearrange("a q t -> (a q) t").bitcast(I32)
         )
         load_w1(0, 1)
-        nc.sync.dma_start(idx2[:], offs2)
         load_words(nc.sync, tab_w, tab_words[0])
         nc.sync.dma_start(w4_w_raw[:].bitcast(I32), w4_words[0].bitcast(I32))
         load_scale_rows(w4_s_raw, w4_scales)
@@ -122,13 +123,12 @@ def tile_list_fourier_landmark_block_kernel(
         w1_bf = [kept([P, PACK, P, PACK], BF16, "w1_bf0"), shared([P, PACK, P, PACK], BF16, "w1_bf1", AT_W1_BF)]
         w1_w = [kept([P, PASS], U32, f"w1_w{a}") for a in range(PASSES)]
         w1_s = [kept([P, PASS], U8, f"w1_s{a}") for a in range(PASSES)]
-        v2_w = {(0, 0): kept([P, PACK, P], U32, "v2_w00"), (0, 1): shared([P, PACK, P], U32, "v2_w01", AT_H01)}
-        for g in range(1, GROUPS):
-            for a in range(PASSES):
-                v2_w[(g, a)] = shared([P, PACK, P], U32, f"v2_w{g}{a}", AT_COS10 + (PASSES * (g - 1) + a) * 2 * KB)
-        v2_s_picked = [kept([P, PASS], U8, "v2_s_picked0")] + [
-            shared([P, PASS], U8, f"v2_s_picked{g}", AT_W1_RAW + g * PASS) for g in range(1, GROUPS)
-        ]
+        v2_w = {(g, 0): kept([P, PACK, P], U32, f"v2_w{g}0") for g in range(2)}
+        v2_w[(0, 1)] = shared([P, PACK, P], U32, "v2_w01", AT_H01)
+        for slot, (g, a) in enumerate([(1, 1), (2, 0), (2, 1)]):
+            v2_w[(g, a)] = shared([P, PACK, P], U32, f"v2_w{g}{a}", AT_COS10 + slot * 2 * KB)
+        v2_s_picked = [kept([P, PASS], U8, f"v2_s_picked{g}") for g in range(GROUPS - 1)]
+        v2_s_picked.append(shared([P, PASS], U8, "v2_s_picked2", AT_W1_RAW))
         v2_s_dealt = kept([P, S2], U8, "v2_s_dealt")
         v2_s = kept([P, S2], U8, "v2_s")
         nc.gpsimd.memset(v2_s[:].bitcast(I32), 0)
@@ -215,9 +215,10 @@ def tile_list_fourier_landmark_block_kernel(
 
         def features(c, a):
             if (c, a) in h_bf_at:
-                h_bf = shared([P, HALF, PACK], BF16, f"h_bf{c}{a}", h_bf_at[(c, a)])
+                at = h_bf_at[(c, a)]
+                h_bf = [shared([P, QUARTER, PACK], BF16, f"h_bf{c}{a}{u}", at + u * 2 * KB) for u in range(2)]
             else:
-                h_bf = kept([P, HALF, PACK], BF16, f"h_bf{c}{a}")
+                h_bf = [kept([P, QUARTER, PACK], BF16, f"h_bf{c}{a}{u}") for u in range(2)]
             h_bf_of[(c, a)] = h_bf
             for j in range(0, HALF, P):
                 q_bank = unit_banks[(c, a)][1][j // P][:].rearrange("p (t n) -> p t n", n=P)
@@ -233,18 +234,19 @@ def tile_list_fourier_landmark_block_kernel(
                         stop=True,
                     )
                 nc.vector.tensor_tensor(
-                    h_bf[:, j : j + P, :].rearrange("p (n i) t -> p n t i", i=2),
+                    h_bf[j // QUARTER][:, j % QUARTER : j % QUARTER + P, :].rearrange("p (n i) t -> p n t i", i=2),
                     q_bank.rearrange("p t (n i) -> p n t i", i=2),
                     cos_of[(c, a)][:, :, j : j + P].rearrange("p t (n i) -> p n t i", i=2),
                     ALU.mult,
                 )
 
         def quantize_h(c, a):
-            nc.vector.quantize_mx(
-                out=h_w[c][a][:].bitcast(E4M3),
-                scales=h_s[c][a][:],
-                in_=h_bf_of[(c, a)][:].rearrange("p n t -> p (n t)"),
-            )
+            for u, h_bf in enumerate(h_bf_of[(c, a)]):
+                nc.vector.quantize_mx(
+                    out=h_w[c][a][:, u * QUARTER : (u + 1) * QUARTER].bitcast(E4M3),
+                    scales=h_s[c][a][:, u * QUARTER : (u + 1) * QUARTER],
+                    in_=h_bf[:].rearrange("p n t -> p (n t)"),
+                )
 
         def block(c, g):
             y = kept([P, PACK, HALF], F32, f"y{c}{g}")
@@ -269,7 +271,7 @@ def tile_list_fourier_landmark_block_kernel(
                     nc.sync.dma_start(rows[:, t - 1 : t + 1, :], y[:, t - 1 : t + 1, :])
 
         def planes(c, g, j0, n, cast):
-            y_bf = shared([P, n, PACK], BF16, f"y_bf{len(rounded)}", AT_Y_BF + (len(rounded) + 1) % 2 * 4 * KB)
+            y_bf = shared([P, n, PACK], BF16, f"y_bf{len(rounded)}", AT_Y_BF + len(rounded) % 2 * 4 * KB)
             rounded.append(y_bf)
             cast(
                 y_bf[:].rearrange("p (n i) t -> p n t i", i=2),

@@ -31,11 +31,11 @@ BLOCKS = QUADRANTS * SCALE_ROWS
 LIST_ROWS = 16
 
 KB = 1024
-AT_W1_BF = 0
-AT_H01 = 4 * KB
-AT_COS10 = 8 * KB
-AT_Y_BF = 16 * KB
-AT_W1_RAW = 24 * KB
+AT_W1_RAW0 = 0
+AT_W1_RAW1 = 4 * KB
+AT_COS11 = 12 * KB
+AT_TAB2 = 20 * KB
+AT_W1_BF = 52 * KB
 
 
 def tile_list_fourier_landmark_block_kernel(
@@ -47,6 +47,7 @@ def tile_list_fourier_landmark_block_kernel(
         lists = ctx.enter_context(tc.tile_pool(name="lists", bufs=1))
         keep = ctx.enter_context(tc.tile_pool(name="keep", bufs=1))
         work = ctx.enter_context(tc.tile_pool(name="work", bufs=2))
+        rounded = ctx.enter_context(tc.tile_pool(name="rounded", bufs=3))
         reuse = ctx.enter_context(tc.tile_pool(name="reuse", bufs=1))
         psum = ctx.enter_context(tc.psum_pool(name="psum", bufs=1))
 
@@ -60,25 +61,23 @@ def tile_list_fourier_landmark_block_kernel(
         idx2 = lists.tile([P, S2 // LIST_ROWS], U16, name="idx2")
 
         banks = [psum.tile([P, PASS], F32, name=f"bank{i}") for i in range(2 * PACK)]
-        low, high = banks[:PACK], banks[PACK:]
-        unit_banks = {(0, 0): (low, high), (0, 1): (low, low), (1, 0): (high, high), (1, 1): (low, low)}
+        scalar_banks, vector_banks = banks[:PACK], banks[PACK:]
 
         warm = kept([P, 2], F32, "warm")
         tab_s = kept([P, T], U8, "tab_s")
-        w4_s_raw = kept([P, H], U8, "w4_s_raw")
+        w4_s_raw = shared([P, H], U8, "w4_s_raw", AT_W1_BF)
         tab2_s = kept([P, T2], U8, "tab2_s")
-        nc.gpsimd.memset(tab_s[:].bitcast(I32), 0)
         nc.gpsimd.memset(warm[:, 0:1], 0.0)
-        for plane in (tab2_s, w4_s_raw):
+        for plane in (tab_s, w4_s_raw, tab2_s):
             nc.vector.memset(plane[:].bitcast(I32), 0)
         nc.scalar.activation(warm[:, 1:2], warm[:, 0:1], ACT.Sin)
 
         tab_w = kept([P, T], I32, "tab_w")
         w4_w_raw = kept([P, 2 * H], U8, "w4_w_raw")
-        tab2_w = [kept([P, T2], I32, "tab2_w0"), shared([P, T2], I32, "tab2_w1", AT_W1_RAW + 2 * KB)]
+        tab2_w = [shared([P, T2], I32, f"tab2_w{a}", AT_TAB2 + a * 16 * KB) for a in range(PASSES)]
         w1_raw = [
-            [kept([P, PACK, PASS // 2], F32, f"w1_raw0{u}") for u in range(2)],
-            [shared([P, PACK, PASS], F32, "w1_raw1", AT_W1_RAW)],
+            [kept([P, PACK, PASS // 2], F32, "w1_raw00"), shared([P, PACK, PASS // 2], F32, "w1_raw01", AT_W1_RAW0)],
+            [shared([P, PACK, PASS], F32, "w1_raw1", AT_W1_RAW1)],
         ]
         b_sb = kept([P, PASSES, PACK], F32, "b_sb")
         mu_sb = kept([P, GROUPS, PACK], F32, "mu_sb")
@@ -96,50 +95,55 @@ def tile_list_fourier_landmark_block_kernel(
                     scales[0, SCALE_ROWS * quad : SCALE_ROWS * (quad + 1), :].bitcast(I32),
                 )
 
-        def load_words(queue, tile, words):
-            queue.dma_start(tile[:], words.rearrange("p n i -> p (n i)").bitcast(I32))
+        def load_words(tile, words):
+            nc.sync.dma_start(tile[:], words.rearrange("p n i -> p (n i)").bitcast(I32))
 
         nc.sync.dma_start(idx[:], offs)
         nc.sync.dma_start(idx2[:], offs2)
         load_scale_rows(tab_s, tab_scales)
+        load_words(tab_w, tab_words[0])
         load_w1(0, 0)
+        load_w1(0, 1)
+        nc.sync.dma_start(w4_w_raw[:].bitcast(I32), w4_words[0].bitcast(I32))
+        load_scale_rows(w4_s_raw, w4_scales)
         nc.sync.dma_start(
             tab2_s[0 : BLOCKS * PASSES, :].bitcast(I32), tab2_scales.rearrange("a q t -> (a q) t").bitcast(I32)
         )
-        load_w1(0, 1)
-        load_words(nc.sync, tab_w, tab_words[0])
-        nc.sync.dma_start(w4_w_raw[:].bitcast(I32), w4_words[0].bitcast(I32))
-        load_scale_rows(w4_s_raw, w4_scales)
         load_w1(1, 0)
-        load_words(nc.sync, tab2_w[0], tab2_words[0])
+        for a in range(PASSES):
+            load_words(tab2_w[a], tab2_words[a])
         nc.gpsimd.dma_start(b_sb[:], b.rearrange("(a p t) -> p a t", p=P, t=PACK))
         nc.gpsimd.dma_start(mu_sb[:], mu.rearrange("(g p t) -> p g t", p=P, t=PACK))
         nc.gpsimd.dma_start(wh_sb[:], wh.rearrange("(g p t) -> p g t", p=P, t=PACK))
 
-        w4_w = kept([P, 2 * H], U8, "w4_w")
+        w4_w = shared([P, 2 * H], U8, "w4_w", AT_W1_RAW0)
         w4_s = kept([P, H], U8, "w4_s")
-        v_w = [kept([P, HALF], U32, f"v_w{c}") for c in range(2)]
-        v_s = [kept([P, HALF], U8, f"v_s{c}") for c in range(2)]
+        v_w = kept([P, S], U32, "v_w")
+        v_s = kept([P, S], U8, "v_s")
         w1_bf = [kept([P, PACK, P, PACK], BF16, "w1_bf0"), shared([P, PACK, P, PACK], BF16, "w1_bf1", AT_W1_BF)]
         w1_w = [kept([P, PASS], U32, f"w1_w{a}") for a in range(PASSES)]
         w1_s = [kept([P, PASS], U8, f"w1_s{a}") for a in range(PASSES)]
-        v2_w = {(g, 0): kept([P, PACK, P], U32, f"v2_w{g}0") for g in range(2)}
-        v2_w[(0, 1)] = shared([P, PACK, P], U32, "v2_w01", AT_H01)
-        for slot, (g, a) in enumerate([(1, 1), (2, 0), (2, 1)]):
-            v2_w[(g, a)] = shared([P, PACK, P], U32, f"v2_w{g}{a}", AT_COS10 + slot * 2 * KB)
-        v2_s_picked = [kept([P, PASS], U8, f"v2_s_picked{g}") for g in range(GROUPS - 1)]
-        v2_s_picked.append(shared([P, PASS], U8, "v2_s_picked2", AT_W1_RAW))
-        v2_s_dealt = kept([P, S2], U8, "v2_s_dealt")
+        v2_w = {(0, a): kept([P, PACK, P], U32, f"v2_w0{a}") for a in range(PASSES)}
+        for g in range(1, GROUPS):
+            for a in range(PASSES):
+                v2_w[(g, a)] = shared([P, PACK, P], U32, f"v2_w{g}{a}", AT_COS11 + (2 * g + a - 2) * 2 * KB)
+        v2_s_picked = kept([P, S2], U8, "v2_s_picked")
+        v2_s_dealt = shared([P, S2], U8, "v2_s_dealt", AT_W1_RAW1)
         v2_s = kept([P, S2], U8, "v2_s")
         nc.gpsimd.memset(v2_s[:].bitcast(I32), 0)
-        h_bf_at = {(0, 0): AT_W1_BF, (0, 1): AT_H01, (1, 1): AT_Y_BF + 2 * KB}
-        h_w = [[kept([P, HALF], U32, f"h_w{c}{a}") for a in range(PASSES)] for c in range(2)]
-        h_s = [[kept([P, HALF], U8, f"h_s{c}{a}") for a in range(PASSES)] for c in range(2)]
-        mu_wh = kept([P, GROUPS, PACK], F32, "mu_wh")
+        h_w = {(c, a): kept([P, HALF], U32, f"h_w{c}{a}")[:] for c in range(2) for a in range(PASSES)}
+        h_s = {(c, a): kept([P, HALF], U8, f"h_s{c}{a}")[:] for c in range(2) for a in range(PASSES)}
+        mu_wh = shared([P, GROUPS, PACK], F32, "mu_wh", AT_W1_RAW1 + 2 * KB)
         shift = kept([P, GROUPS, PACK], F32, "shift")
         y_s = kept([P, GROUPS, S], U8, "y_s")
         y_w = [kept([P, GROUPS, HALF], U32, f"y_w{c}") for c in range(2)]
-        cos_of, h_bf_of, y_of, rounded = {}, {}, {}, []
+        y_at = {key: AT_TAB2 + slot * 8 * KB for slot, key in enumerate([(1, 1), (0, 2), (1, 2)])}
+        cos_of, h_bf_of, y_of, y_bf_of = {}, {}, {}, {}
+
+        def placed(shape, dtype, name, offsets, key):
+            if key in offsets:
+                return shared(shape, dtype, name, offsets[key])
+            return kept(shape, dtype, name)
 
         def entries(lst, part):
             return lst[:, part * PASS // LIST_ROWS : (part + 1) * PASS // LIST_ROWS]
@@ -150,35 +154,29 @@ def tile_list_fourier_landmark_block_kernel(
                 in_.rearrange("p (g m t) -> p g t m", t=PACK, m=P),
             )
 
-        def gather_v_scales(c):
-            nc.vector.tensor_copy(v_s[c][:], tab_s[:].indirect(entries(idx, c)))
+        def gpsimd_cast(out, in_):
+            nc.gpsimd.tensor_scalar(out, in_, 1.0, 0.0, ALU.mult, ALU.add)
 
-        def gather_v_words(c):
-            nc.vector.tensor_copy(v_w[c][:], tab_w[:].bitcast(U32).indirect(entries(idx, c)))
-
-        def round_w1(a, cast):
-            for u, raw in enumerate(w1_raw[a]):
-                count = P // len(w1_raw[a])
-                cast(
-                    w1_bf[a][:, :, u * count : (u + 1) * count, :].rearrange("p t m j -> p m t j"),
-                    raw[:].rearrange("p j (m t) -> p m t j", t=PACK),
-                )
-
-        def quantize_w1(a):
-            nc.vector.quantize_mx(
-                out=w1_w[a][:].bitcast(E4M3),
-                scales=w1_s[a][:],
-                in_=w1_bf[a][:].rearrange("p t m j -> p (t m j)"),
+        def round_w1(a, u, cast, ms, ts):
+            m0 = u * P // len(w1_raw[a])
+            cast(
+                w1_bf[a][:, ts, m0 + ms.start : m0 + ms.stop, :].rearrange("p t m j -> p m t j"),
+                w1_raw[a][u][:].rearrange("p j (m t) -> p m t j", t=PACK)[:, ms, ts, :],
             )
+
+        def quantize_w1(a, pieces):
+            width = PASS // pieces
+            for c0 in range(0, PASS, width):
+                nc.vector.quantize_mx(
+                    out=w1_w[a][:, c0 : c0 + width].bitcast(E4M3),
+                    scales=w1_s[a][:, c0 : c0 + width],
+                    in_=w1_bf[a][:].rearrange("p t m j -> p (t m j)")[:, PACK * c0 : PACK * (c0 + width)],
+                )
 
         def gather_v2_words(g, a):
             nc.vector.tensor_copy(
                 v2_w[(g, a)][:].rearrange("p t m -> p m t"), tab2_w[a][:].bitcast(U32).indirect(entries(idx2, g))
             )
-
-        def gather_v2_scales(g):
-            nc.vector.tensor_copy(v2_s_picked[g][:], tab2_s[:].indirect(entries(idx2, g)))
-            deal(v2_s_dealt[:, g * PASS : (g + 1) * PASS], v2_s_picked[g][:])
 
         def place_v2_scales():
             for a in range(PASSES):
@@ -191,97 +189,112 @@ def tile_list_fourier_landmark_block_kernel(
 
         def cosines(c, a):
             dist = work.tile([P, PACK, HALF], F32, name="dist", tag="dist")
-            if (c, a) == (1, 0):
-                cos = shared([P, PACK, HALF], F32, "cos10", AT_COS10)
+            if (c, a) == (1, 1):
+                cos = shared([P, PACK, HALF], F32, "cos11", AT_COS11)
             else:
                 cos = work.tile([P, PACK, HALF], F32, name="cos", tag="cos")
             cos_of[(c, a)] = cos
             for t in range(PACK):
-                p_bank = unit_banks[(c, a)][0][t]
                 nc.tensor.matmul_mx(
-                    out=p_bank[:],
+                    out=scalar_banks[t][:],
                     lhsT=w1_w[a][:, t * P : (t + 1) * P].bitcast(E4M3),
                     lhsT_scale=w1_s[a][:, t * P : (t + 1) * P],
-                    rhs=v_w[c][:].bitcast(E4M3),
-                    rhs_scale=v_s[c][:],
+                    rhs=v_w[:, c * HALF : (c + 1) * HALF].bitcast(E4M3),
+                    rhs_scale=v_s[:, c * HALF : (c + 1) * HALF],
                     start=True,
                     stop=True,
                 )
-                nc.scalar.activation(dist[:, t, :], p_bank[:], ACT.Abs, bias=b_sb[:, a, t : t + 1])
-                if t % 2 == 1:
-                    nc.scalar.activation(
-                        cos[:, t - 1 : t + 1, :], dist[:, t - 1 : t + 1, :], ACT.Sin, bias=math.pi / 2, scale=-1.0
-                    )
+                nc.scalar.activation(dist[:, t, :], scalar_banks[t][:], ACT.Abs, bias=b_sb[:, a, t : t + 1])
+            for e in range(2):
+                nc.scalar.activation(
+                    cos[:].rearrange("p t (u e n) -> p (t u) e n", e=2, n=P)[:, :, e, :],
+                    dist[:].rearrange("p t (u e n) -> p (t u) e n", e=2, n=P)[:, :, e, :],
+                    ACT.Sin,
+                    bias=math.pi / 2,
+                    scale=-1.0,
+                )
 
         def features(c, a):
-            if (c, a) in h_bf_at:
-                at = h_bf_at[(c, a)]
-                h_bf = [shared([P, QUARTER, PACK], BF16, f"h_bf{c}{a}{u}", at + u * 2 * KB) for u in range(2)]
-            else:
-                h_bf = [kept([P, QUARTER, PACK], BF16, f"h_bf{c}{a}{u}") for u in range(2)]
+            h_bf = [kept([P, QUARTER, PACK], BF16, f"h_bf{c}{a}{u}") for u in range(2)]
             h_bf_of[(c, a)] = h_bf
-            for j in range(0, HALF, P):
-                q_bank = unit_banks[(c, a)][1][j // P][:].rearrange("p (t n) -> p t n", n=P)
-                for t in range(PACK):
-                    col = a * PASS + t * P
-                    nc.tensor.matmul_mx(
-                        out=q_bank[:, t, :],
-                        lhsT=w4_w[:, 2 * col : 2 * (col + P)].bitcast(E2M1),
-                        lhsT_scale=w4_s[:, col : col + P],
-                        rhs=v_w[c][:, j : j + P].bitcast(E4M3),
-                        rhs_scale=v_s[c][:, j : j + P],
-                        start=True,
-                        stop=True,
+            for e in range(2):
+                for u in range(2):
+                    j = u * QUARTER + e * P
+                    q_bank = vector_banks[2 * e + u][:].rearrange("p (t n) -> p t n", n=P)
+                    for t in range(PACK):
+                        col = a * PASS + t * P
+                        nc.tensor.matmul_mx(
+                            out=q_bank[:, t, :],
+                            lhsT=w4_w[:, 2 * col : 2 * (col + P)].bitcast(E2M1),
+                            lhsT_scale=w4_s[:, col : col + P],
+                            rhs=v_w[:, c * HALF + j : c * HALF + j + P].bitcast(E4M3),
+                            rhs_scale=v_s[:, c * HALF + j : c * HALF + j + P],
+                            start=True,
+                            stop=True,
+                        )
+                    nc.vector.tensor_tensor(
+                        h_bf[u][:, e * P : (e + 1) * P, :].rearrange("p (n i) t -> p n t i", i=2),
+                        q_bank.rearrange("p t (n i) -> p n t i", i=2),
+                        cos_of[(c, a)][:, :, j : j + P].rearrange("p t (n i) -> p n t i", i=2),
+                        ALU.mult,
                     )
-                nc.vector.tensor_tensor(
-                    h_bf[j // QUARTER][:, j % QUARTER : j % QUARTER + P, :].rearrange("p (n i) t -> p n t i", i=2),
-                    q_bank.rearrange("p t (n i) -> p n t i", i=2),
-                    cos_of[(c, a)][:, :, j : j + P].rearrange("p t (n i) -> p n t i", i=2),
-                    ALU.mult,
-                )
 
         def quantize_h(c, a):
             for u, h_bf in enumerate(h_bf_of[(c, a)]):
                 nc.vector.quantize_mx(
-                    out=h_w[c][a][:, u * QUARTER : (u + 1) * QUARTER].bitcast(E4M3),
-                    scales=h_s[c][a][:, u * QUARTER : (u + 1) * QUARTER],
+                    out=h_w[(c, a)][:, u * QUARTER : (u + 1) * QUARTER].bitcast(E4M3),
+                    scales=h_s[(c, a)][:, u * QUARTER : (u + 1) * QUARTER],
                     in_=h_bf[:].rearrange("p n t -> p (n t)"),
                 )
 
-        def block(c, g):
-            y = kept([P, PACK, HALF], F32, f"y{c}{g}")
+        def block(c, g, bank_set=scalar_banks):
+            y = placed([P, PACK, HALF], F32, f"y{c}{g}", y_at, (c, g))
             y_of[(c, g)] = y
             rows = out_0[g * PASS : (g + 1) * PASS, c * HALF : (c + 1) * HALF].rearrange("(p t) j -> p t j", t=PACK)
             for t in range(PACK):
                 col = g * PASS + t * P
                 for a in reversed(range(PASSES)):
                     nc.tensor.matmul_mx(
-                        out=high[t][:],
+                        out=bank_set[t][:],
                         lhsT=v2_w[(g, a)][:, t, :].bitcast(E4M3),
                         lhsT_scale=v2_s[SCALE_ROWS * a : P, col : col + P],
-                        rhs=h_w[c][a][:].bitcast(E4M3),
-                        rhs_scale=h_s[c][a][:],
+                        rhs=h_w[(c, a)].bitcast(E4M3),
+                        rhs_scale=h_s[(c, a)],
                         start=(a == PASSES - 1),
                         stop=(a == 0),
                     )
                 nc.scalar.activation(
-                    y[:, t, :], high[t][:], ACT.Identity, bias=shift[:, g, t : t + 1], scale=wh_sb[:, g, t : t + 1]
+                    y[:, t, :],
+                    bank_set[t][:],
+                    ACT.Identity,
+                    bias=shift[:, g, t : t + 1],
+                    scale=wh_sb[:, g, t : t + 1],
                 )
                 if t % 2 == 1:
                     nc.sync.dma_start(rows[:, t - 1 : t + 1, :], y[:, t - 1 : t + 1, :])
 
-        def planes(c, g, j0, n, cast):
-            y_bf = shared([P, n, PACK], BF16, f"y_bf{len(rounded)}", AT_Y_BF + len(rounded) % 2 * 4 * KB)
-            rounded.append(y_bf)
-            cast(
-                y_bf[:].rearrange("p (n i) t -> p n t i", i=2),
-                y_of[(c, g)][:, :, j0 : j0 + n].rearrange("p t (n i) -> p n t i", i=2),
-            )
+        def round_y(c, g, u, cast, pairs=True):
+            y_bf = rounded.tile([P, QUARTER, PACK], BF16, name="y_bf", tag=f"y_bf{u}", align_bytes=64)
+            y_bf_of[(c, g, u)] = y_bf
+            y = y_of[(c, g)][:, :, u * QUARTER : (u + 1) * QUARTER]
+            if pairs:
+                cast(y_bf[:].rearrange("p (n i) t -> p n t i", i=2), y.rearrange("p t (n i) -> p n t i", i=2))
+            else:
+                cast(y_bf[:], y.rearrange("p t n -> p n t"))
+
+        def quantize_y(c, g, u):
+            j0 = u * QUARTER
             nc.vector.quantize_mx(
-                out=y_w[c][:, g, j0 : j0 + n].bitcast(E4M3),
-                scales=y_s[:, g, c * HALF + j0 : c * HALF + j0 + n],
-                in_=y_bf[:].rearrange("p n t -> p (n t)"),
+                out=y_w[c][:, g, j0 : j0 + QUARTER].bitcast(E4M3),
+                scales=y_s[:, g, c * HALF + j0 : c * HALF + j0 + QUARTER],
+                in_=y_bf_of[(c, g, u)][:].rearrange("p n t -> p (n t)"),
             )
+
+        def planes(c, g, casts):
+            for u in range(2):
+                round_y(c, g, u, casts[u])
+            for u in range(2):
+                quantize_y(c, g, u)
 
         def store_words(c, g):
             nc.sync.dma_start(
@@ -296,49 +309,52 @@ def tile_list_fourier_landmark_block_kernel(
                     y_s[QUADRANT * quad : QUADRANT * quad + SCALE_ROWS, :, :].bitcast(I32),
                 )
 
-        gather_v_scales(0)
-        round_w1(0, nc.scalar.copy)
-        quantize_w1(0)
-        gather_v_words(0)
-        gather_v_scales(1)
-        gather_v_words(1)
-        gather_v2_scales(0)
+        nc.vector.tensor_copy(v_s[:], tab_s[:].indirect(idx[:]))
+        nc.vector.tensor_copy(v_w[:], tab_w[:].bitcast(U32).indirect(idx[:]))
+        round_w1(0, 0, nc.scalar.copy, slice(0, P // 2), slice(0, PACK))
+        round_w1(0, 1, nc.vector.tensor_copy, slice(0, P // 2), slice(0, 2))
+        round_w1(0, 1, nc.scalar.copy, slice(0, P // 2), slice(2, PACK))
+        quantize_w1(0, 2)
         deal(w4_w[:].bitcast(U16), w4_w_raw[:].bitcast(U16))
         deal(w4_s[:], w4_s_raw[:])
-        round_w1(1, nc.vector.tensor_copy)
-        load_words(nc.scalar, tab2_w[1], tab2_words[1])
-        quantize_w1(1)
-        for g in range(1, GROUPS):
-            gather_v2_scales(g)
-        place_v2_scales()
+        nc.vector.tensor_copy(v2_s_picked[:], tab2_s[:].indirect(idx2[:]))
+        round_w1(1, 0, gpsimd_cast, slice(0, P), slice(0, PACK))
         nc.gpsimd.tensor_tensor(mu_wh[:], mu_sb[:], wh_sb[:], ALU.mult)
         nc.gpsimd.tensor_scalar(shift[:], mu_wh[:], -1.0, 0.0, ALU.mult, ALU.add)
+        quantize_w1(1, 1)
+        deal(v2_s_dealt[:], v2_s_picked[:])
+        place_v2_scales()
 
-        for a in range(PASSES):
-            cosines(0, a)
-            features(0, a)
-            quantize_h(0, a)
-            gather_v2_words(0, a)
+        cosines(0, 0)
+        features(0, 0)
+        quantize_h(0, 0)
         cosines(1, 0)
         features(1, 0)
-        for g in range(1, GROUPS):
-            for a in reversed(range(PASSES)):
-                gather_v2_words(g, a)
         quantize_h(1, 0)
+        gather_v2_words(0, 0)
+        cosines(0, 1)
+        features(0, 1)
+        gather_v2_words(0, 1)
+        quantize_h(0, 1)
         cosines(1, 1)
         block(0, 0)
         features(1, 1)
         quantize_h(1, 1)
         for g in range(1, GROUPS):
-            block(0, g)
-        for g in range(GROUPS):
-            planes(0, g, 0, HALF, nc.vector.tensor_copy)
-            block(1, g)
-            store_words(0, g)
-        for g in range(GROUPS - 1):
-            planes(1, g, 0, HALF, nc.vector.tensor_copy)
-            store_words(1, g)
-        planes(1, GROUPS - 1, 0, HALF // 2, nc.scalar.copy)
-        planes(1, GROUPS - 1, HALF // 2, HALF // 2, nc.vector.tensor_copy)
-        store_words(1, GROUPS - 1)
+            for a in reversed(range(PASSES)):
+                gather_v2_words(g, a)
+        for u in range(2):
+            round_y(0, 0, u, gpsimd_cast, pairs=False)
+        for u in range(2):
+            quantize_y(0, 0, u)
+        on_vector = [nc.vector.tensor_copy, nc.vector.tensor_copy]
+        order = [(c, g) for g in range(GROUPS) for c in range(2)]
+        block(*order[1])
+        for n in range(2, len(order)):
+            block(*order[n])
+            planes(*order[n - 1], on_vector)
+            store_words(*order[n - 2])
+        planes(*order[-1], [nc.vector.tensor_copy, nc.scalar.copy])
+        for done in order[-2:]:
+            store_words(*done)
         store_scales()

@@ -343,18 +343,14 @@ def tile_list_fourier_landmark_block_kernel(
         for g in range(1, GROUPS):
             for a in reversed(range(PASSES)):
                 gather_v2_words(g, a)
-        for u in range(2):
-            round_y(0, 0, u, gpsimd_cast, pairs=False)
-        for u in range(2):
-            quantize_y(0, 0, u)
         on_vector = [nc.vector.tensor_copy, nc.vector.tensor_copy]
         order = [(c, g) for g in range(GROUPS) for c in range(2)]
         block(*order[1])
+        planes(*order[0], on_vector)
         for n in range(2, len(order)):
             block(*order[n])
             planes(*order[n - 1], on_vector)
-            store_words(*order[n - 2])
         planes(*order[-1], [nc.vector.tensor_copy, nc.scalar.copy])
-        for done in order[-2:]:
+        for done in order:
             store_words(*done)
         store_scales()

@@ -34,6 +34,7 @@ KB = 1024
 AT_W1_RAW0 = 0
 AT_W1_RAW1 = 4 * KB
 AT_COS11 = 12 * KB
+AT_COS01 = 56 * KB
 AT_TAB2 = 20 * KB
 AT_W1_BF = 52 * KB
 
@@ -123,10 +124,11 @@ def tile_list_fourier_landmark_block_kernel(
         w1_bf = [kept([P, PACK, P, PACK], BF16, "w1_bf0"), shared([P, PACK, P, PACK], BF16, "w1_bf1", AT_W1_BF)]
         w1_w = [kept([P, PASS], U32, f"w1_w{a}") for a in range(PASSES)]
         w1_s = [kept([P, PASS], U8, f"w1_s{a}") for a in range(PASSES)]
+        cos_at = {(0, 1): AT_COS01, (1, 1): AT_COS11}
         v2_w = {(0, a): kept([P, PACK, P], U32, f"v2_w0{a}") for a in range(PASSES)}
         for g in range(1, GROUPS):
             for a in range(PASSES):
-                v2_w[(g, a)] = shared([P, PACK, P], U32, f"v2_w{g}{a}", AT_COS11 + (2 * g + a - 2) * 2 * KB)
+                v2_w[(g, a)] = shared([P, PACK, P], U32, f"v2_w{g}{a}", cos_at[(g - 1, 1)] + a * 2 * KB)
         v2_s_picked = kept([P, S2], U8, "v2_s_picked")
         v2_s_dealt = shared([P, S2], U8, "v2_s_dealt", AT_W1_RAW1)
         v2_s = kept([P, S2], U8, "v2_s")
@@ -138,6 +140,7 @@ def tile_list_fourier_landmark_block_kernel(
         y_s = kept([P, GROUPS, S], U8, "y_s")
         y_w = [kept([P, GROUPS, HALF], U32, f"y_w{c}") for c in range(2)]
         y_at = {key: AT_TAB2 + slot * 8 * KB for slot, key in enumerate([(1, 1), (0, 2), (1, 2)])}
+        h_bf_at = {(0, 1, u): AT_W1_RAW1 + (2 * u - 1) * KB for u in range(2)}
         cos_of, h_bf_of, y_of, y_bf_of = {}, {}, {}, {}
 
         def placed(shape, dtype, name, offsets, key):
@@ -189,10 +192,7 @@ def tile_list_fourier_landmark_block_kernel(
 
         def cosines(c, a):
             dist = work.tile([P, PACK, HALF], F32, name="dist", tag="dist")
-            if (c, a) == (1, 1):
-                cos = shared([P, PACK, HALF], F32, "cos11", AT_COS11)
-            else:
-                cos = work.tile([P, PACK, HALF], F32, name="cos", tag="cos")
+            cos = placed([P, PACK, HALF], F32, f"cos{c}{a}", cos_at, (c, a))
             cos_of[(c, a)] = cos
             for t in range(PACK):
                 nc.tensor.matmul_mx(
@@ -215,7 +215,7 @@ def tile_list_fourier_landmark_block_kernel(
                 )
 
         def features(c, a):
-            h_bf = [kept([P, QUARTER, PACK], BF16, f"h_bf{c}{a}{u}") for u in range(2)]
+            h_bf = [placed([P, QUARTER, PACK], BF16, f"h_bf{c}{a}{u}", h_bf_at, (c, a, u)) for u in range(2)]
             h_bf_of[(c, a)] = h_bf
             for e in range(2):
                 for u in range(2):
@@ -250,18 +250,19 @@ def tile_list_fourier_landmark_block_kernel(
         def block(c, g, bank_set=scalar_banks):
             y = placed([P, PACK, HALF], F32, f"y{c}{g}", y_at, (c, g))
             y_of[(c, g)] = y
+            passes = [0, 1] if (c, g) == (0, 0) else [1, 0]
             rows = out_0[g * PASS : (g + 1) * PASS, c * HALF : (c + 1) * HALF].rearrange("(p t) j -> p t j", t=PACK)
             for t in range(PACK):
                 col = g * PASS + t * P
-                for a in reversed(range(PASSES)):
+                for a in passes:
                     nc.tensor.matmul_mx(
                         out=bank_set[t][:],
                         lhsT=v2_w[(g, a)][:, t, :].bitcast(E4M3),
                         lhsT_scale=v2_s[SCALE_ROWS * a : P, col : col + P],
                         rhs=h_w[(c, a)].bitcast(E4M3),
                         rhs_scale=h_s[(c, a)],
-                        start=(a == PASSES - 1),
-                        stop=(a == 0),
+                        start=(a == passes[0]),
+                        stop=(a == passes[-1]),
                     )
                 nc.scalar.activation(
                     y[:, t, :],
@@ -331,20 +332,21 @@ def tile_list_fourier_landmark_block_kernel(
         cosines(1, 0)
         features(1, 0)
         quantize_h(1, 0)
-        gather_v2_words(0, 0)
+        for a in range(PASSES):
+            gather_v2_words(0, a)
         cosines(0, 1)
         features(0, 1)
-        gather_v2_words(0, 1)
         quantize_h(0, 1)
+        for a in reversed(range(PASSES)):
+            gather_v2_words(1, a)
         cosines(1, 1)
         block(0, 0)
         features(1, 1)
         quantize_h(1, 1)
-        for g in range(1, GROUPS):
-            for a in reversed(range(PASSES)):
-                gather_v2_words(g, a)
+        for a in reversed(range(PASSES)):
+            gather_v2_words(2, a)
         on_vector = [nc.vector.tensor_copy, nc.vector.tensor_copy]
-        order = [(c, g) for g in range(GROUPS) for c in range(2)]
+        order = [(0, 0), (0, 1), (1, 0), (1, 1), (0, 2), (1, 2)]
         block(*order[1])
         planes(*order[0], on_vector)
         for n in range(2, len(order)):

@@ -124,22 +124,25 @@ def tile_list_fourier_landmark_block_kernel(
         w1_bf = [kept([P, PACK, P, PACK], BF16, "w1_bf0"), shared([P, PACK, P, PACK], BF16, "w1_bf1", AT_W1_BF)]
         w1_w = [kept([P, PASS], U32, f"w1_w{a}") for a in range(PASSES)]
         w1_s = [kept([P, PASS], U8, f"w1_s{a}") for a in range(PASSES)]
-        cos_at = {(0, 1): AT_COS01, (1, 1): AT_COS11}
+        cos_at = {(0, 1): AT_COS01}
         v2_w = {(0, a): kept([P, PACK, P], U32, f"v2_w0{a}") for a in range(PASSES)}
         for g in range(1, GROUPS):
             for a in range(PASSES):
-                v2_w[(g, a)] = shared([P, PACK, P], U32, f"v2_w{g}{a}", cos_at[(g - 1, 1)] + a * 2 * KB)
+                v2_w[(g, a)] = shared([P, PACK, P], U32, f"v2_w{g}{a}", AT_COS01 + (2 * g + a - 2) * 2 * KB)
         v2_s_picked = kept([P, S2], U8, "v2_s_picked")
         v2_s_dealt = shared([P, S2], U8, "v2_s_dealt", AT_W1_RAW1)
         v2_s = kept([P, S2], U8, "v2_s")
         nc.gpsimd.memset(v2_s[:].bitcast(I32), 0)
         h_w = {(c, a): kept([P, HALF], U32, f"h_w{c}{a}")[:] for c in range(2) for a in range(PASSES)}
+        h_w[(1, 0)] = shared([P, HALF], U32, "h_w10_late", AT_COS11)[:]
         h_s = {(c, a): kept([P, HALF], U8, f"h_s{c}{a}")[:] for c in range(2) for a in range(PASSES)}
         mu_wh = shared([P, GROUPS, PACK], F32, "mu_wh", AT_W1_RAW1 + 2 * KB)
         shift = kept([P, GROUPS, PACK], F32, "shift")
+        square = shared([P, QUARTER, PACK], F32, "square", AT_W1_RAW1 + KB)
+        half_phase = kept([P, PACK], F32, "half_phase")
         y_s = kept([P, GROUPS, S], U8, "y_s")
         y_w = [kept([P, GROUPS, HALF], U32, f"y_w{c}") for c in range(2)]
-        y_at = {key: AT_TAB2 + slot * 8 * KB for slot, key in enumerate([(1, 1), (0, 2), (1, 2)])}
+        y_at = {key: AT_TAB2 + slot * 8 * KB for slot, key in enumerate([(1, 0), (1, 1), (1, 2)])}
         h_bf_at = {(0, 1, u): AT_W1_RAW1 + (2 * u - 1) * KB for u in range(2)}
         cos_of, h_bf_of, y_of, y_bf_of = {}, {}, {}, {}
 
@@ -214,30 +217,69 @@ def tile_list_fourier_landmark_block_kernel(
                     scale=-1.0,
                 )
 
+        def mixed_cosines(c, a):
+            first = work.tile([P, PACK, HALF], F32, name="dist", tag="dist")
+            cos = shared([P, PACK, HALF], F32, f"cos{c}{a}", AT_COS11)
+            cos_of[(c, a)] = cos
+            for t in range(PACK):
+                bank = scalar_banks[t]
+                nc.tensor.matmul_mx(
+                    out=bank[:],
+                    lhsT=w1_w[a][:, t * P : (t + 1) * P].bitcast(E4M3),
+                    lhsT_scale=w1_s[a][:, t * P : (t + 1) * P],
+                    rhs=v_w[:, c * HALF : (c + 1) * HALF].bitcast(E4M3),
+                    rhs_scale=v_s[:, c * HALF : (c + 1) * HALF],
+                    start=True,
+                    stop=True,
+                )
+                nc.scalar.activation(
+                    first[:, t, :QUARTER], bank[:, :QUARTER], ACT.Sin, bias=half_phase[:, t : t + 1], scale=0.5
+                )
+                nc.scalar.activation(first[:, t, QUARTER:], bank[:, QUARTER:], ACT.Abs, bias=b_sb[:, a, t : t + 1])
+            nc.scalar.activation(
+                cos[:, :, QUARTER:], first[:, :, QUARTER:], ACT.Sin, bias=math.pi / 2, scale=-1.0
+            )
+            for j in (0, P):
+                part = first[:, :, j : j + P].rearrange("p t n -> p n t")
+                nc.gpsimd.tensor_tensor(square[:, j : j + P, :], part, part, ALU.mult)
+
         def features(c, a):
             h_bf = [placed([P, QUARTER, PACK], BF16, f"h_bf{c}{a}{u}", h_bf_at, (c, a, u)) for u in range(2)]
             h_bf_of[(c, a)] = h_bf
             for e in range(2):
                 for u in range(2):
                     j = u * QUARTER + e * P
+                    repeats = 2 if (c, a, u) == (1, 1, 0) else 1
                     q_bank = vector_banks[2 * e + u][:].rearrange("p (t n) -> p t n", n=P)
                     for t in range(PACK):
                         col = a * PASS + t * P
-                        nc.tensor.matmul_mx(
-                            out=q_bank[:, t, :],
-                            lhsT=w4_w[:, 2 * col : 2 * (col + P)].bitcast(E2M1),
-                            lhsT_scale=w4_s[:, col : col + P],
-                            rhs=v_w[:, c * HALF + j : c * HALF + j + P].bitcast(E4M3),
-                            rhs_scale=v_s[:, c * HALF + j : c * HALF + j + P],
-                            start=True,
-                            stop=True,
+                        for repeat in range(repeats):
+                            nc.tensor.matmul_mx(
+                                out=q_bank[:, t, :],
+                                lhsT=w4_w[:, 2 * col : 2 * (col + P)].bitcast(E2M1),
+                                lhsT_scale=w4_s[:, col : col + P],
+                                rhs=v_w[:, c * HALF + j : c * HALF + j + P].bitcast(E4M3),
+                                rhs_scale=v_s[:, c * HALF + j : c * HALF + j + P],
+                                start=(repeat == 0),
+                                stop=(repeat == repeats - 1),
+                            )
+                    out = h_bf[u][:, e * P : (e + 1) * P, :]
+                    if repeats == 1:
+                        nc.vector.tensor_tensor(
+                            out.rearrange("p (n i) t -> p n t i", i=2),
+                            q_bank.rearrange("p t (n i) -> p n t i", i=2),
+                            cos_of[(c, a)][:, :, j : j + P].rearrange("p t (n i) -> p n t i", i=2),
+                            ALU.mult,
                         )
-                    nc.vector.tensor_tensor(
-                        h_bf[u][:, e * P : (e + 1) * P, :].rearrange("p (n i) t -> p n t i", i=2),
-                        q_bank.rearrange("p t (n i) -> p n t i", i=2),
-                        cos_of[(c, a)][:, :, j : j + P].rearrange("p t (n i) -> p n t i", i=2),
-                        ALU.mult,
-                    )
+                    else:
+                        nc.vector.scalar_tensor_tensor(
+                            out,
+                            square[:, j : j + P, :],
+                            0.5,
+                            q_bank.rearrange("p t n -> p n t"),
+                            ALU.subtract,
+                            ALU.mult,
+                        )
 
         def quantize_h(c, a):
             for u, h_bf in enumerate(h_bf_of[(c, a)]):
@@ -250,7 +292,7 @@ def tile_list_fourier_landmark_block_kernel(
         def block(c, g, bank_set=scalar_banks):
             y = placed([P, PACK, HALF], F32, f"y{c}{g}", y_at, (c, g))
             y_of[(c, g)] = y
-            passes = [0, 1] if (c, g) == (0, 0) else [1, 0]
+            passes = [0, 1] if c == 1 else [1, 0]
             rows = out_0[g * PASS : (g + 1) * PASS, c * HALF : (c + 1) * HALF].rearrange("(p t) j -> p t j", t=PACK)
             for t in range(PACK):
                 col = g * PASS + t * P
@@ -275,7 +317,10 @@ def tile_list_fourier_landmark_block_kernel(
                     nc.sync.dma_start(rows[:, t - 1 : t + 1, :], y[:, t - 1 : t + 1, :])
 
         def round_y(c, g, u, cast, pairs=True):
-            y_bf = rounded.tile([P, QUARTER, PACK], BF16, name="y_bf", tag=f"y_bf{u}", align_bytes=64)
+            if c == 0 and 1 <= 2 * g + u <= 2:
+                y_bf = shared([P, QUARTER, PACK], BF16, f"y_bf0{g}{u}", AT_W1_RAW1 + (4 * g + 2 * u - 1) * KB)
+            else:
+                y_bf = rounded.tile([P, QUARTER, PACK], BF16, name="y_bf", tag=f"y_bf{u}", align_bytes=64)
             y_bf_of[(c, g, u)] = y_bf
             y = y_of[(c, g)][:, :, u * QUARTER : (u + 1) * QUARTER]
             if pairs:
@@ -321,6 +366,7 @@ def tile_list_fourier_landmark_block_kernel(
         nc.vector.tensor_copy(v2_s_picked[:], tab2_s[:].indirect(idx2[:]))
         round_w1(1, 0, gpsimd_cast, slice(0, P), slice(0, PACK))
         nc.gpsimd.tensor_tensor(mu_wh[:], mu_sb[:], wh_sb[:], ALU.mult)
+        nc.gpsimd.tensor_scalar(half_phase[:], b_sb[:, 1, :], 0.5, math.pi / 2, ALU.mult, ALU.add)
         nc.gpsimd.tensor_scalar(shift[:], mu_wh[:], -1.0, 0.0, ALU.mult, ALU.add)
         quantize_w1(1, 1)
         deal(v2_s_dealt[:], v2_s_picked[:])
@@ -331,28 +377,31 @@ def tile_list_fourier_landmark_block_kernel(
         quantize_h(0, 0)
         cosines(1, 0)
         features(1, 0)
-        quantize_h(1, 0)
         for a in range(PASSES):
             gather_v2_words(0, a)
         cosines(0, 1)
         features(0, 1)
         quantize_h(0, 1)
-        for a in reversed(range(PASSES)):
-            gather_v2_words(1, a)
-        cosines(1, 1)
+        for g in range(1, GROUPS):
+            for a in reversed(range(PASSES)):
+                gather_v2_words(g, a)
+        mixed_cosines(1, 1)
         block(0, 0)
         features(1, 1)
+        quantize_h(1, 0)
         quantize_h(1, 1)
-        for a in reversed(range(PASSES)):
-            gather_v2_words(2, a)
         on_vector = [nc.vector.tensor_copy, nc.vector.tensor_copy]
-        order = [(0, 0), (0, 1), (1, 0), (1, 1), (0, 2), (1, 2)]
+        order = [(c, g) for c in range(2) for g in range(GROUPS)]
         block(*order[1])
-        planes(*order[0], on_vector)
+        round_y(0, 0, 0, gpsimd_cast, pairs=False)
+        round_y(0, 0, 1, nc.vector.tensor_copy)
+        for u in range(2):
+            quantize_y(0, 0, u)
         for n in range(2, len(order)):
             block(*order[n])
             planes(*order[n - 1], on_vector)
+            store_words(*order[n - 2])
         planes(*order[-1], [nc.vector.tensor_copy, nc.scalar.copy])
-        for done in order:
+        for done in order[-2:]:
             store_words(*done)
         store_scales()

@@ -33,10 +33,17 @@ LIST_ROWS = 16
 KB = 1024
 AT_W1_RAW0 = 0
 AT_W1_RAW1 = 4 * KB
+AT_MU_WH = 6 * KB
+AT_H01 = 3 * KB
+AT_SQUARE = 5 * KB
 AT_COS11 = 12 * KB
-AT_COS01 = 56 * KB
 AT_TAB2 = 20 * KB
 AT_W1_BF = 52 * KB
+AT_COS01 = 56 * KB
+QUARTER_BF_BYTES = QUARTER * PACK * 2
+WORDS_BYTES = PASS * 4
+PANEL_BYTES = PACK * HALF * 4
+WALK = 4
 
 
 def tile_list_fourier_landmark_block_kernel(
@@ -75,7 +82,7 @@ def tile_list_fourier_landmark_block_kernel(
 
         tab_w = kept([P, T], I32, "tab_w")
         w4_w_raw = kept([P, 2 * H], U8, "w4_w_raw")
-        tab2_w = [shared([P, T2], I32, f"tab2_w{a}", AT_TAB2 + a * 16 * KB) for a in range(PASSES)]
+        tab2_w = [shared([P, T2], I32, f"tab2_w{a}", AT_TAB2 + a * T2 * 4) for a in range(PASSES)]
         w1_raw = [
             [kept([P, PACK, PASS // 2], F32, "w1_raw00"), shared([P, PACK, PASS // 2], F32, "w1_raw01", AT_W1_RAW0)],
             [shared([P, PACK, PASS], F32, "w1_raw1", AT_W1_RAW1)],
@@ -124,26 +131,26 @@ def tile_list_fourier_landmark_block_kernel(
         w1_bf = [kept([P, PACK, P, PACK], BF16, "w1_bf0"), shared([P, PACK, P, PACK], BF16, "w1_bf1", AT_W1_BF)]
         w1_w = [kept([P, PASS], U32, f"w1_w{a}") for a in range(PASSES)]
         w1_s = [kept([P, PASS], U8, f"w1_s{a}") for a in range(PASSES)]
-        cos_at = {(0, 1): AT_COS01}
+        cos_at = {(0, 1): AT_COS01, (1, 1): AT_COS11}
         v2_w = {(0, a): kept([P, PACK, P], U32, f"v2_w0{a}") for a in range(PASSES)}
         for g in range(1, GROUPS):
             for a in range(PASSES):
-                v2_w[(g, a)] = shared([P, PACK, P], U32, f"v2_w{g}{a}", AT_COS01 + (2 * g + a - 2) * 2 * KB)
+                v2_w[(g, a)] = shared([P, PACK, P], U32, f"v2_w{g}{a}", AT_COS01 + (PASSES * (g - 1) + a) * WORDS_BYTES)
         v2_s_picked = kept([P, S2], U8, "v2_s_picked")
         v2_s_dealt = shared([P, S2], U8, "v2_s_dealt", AT_W1_RAW1)
         v2_s = kept([P, S2], U8, "v2_s")
         nc.gpsimd.memset(v2_s[:].bitcast(I32), 0)
-        h_w = {(c, a): kept([P, HALF], U32, f"h_w{c}{a}")[:] for c in range(2) for a in range(PASSES)}
-        h_w[(1, 0)] = shared([P, HALF], U32, "h_w10_late", AT_COS11)[:]
-        h_s = {(c, a): kept([P, HALF], U8, f"h_s{c}{a}")[:] for c in range(2) for a in range(PASSES)}
-        mu_wh = shared([P, GROUPS, PACK], F32, "mu_wh", AT_W1_RAW1 + 2 * KB)
+        h_w = {(c, a): kept([P, HALF], U32, f"h_w{c}{a}") for c, a in [(0, 0), (0, 1), (1, 1)]}
+        h_w[(1, 0)] = shared([P, HALF], U32, "h_w10", AT_COS11)
+        h_s = {(c, a): kept([P, HALF], U8, f"h_s{c}{a}") for c in range(2) for a in range(PASSES)}
+        mu_wh = shared([P, GROUPS, PACK], F32, "mu_wh", AT_MU_WH)
         shift = kept([P, GROUPS, PACK], F32, "shift")
-        square = shared([P, QUARTER, PACK], F32, "square", AT_W1_RAW1 + KB)
+        square = shared([P, QUARTER, PACK], F32, "square", AT_SQUARE)
         half_phase = kept([P, PACK], F32, "half_phase")
         y_s = kept([P, GROUPS, S], U8, "y_s")
         y_w = [kept([P, GROUPS, HALF], U32, f"y_w{c}") for c in range(2)]
-        y_at = {key: AT_TAB2 + slot * 8 * KB for slot, key in enumerate([(1, 0), (1, 1), (1, 2)])}
-        h_bf_at = {(0, 1, u): AT_W1_RAW1 + (2 * u - 1) * KB for u in range(2)}
+        y_at = {(1, g): AT_TAB2 + g * PANEL_BYTES for g in range(GROUPS)}
+        h_bf_at = {(0, 1, u): AT_H01 + u * QUARTER_BF_BYTES for u in range(2)}
         cos_of, h_bf_of, y_of, y_bf_of = {}, {}, {}, {}
 
         def placed(shape, dtype, name, offsets, key):
@@ -163,11 +170,11 @@ def tile_list_fourier_landmark_block_kernel(
         def gpsimd_cast(out, in_):
             nc.gpsimd.tensor_scalar(out, in_, 1.0, 0.0, ALU.mult, ALU.add)
 
-        def round_w1(a, u, cast, ms, ts):
-            m0 = u * P // len(w1_raw[a])
+        def round_w1(a, u, cast, ts=slice(0, PACK)):
+            count = P // len(w1_raw[a])
             cast(
-                w1_bf[a][:, ts, m0 + ms.start : m0 + ms.stop, :].rearrange("p t m j -> p m t j"),
-                w1_raw[a][u][:].rearrange("p j (m t) -> p m t j", t=PACK)[:, ms, ts, :],
+                w1_bf[a][:, ts, u * count : (u + 1) * count, :].rearrange("p t m j -> p m t j"),
+                w1_raw[a][u][:].rearrange("p j (m t) -> p m t j", t=PACK)[:, :, ts, :],
             )
 
         def quantize_w1(a, pieces):
@@ -185,63 +192,59 @@ def tile_list_fourier_landmark_block_kernel(
             )
 
         def place_v2_scales():
-            for a in range(PASSES):
-                for quad in range(QUADRANTS):
-                    src = BLOCKS * a + SCALE_ROWS * quad
-                    dst = QUADRANT * quad + SCALE_ROWS * a
-                    nc.sync.dma_start(
-                        v2_s[dst : dst + SCALE_ROWS, :].bitcast(I32), v2_s_dealt[src : src + SCALE_ROWS, :].bitcast(I32)
-                    )
+            moves = [(a, quad) for a in range(PASSES) for quad in range(QUADRANTS)]
+            for a, quad in moves:
+                src = BLOCKS * a + SCALE_ROWS * quad
+                dst = QUADRANT * quad + SCALE_ROWS * a
+                queue = nc.gpsimd if (a, quad) == moves[-1] else nc.sync
+                queue.dma_start(
+                    v2_s[dst : dst + SCALE_ROWS, :].bitcast(I32), v2_s_dealt[src : src + SCALE_ROWS, :].bitcast(I32)
+                )
+
+        def project(c, a, t):
+            nc.tensor.matmul_mx(
+                out=scalar_banks[t][:],
+                lhsT=w1_w[a][:, t * P : (t + 1) * P].bitcast(E4M3),
+                lhsT_scale=w1_s[a][:, t * P : (t + 1) * P],
+                rhs=v_w[:, c * HALF : (c + 1) * HALF].bitcast(E4M3),
+                rhs_scale=v_s[:, c * HALF : (c + 1) * HALF],
+                start=True,
+                stop=True,
+            )
+
+        def cos_of_distance(out, in_):
+            nc.scalar.activation(out, in_, ACT.Sin, bias=math.pi / 2, scale=-1.0)
 
         def cosines(c, a):
             dist = work.tile([P, PACK, HALF], F32, name="dist", tag="dist")
             cos = placed([P, PACK, HALF], F32, f"cos{c}{a}", cos_at, (c, a))
             cos_of[(c, a)] = cos
             for t in range(PACK):
-                nc.tensor.matmul_mx(
-                    out=scalar_banks[t][:],
-                    lhsT=w1_w[a][:, t * P : (t + 1) * P].bitcast(E4M3),
-                    lhsT_scale=w1_s[a][:, t * P : (t + 1) * P],
-                    rhs=v_w[:, c * HALF : (c + 1) * HALF].bitcast(E4M3),
-                    rhs_scale=v_s[:, c * HALF : (c + 1) * HALF],
-                    start=True,
-                    stop=True,
-                )
+                project(c, a, t)
                 nc.scalar.activation(dist[:, t, :], scalar_banks[t][:], ACT.Abs, bias=b_sb[:, a, t : t + 1])
             for e in range(2):
-                nc.scalar.activation(
+                cos_of_distance(
                     cos[:].rearrange("p t (u e n) -> p (t u) e n", e=2, n=P)[:, :, e, :],
                     dist[:].rearrange("p t (u e n) -> p (t u) e n", e=2, n=P)[:, :, e, :],
-                    ACT.Sin,
-                    bias=math.pi / 2,
-                    scale=-1.0,
                 )
 
         def mixed_cosines(c, a):
-            first = work.tile([P, PACK, HALF], F32, name="dist", tag="dist")
-            cos = shared([P, PACK, HALF], F32, f"cos{c}{a}", AT_COS11)
+            first_pass = work.tile([P, PACK, HALF], F32, name="dist", tag="dist")
+            cos = placed([P, PACK, HALF], F32, f"cos{c}{a}", cos_at, (c, a))
             cos_of[(c, a)] = cos
             for t in range(PACK):
+                project(c, a, t)
                 bank = scalar_banks[t]
-                nc.tensor.matmul_mx(
-                    out=bank[:],
-                    lhsT=w1_w[a][:, t * P : (t + 1) * P].bitcast(E4M3),
-                    lhsT_scale=w1_s[a][:, t * P : (t + 1) * P],
-                    rhs=v_w[:, c * HALF : (c + 1) * HALF].bitcast(E4M3),
-                    rhs_scale=v_s[:, c * HALF : (c + 1) * HALF],
-                    start=True,
-                    stop=True,
+                nc.scalar.activation(
+                    first_pass[:, t, :QUARTER], bank[:, :QUARTER], ACT.Sin, bias=half_phase[:, t : t + 1], scale=0.5
                 )
                 nc.scalar.activation(
-                    first[:, t, :QUARTER], bank[:, :QUARTER], ACT.Sin, bias=half_phase[:, t : t + 1], scale=0.5
+                    first_pass[:, t, QUARTER:], bank[:, QUARTER:], ACT.Abs, bias=b_sb[:, a, t : t + 1]
                 )
-                nc.scalar.activation(first[:, t, QUARTER:], bank[:, QUARTER:], ACT.Abs, bias=b_sb[:, a, t : t + 1])
-            nc.scalar.activation(
-                cos[:, :, QUARTER:], first[:, :, QUARTER:], ACT.Sin, bias=math.pi / 2, scale=-1.0
-            )
-            for j in (0, P):
-                part = first[:, :, j : j + P].rearrange("p t n -> p n t")
-                nc.gpsimd.tensor_tensor(square[:, j : j + P, :], part, part, ALU.mult)
+            cos_of_distance(cos[:, :, QUARTER:], first_pass[:, :, QUARTER:])
+            for j in range(0, QUARTER, P):
+                half_cos = first_pass[:, :, j : j + P].rearrange("p t n -> p n t")
+                nc.gpsimd.tensor_tensor(square[:, j : j + P, :], half_cos, half_cos, ALU.mult)
 
         def features(c, a):
             h_bf = [placed([P, QUARTER, PACK], BF16, f"h_bf{c}{a}{u}", h_bf_at, (c, a, u)) for u in range(2)]
@@ -249,7 +252,8 @@ def tile_list_fourier_landmark_block_kernel(
             for e in range(2):
                 for u in range(2):
                     j = u * QUARTER + e * P
-                    repeats = 2 if (c, a, u) == (1, 1, 0) else 1
+                    by_half_angle = (c, a, u) == (1, 1, 0)
+                    repeats = 2 if by_half_angle else 1
                     q_bank = vector_banks[2 * e + u][:].rearrange("p (t n) -> p t n", n=P)
                     for t in range(PACK):
                         col = a * PASS + t * P
@@ -264,20 +268,20 @@ def tile_list_fourier_landmark_block_kernel(
                                 stop=(repeat == repeats - 1),
                             )
                     out = h_bf[u][:, e * P : (e + 1) * P, :]
-                    if repeats == 1:
-                        nc.vector.tensor_tensor(
-                            out.rearrange("p (n i) t -> p n t i", i=2),
-                            q_bank.rearrange("p t (n i) -> p n t i", i=2),
-                            cos_of[(c, a)][:, :, j : j + P].rearrange("p t (n i) -> p n t i", i=2),
-                            ALU.mult,
-                        )
-                    else:
+                    if by_half_angle:
                         nc.vector.scalar_tensor_tensor(
                             out,
                             square[:, j : j + P, :],
                             0.5,
                             q_bank.rearrange("p t n -> p n t"),
                             ALU.subtract,
+                            ALU.mult,
+                        )
+                    else:
+                        nc.vector.tensor_tensor(
+                            out.rearrange("p (n i) t -> p n t i", i=WALK),
+                            q_bank.rearrange("p t (n i) -> p n t i", i=WALK),
+                            cos_of[(c, a)][:, :, j : j + P].rearrange("p t (n i) -> p n t i", i=WALK),
                             ALU.mult,
                         )
 
@@ -289,7 +293,7 @@ def tile_list_fourier_landmark_block_kernel(
                     in_=h_bf[:].rearrange("p n t -> p (n t)"),
                 )
 
-        def block(c, g, bank_set=scalar_banks):
+        def panel(c, g):
             y = placed([P, PACK, HALF], F32, f"y{c}{g}", y_at, (c, g))
             y_of[(c, g)] = y
             passes = [0, 1] if c == 1 else [1, 0]
@@ -298,17 +302,17 @@ def tile_list_fourier_landmark_block_kernel(
                 col = g * PASS + t * P
                 for a in passes:
                     nc.tensor.matmul_mx(
-                        out=bank_set[t][:],
+                        out=scalar_banks[t][:],
                         lhsT=v2_w[(g, a)][:, t, :].bitcast(E4M3),
                         lhsT_scale=v2_s[SCALE_ROWS * a : P, col : col + P],
-                        rhs=h_w[(c, a)].bitcast(E4M3),
-                        rhs_scale=h_s[(c, a)],
+                        rhs=h_w[(c, a)][:].bitcast(E4M3),
+                        rhs_scale=h_s[(c, a)][:],
                         start=(a == passes[0]),
                         stop=(a == passes[-1]),
                     )
                 nc.scalar.activation(
                     y[:, t, :],
-                    bank_set[t][:],
+                    scalar_banks[t][:],
                     ACT.Identity,
                     bias=shift[:, g, t : t + 1],
                     scale=wh_sb[:, g, t : t + 1],
@@ -316,17 +320,17 @@ def tile_list_fourier_landmark_block_kernel(
                 if t % 2 == 1:
                     nc.sync.dma_start(rows[:, t - 1 : t + 1, :], y[:, t - 1 : t + 1, :])
 
-        def round_y(c, g, u, cast, pairs=True):
-            if c == 0 and 1 <= 2 * g + u <= 2:
-                y_bf = shared([P, QUARTER, PACK], BF16, f"y_bf0{g}{u}", AT_W1_RAW1 + (4 * g + 2 * u - 1) * KB)
+        def round_y(c, g, u, cast):
+            if (c, g) == (0, 1):
+                y_bf = shared([P, QUARTER, PACK], BF16, f"y_bf01{u}", AT_SQUARE + u * QUARTER_BF_BYTES)
             else:
                 y_bf = rounded.tile([P, QUARTER, PACK], BF16, name="y_bf", tag=f"y_bf{u}", align_bytes=64)
             y_bf_of[(c, g, u)] = y_bf
             y = y_of[(c, g)][:, :, u * QUARTER : (u + 1) * QUARTER]
-            if pairs:
-                cast(y_bf[:].rearrange("p (n i) t -> p n t i", i=2), y.rearrange("p t (n i) -> p n t i", i=2))
-            else:
+            if cast is gpsimd_cast:
                 cast(y_bf[:], y.rearrange("p t n -> p n t"))
+            else:
+                cast(y_bf[:].rearrange("p (n i) t -> p n t i", i=WALK), y.rearrange("p t (n i) -> p n t i", i=WALK))
 
         def quantize_y(c, g, u):
             j0 = u * QUARTER
@@ -357,14 +361,14 @@ def tile_list_fourier_landmark_block_kernel(
 
         nc.vector.tensor_copy(v_s[:], tab_s[:].indirect(idx[:]))
         nc.vector.tensor_copy(v_w[:], tab_w[:].bitcast(U32).indirect(idx[:]))
-        round_w1(0, 0, nc.scalar.copy, slice(0, P // 2), slice(0, PACK))
-        round_w1(0, 1, nc.vector.tensor_copy, slice(0, P // 2), slice(0, 2))
-        round_w1(0, 1, nc.scalar.copy, slice(0, P // 2), slice(2, PACK))
+        round_w1(0, 0, nc.scalar.copy)
+        round_w1(0, 1, nc.vector.tensor_copy, slice(0, PACK // 2))
+        round_w1(0, 1, nc.scalar.copy, slice(PACK // 2, PACK))
         quantize_w1(0, 2)
         deal(w4_w[:].bitcast(U16), w4_w_raw[:].bitcast(U16))
         deal(w4_s[:], w4_s_raw[:])
         nc.vector.tensor_copy(v2_s_picked[:], tab2_s[:].indirect(idx2[:]))
-        round_w1(1, 0, gpsimd_cast, slice(0, P), slice(0, PACK))
+        round_w1(1, 0, gpsimd_cast)
         nc.gpsimd.tensor_tensor(mu_wh[:], mu_sb[:], wh_sb[:], ALU.mult)
         nc.gpsimd.tensor_scalar(half_phase[:], b_sb[:, 1, :], 0.5, math.pi / 2, ALU.mult, ALU.add)
         nc.gpsimd.tensor_scalar(shift[:], mu_wh[:], -1.0, 0.0, ALU.mult, ALU.add)
@@ -386,20 +390,17 @@ def tile_list_fourier_landmark_block_kernel(
             for a in reversed(range(PASSES)):
                 gather_v2_words(g, a)
         mixed_cosines(1, 1)
-        block(0, 0)
+        panel(0, 0)
         features(1, 1)
-        quantize_h(1, 0)
-        quantize_h(1, 1)
-        on_vector = [nc.vector.tensor_copy, nc.vector.tensor_copy]
+        for a in range(PASSES):
+            quantize_h(1, a)
+
         order = [(c, g) for c in range(2) for g in range(GROUPS)]
-        block(*order[1])
-        round_y(0, 0, 0, gpsimd_cast, pairs=False)
-        round_y(0, 0, 1, nc.vector.tensor_copy)
-        for u in range(2):
-            quantize_y(0, 0, u)
+        panel(*order[1])
+        planes(*order[0], [gpsimd_cast, gpsimd_cast])
         for n in range(2, len(order)):
-            block(*order[n])
-            planes(*order[n - 1], on_vector)
+            panel(*order[n])
+            planes(*order[n - 1], [nc.vector.tensor_copy, nc.vector.tensor_copy])
             store_words(*order[n - 2])
         planes(*order[-1], [nc.vector.tensor_copy, nc.scalar.copy])
         for done in order[-2:]:

@@ -106,11 +106,11 @@ def tile_list_fourier_landmark_block_kernel(
         def load_words(tile, words):
             nc.sync.dma_start(tile[:], words.rearrange("p n i -> p (n i)").bitcast(I32))
 
+        load_w1(0, 0)
         nc.sync.dma_start(idx[:], offs)
         nc.sync.dma_start(idx2[:], offs2)
         load_scale_rows(tab_s, tab_scales)
         load_words(tab_w, tab_words[0])
-        load_w1(0, 0)
         load_w1(0, 1)
         nc.sync.dma_start(w4_w_raw[:].bitcast(I32), w4_words[0].bitcast(I32))
         load_scale_rows(w4_s_raw, w4_scales)
@@ -124,9 +124,9 @@ def tile_list_fourier_landmark_block_kernel(
         nc.gpsimd.dma_start(mu_sb[:], mu.rearrange("(g p t) -> p g t", p=P, t=PACK))
         nc.gpsimd.dma_start(wh_sb[:], wh.rearrange("(g p t) -> p g t", p=P, t=PACK))
 
-        w4_w = shared([P, 2 * H], U8, "w4_w", AT_W1_RAW0)
+        w4_w = kept([P, 2 * H], U8, "w4_w")
         w4_s = kept([P, H], U8, "w4_s")
-        v_w = kept([P, S], U32, "v_w")
+        v_w = [kept([P, HALF], U32, "v_w0"), shared([P, HALF], U32, "v_w1", AT_W1_RAW0)]
         v_s = kept([P, S], U8, "v_s")
         w1_bf = [kept([P, PACK, P, PACK], BF16, "w1_bf0"), shared([P, PACK, P, PACK], BF16, "w1_bf1", AT_W1_BF)]
         w1_w = [kept([P, PASS], U32, f"w1_w{a}") for a in range(PASSES)]
@@ -161,10 +161,10 @@ def tile_list_fourier_landmark_block_kernel(
         def entries(lst, part):
             return lst[:, part * PASS // LIST_ROWS : (part + 1) * PASS // LIST_ROWS]
 
-        def deal(out, in_):
-            nc.vector.tensor_copy(
-                out.rearrange("p (g t m) -> p g t m", t=PACK, m=P),
-                in_.rearrange("p (g m t) -> p g t m", t=PACK, m=P),
+        def deal(copy, out, in_):
+            copy(
+                out.rearrange("p (g t m) -> p t g m", t=PACK, m=P),
+                in_.rearrange("p (g m t) -> p t g m", t=PACK, m=P),
             )
 
         def gpsimd_cast(out, in_):
@@ -186,6 +186,10 @@ def tile_list_fourier_landmark_block_kernel(
                     in_=w1_bf[a][:].rearrange("p t m j -> p (t m j)")[:, PACK * c0 : PACK * (c0 + width)],
                 )
 
+        def gather_v_words(c):
+            cols = HALF // LIST_ROWS
+            nc.vector.tensor_copy(v_w[c][:], tab_w[:].bitcast(U32).indirect(idx[:, c * cols : (c + 1) * cols]))
+
         def gather_v2_words(g, a):
             nc.vector.tensor_copy(
                 v2_w[(g, a)][:].rearrange("p t m -> p m t"), tab2_w[a][:].bitcast(U32).indirect(entries(idx2, g))
@@ -206,7 +210,7 @@ def tile_list_fourier_landmark_block_kernel(
                 out=scalar_banks[t][:],
                 lhsT=w1_w[a][:, t * P : (t + 1) * P].bitcast(E4M3),
                 lhsT_scale=w1_s[a][:, t * P : (t + 1) * P],
-                rhs=v_w[:, c * HALF : (c + 1) * HALF].bitcast(E4M3),
+                rhs=v_w[c][:].bitcast(E4M3),
                 rhs_scale=v_s[:, c * HALF : (c + 1) * HALF],
                 start=True,
                 stop=True,
@@ -262,7 +266,7 @@ def tile_list_fourier_landmark_block_kernel(
                                 out=q_bank[:, t, :],
                                 lhsT=w4_w[:, 2 * col : 2 * (col + P)].bitcast(E2M1),
                                 lhsT_scale=w4_s[:, col : col + P],
-                                rhs=v_w[:, c * HALF + j : c * HALF + j + P].bitcast(E4M3),
+                                rhs=v_w[c][:, j : j + P].bitcast(E4M3),
                                 rhs_scale=v_s[:, c * HALF + j : c * HALF + j + P],
                                 start=(repeat == 0),
                                 stop=(repeat == repeats - 1),
@@ -360,20 +364,21 @@ def tile_list_fourier_landmark_block_kernel(
                 )
 
         nc.vector.tensor_copy(v_s[:], tab_s[:].indirect(idx[:]))
-        nc.vector.tensor_copy(v_w[:], tab_w[:].bitcast(U32).indirect(idx[:]))
+        gather_v_words(0)
         round_w1(0, 0, nc.scalar.copy)
         round_w1(0, 1, nc.vector.tensor_copy, slice(0, PACK // 2))
         round_w1(0, 1, nc.scalar.copy, slice(PACK // 2, PACK))
         quantize_w1(0, 2)
-        deal(w4_w[:].bitcast(U16), w4_w_raw[:].bitcast(U16))
-        deal(w4_s[:], w4_s_raw[:])
+        gather_v_words(1)
+        deal(nc.scalar.copy, w4_w[:].bitcast(U16), w4_w_raw[:].bitcast(U16))
+        deal(nc.vector.tensor_copy, w4_s[:], w4_s_raw[:])
         nc.vector.tensor_copy(v2_s_picked[:], tab2_s[:].indirect(idx2[:]))
         round_w1(1, 0, gpsimd_cast)
         nc.gpsimd.tensor_tensor(mu_wh[:], mu_sb[:], wh_sb[:], ALU.mult)
         nc.gpsimd.tensor_scalar(half_phase[:], b_sb[:, 1, :], 0.5, math.pi / 2, ALU.mult, ALU.add)
         nc.gpsimd.tensor_scalar(shift[:], mu_wh[:], -1.0, 0.0, ALU.mult, ALU.add)
         quantize_w1(1, 1)
-        deal(v2_s_dealt[:], v2_s_picked[:])
+        deal(nc.vector.tensor_copy, v2_s_dealt[:], v2_s_picked[:])
         place_v2_scales()
 
         cosines(0, 0)

@@ -39,6 +39,7 @@ AT_SQUARE = 5 * KB
 AT_COS11 = 12 * KB
 AT_TAB2 = 20 * KB
 AT_W1_BF = 52 * KB
+AT_PICKED = 64 * KB
 AT_COS01 = 56 * KB
 QUARTER_BF_BYTES = QUARTER * PACK * 2
 WORDS_BYTES = PASS * 4
@@ -54,7 +55,7 @@ def tile_list_fourier_landmark_block_kernel(
     with ExitStack() as ctx:
         lists = ctx.enter_context(tc.tile_pool(name="lists", bufs=1))
         keep = ctx.enter_context(tc.tile_pool(name="keep", bufs=1))
-        work = ctx.enter_context(tc.tile_pool(name="work", bufs=2))
+        work = ctx.enter_context(tc.tile_pool(name="work", bufs=3))
         rounded = ctx.enter_context(tc.tile_pool(name="rounded", bufs=3))
         reuse = ctx.enter_context(tc.tile_pool(name="reuse", bufs=1))
         psum = ctx.enter_context(tc.psum_pool(name="psum", bufs=1))
@@ -91,10 +92,10 @@ def tile_list_fourier_landmark_block_kernel(
         mu_sb = kept([P, GROUPS, PACK], F32, "mu_sb")
         wh_sb = kept([P, GROUPS, PACK], F32, "wh_sb")
 
-        def load_w1(a, u):
+        def load_w1(a, u, queue=nc.sync):
             width = PASS // len(w1_raw[a])
             c0 = a * PASS + u * width
-            nc.sync.dma_start(w1_raw[a][u][:], w1[:, c0 : c0 + width].rearrange("(p j) c -> p j c", j=PACK))
+            queue.dma_start(w1_raw[a][u][:], w1[:, c0 : c0 + width].rearrange("(p j) c -> p j c", j=PACK))
 
         def load_scale_rows(plane, scales):
             for quad in range(QUADRANTS):
@@ -106,7 +107,7 @@ def tile_list_fourier_landmark_block_kernel(
         def load_words(tile, words):
             nc.sync.dma_start(tile[:], words.rearrange("p n i -> p (n i)").bitcast(I32))
 
-        load_w1(0, 0)
+        load_w1(0, 0, nc.scalar)
         nc.sync.dma_start(idx[:], offs)
         nc.sync.dma_start(idx2[:], offs2)
         load_scale_rows(tab_s, tab_scales)
@@ -136,7 +137,7 @@ def tile_list_fourier_landmark_block_kernel(
         for g in range(1, GROUPS):
             for a in range(PASSES):
                 v2_w[(g, a)] = shared([P, PACK, P], U32, f"v2_w{g}{a}", AT_COS01 + (PASSES * (g - 1) + a) * WORDS_BYTES)
-        v2_s_picked = kept([P, S2], U8, "v2_s_picked")
+        v2_s_picked = shared([P, S2], U8, "v2_s_picked", AT_PICKED)
         v2_s_dealt = shared([P, S2], U8, "v2_s_dealt", AT_W1_RAW1)
         v2_s = kept([P, S2], U8, "v2_s")
         nc.gpsimd.memset(v2_s[:].bitcast(I32), 0)
@@ -145,12 +146,15 @@ def tile_list_fourier_landmark_block_kernel(
         h_s = {(c, a): kept([P, HALF], U8, f"h_s{c}{a}") for c in range(2) for a in range(PASSES)}
         mu_wh = shared([P, GROUPS, PACK], F32, "mu_wh", AT_MU_WH)
         shift = kept([P, GROUPS, PACK], F32, "shift")
-        square = shared([P, QUARTER, PACK], F32, "square", AT_SQUARE)
-        half_phase = kept([P, PACK], F32, "half_phase")
+        square = {
+            (1, 0): shared([P, QUARTER, PACK], F32, "square10", AT_PICKED),
+            (1, 1): shared([P, QUARTER, PACK], F32, "square11", AT_SQUARE),
+        }
+        half_phase = kept([P, PASSES, PACK], F32, "half_phase")
         y_s = kept([P, GROUPS, S], U8, "y_s")
         y_w = [kept([P, GROUPS, HALF], U32, f"y_w{c}") for c in range(2)]
         y_at = {(1, g): AT_TAB2 + g * PANEL_BYTES for g in range(GROUPS)}
-        h_bf_at = {(0, 1, u): AT_H01 + u * QUARTER_BF_BYTES for u in range(2)}
+        h_bf_at = {(1, 0, 0): AT_H01, (0, 1, 1): AT_H01 + QUARTER_BF_BYTES}
         cos_of, h_bf_of, y_of, y_bf_of = {}, {}, {}, {}
 
         def placed(shape, dtype, name, offsets, key):
@@ -200,8 +204,7 @@ def tile_list_fourier_landmark_block_kernel(
             for a, quad in moves:
                 src = BLOCKS * a + SCALE_ROWS * quad
                 dst = QUADRANT * quad + SCALE_ROWS * a
-                queue = nc.gpsimd if (a, quad) == moves[-1] else nc.sync
-                queue.dma_start(
+                nc.sync.dma_start(
                     v2_s[dst : dst + SCALE_ROWS, :].bitcast(I32), v2_s_dealt[src : src + SCALE_ROWS, :].bitcast(I32)
                 )
 
@@ -240,7 +243,7 @@ def tile_list_fourier_landmark_block_kernel(
                 project(c, a, t)
                 bank = scalar_banks[t]
                 nc.scalar.activation(
-                    first_pass[:, t, :QUARTER], bank[:, :QUARTER], ACT.Sin, bias=half_phase[:, t : t + 1], scale=0.5
+                    first_pass[:, t, :QUARTER], bank[:, :QUARTER], ACT.Sin, bias=half_phase[:, a, t : t + 1], scale=0.5
                 )
                 nc.scalar.activation(
                     first_pass[:, t, QUARTER:], bank[:, QUARTER:], ACT.Abs, bias=b_sb[:, a, t : t + 1]
@@ -248,15 +251,16 @@ def tile_list_fourier_landmark_block_kernel(
             cos_of_distance(cos[:, :, QUARTER:], first_pass[:, :, QUARTER:])
             for j in range(0, QUARTER, P):
                 half_cos = first_pass[:, :, j : j + P].rearrange("p t n -> p n t")
-                nc.gpsimd.tensor_tensor(square[:, j : j + P, :], half_cos, half_cos, ALU.mult)
+                nc.gpsimd.tensor_tensor(square[(c, a)][:, j : j + P, :], half_cos, half_cos, ALU.mult)
 
-        def features(c, a):
-            h_bf = [placed([P, QUARTER, PACK], BF16, f"h_bf{c}{a}{u}", h_bf_at, (c, a, u)) for u in range(2)]
-            h_bf_of[(c, a)] = h_bf
+        def features(c, a, quarters=(0, 1)):
+            h_bf = h_bf_of.setdefault((c, a), [None, None])
+            for u in quarters:
+                h_bf[u] = placed([P, QUARTER, PACK], BF16, f"h_bf{c}{a}{u}", h_bf_at, (c, a, u))
             for e in range(2):
-                for u in range(2):
+                for u in quarters:
                     j = u * QUARTER + e * P
-                    by_half_angle = (c, a, u) == (1, 1, 0)
+                    by_half_angle = (c, u) == (1, 0)
                     repeats = 2 if by_half_angle else 1
                     q_bank = vector_banks[2 * e + u][:].rearrange("p (t n) -> p t n", n=P)
                     for t in range(PACK):
@@ -275,7 +279,7 @@ def tile_list_fourier_landmark_block_kernel(
                     if by_half_angle:
                         nc.vector.scalar_tensor_tensor(
                             out,
-                            square[:, j : j + P, :],
+                            square[(c, a)][:, j : j + P, :],
                             0.5,
                             q_bank.rearrange("p t n -> p n t"),
                             ALU.subtract,
@@ -375,7 +379,7 @@ def tile_list_fourier_landmark_block_kernel(
         nc.vector.tensor_copy(v2_s_picked[:], tab2_s[:].indirect(idx2[:]))
         round_w1(1, 0, gpsimd_cast)
         nc.gpsimd.tensor_tensor(mu_wh[:], mu_sb[:], wh_sb[:], ALU.mult)
-        nc.gpsimd.tensor_scalar(half_phase[:], b_sb[:, 1, :], 0.5, math.pi / 2, ALU.mult, ALU.add)
+        nc.gpsimd.tensor_scalar(half_phase[:], b_sb[:], 0.5, math.pi / 2, ALU.mult, ALU.add)
         nc.gpsimd.tensor_scalar(shift[:], mu_wh[:], -1.0, 0.0, ALU.mult, ALU.add)
         quantize_w1(1, 1)
         deal(nc.vector.tensor_copy, v2_s_dealt[:], v2_s_picked[:])
@@ -384,10 +388,11 @@ def tile_list_fourier_landmark_block_kernel(
         cosines(0, 0)
         features(0, 0)
         quantize_h(0, 0)
-        cosines(1, 0)
-        features(1, 0)
+        mixed_cosines(1, 0)
+        features(1, 0, [1])
         for a in range(PASSES):
             gather_v2_words(0, a)
+        features(1, 0, [0])
         cosines(0, 1)
         features(0, 1)
         quantize_h(0, 1)

@@ -146,11 +146,8 @@ def tile_list_fourier_landmark_block_kernel(
         h_s = {(c, a): kept([P, HALF], U8, f"h_s{c}{a}") for c in range(2) for a in range(PASSES)}
         mu_wh = shared([P, GROUPS, PACK], F32, "mu_wh", AT_MU_WH)
         shift = kept([P, GROUPS, PACK], F32, "shift")
-        square = {
-            (1, 0): shared([P, QUARTER, PACK], F32, "square10", AT_PICKED),
-            (1, 1): shared([P, QUARTER, PACK], F32, "square11", AT_SQUARE),
-        }
-        half_phase = kept([P, PASSES, PACK], F32, "half_phase")
+        square = shared([P, QUARTER, PACK], F32, "square", AT_PICKED)
+        half_phase = kept([P, PACK], F32, "half_phase")
         y_s = kept([P, GROUPS, S], U8, "y_s")
         y_w = [kept([P, GROUPS, HALF], U32, f"y_w{c}") for c in range(2)]
         y_at = {(1, g): AT_TAB2 + g * PANEL_BYTES for g in range(GROUPS)}
@@ -176,10 +173,14 @@ def tile_list_fourier_landmark_block_kernel(
 
         def round_w1(a, u, cast, ts=slice(0, PACK)):
             count = P // len(w1_raw[a])
-            cast(
-                w1_bf[a][:, ts, u * count : (u + 1) * count, :].rearrange("p t m j -> p m t j"),
-                w1_raw[a][u][:].rearrange("p j (m t) -> p m t j", t=PACK)[:, :, ts, :],
-            )
+            out = w1_bf[a][:, ts, u * count : (u + 1) * count, :]
+            if cast is gpsimd_cast:
+                cast(out, w1_raw[a][u][:].rearrange("p j (m t) -> p t m j", t=PACK)[:, ts, :, :])
+            else:
+                cast(
+                    out.rearrange("p t m j -> p m t j"),
+                    w1_raw[a][u][:].rearrange("p j (m t) -> p m t j", t=PACK)[:, :, ts, :],
+                )
 
         def quantize_w1(a, pieces):
             width = PASS // pieces
@@ -243,7 +244,7 @@ def tile_list_fourier_landmark_block_kernel(
                 project(c, a, t)
                 bank = scalar_banks[t]
                 nc.scalar.activation(
-                    first_pass[:, t, :QUARTER], bank[:, :QUARTER], ACT.Sin, bias=half_phase[:, a, t : t + 1], scale=0.5
+                    first_pass[:, t, :QUARTER], bank[:, :QUARTER], ACT.Sin, bias=half_phase[:, t : t + 1], scale=0.5
                 )
                 nc.scalar.activation(
                     first_pass[:, t, QUARTER:], bank[:, QUARTER:], ACT.Abs, bias=b_sb[:, a, t : t + 1]
@@ -251,7 +252,7 @@ def tile_list_fourier_landmark_block_kernel(
             cos_of_distance(cos[:, :, QUARTER:], first_pass[:, :, QUARTER:])
             for j in range(0, QUARTER, P):
                 half_cos = first_pass[:, :, j : j + P].rearrange("p t n -> p n t")
-                nc.gpsimd.tensor_tensor(square[(c, a)][:, j : j + P, :], half_cos, half_cos, ALU.mult)
+                nc.gpsimd.tensor_tensor(square[:, j : j + P, :], half_cos, half_cos, ALU.mult)
 
         def features(c, a, quarters=(0, 1)):
             h_bf = h_bf_of.setdefault((c, a), [None, None])
@@ -260,7 +261,7 @@ def tile_list_fourier_landmark_block_kernel(
             for e in range(2):
                 for u in quarters:
                     j = u * QUARTER + e * P
-                    by_half_angle = (c, u) == (1, 0)
+                    by_half_angle = (c, a, u) == (1, 0, 0)
                     repeats = 2 if by_half_angle else 1
                     q_bank = vector_banks[2 * e + u][:].rearrange("p (t n) -> p t n", n=P)
                     for t in range(PACK):
@@ -279,7 +280,7 @@ def tile_list_fourier_landmark_block_kernel(
                     if by_half_angle:
                         nc.vector.scalar_tensor_tensor(
                             out,
-                            square[(c, a)][:, j : j + P, :],
+                            square[:, j : j + P, :],
                             0.5,
                             q_bank.rearrange("p t n -> p n t"),
                             ALU.subtract,
@@ -330,7 +331,7 @@ def tile_list_fourier_landmark_block_kernel(
 
         def round_y(c, g, u, cast):
             if (c, g) == (0, 1):
-                y_bf = shared([P, QUARTER, PACK], BF16, f"y_bf01{u}", AT_SQUARE + u * QUARTER_BF_BYTES)
+                y_bf = shared([P, QUARTER, PACK], BF16, f"y_bf01{u}", AT_COS11 + WORDS_BYTES + u * QUARTER_BF_BYTES)
             else:
                 y_bf = rounded.tile([P, QUARTER, PACK], BF16, name="y_bf", tag=f"y_bf{u}", align_bytes=64)
             y_bf_of[(c, g, u)] = y_bf
@@ -379,7 +380,7 @@ def tile_list_fourier_landmark_block_kernel(
         nc.vector.tensor_copy(v2_s_picked[:], tab2_s[:].indirect(idx2[:]))
         round_w1(1, 0, gpsimd_cast)
         nc.gpsimd.tensor_tensor(mu_wh[:], mu_sb[:], wh_sb[:], ALU.mult)
-        nc.gpsimd.tensor_scalar(half_phase[:], b_sb[:], 0.5, math.pi / 2, ALU.mult, ALU.add)
+        nc.gpsimd.tensor_scalar(half_phase[:], b_sb[:, 0, :], 0.5, math.pi / 2, ALU.mult, ALU.add)
         nc.gpsimd.tensor_scalar(shift[:], mu_wh[:], -1.0, 0.0, ALU.mult, ALU.add)
         quantize_w1(1, 1)
         deal(nc.vector.tensor_copy, v2_s_dealt[:], v2_s_picked[:])
@@ -399,7 +400,7 @@ def tile_list_fourier_landmark_block_kernel(
         for g in range(1, GROUPS):
             for a in reversed(range(PASSES)):
                 gather_v2_words(g, a)
-        mixed_cosines(1, 1)
+        cosines(1, 1)
         panel(0, 0)
         features(1, 1)
         for a in range(PASSES):

@@ -76,8 +76,9 @@ def tile_list_fourier_landmark_block_kernel(
         tab_s = kept([P, T], U8, "tab_s")
         w4_s_raw = shared([P, H], U8, "w4_s_raw", AT_W1_BF)
         tab2_s = kept([P, T2], U8, "tab2_s")
-        nc.gpsimd.memset(warm[:, 0:1], 0.0)
-        for plane in (tab_s, w4_s_raw, tab2_s):
+        nc.gpsimd.memset(tab_s[:].bitcast(I32), 0)
+        nc.vector.memset(warm[:, 0:1], 0.0)
+        for plane in (w4_s_raw, tab2_s):
             nc.vector.memset(plane[:].bitcast(I32), 0)
         nc.scalar.activation(warm[:, 1:2], warm[:, 0:1], ACT.Sin)
 
@@ -137,21 +138,25 @@ def tile_list_fourier_landmark_block_kernel(
         for g in range(1, GROUPS):
             for a in range(PASSES):
                 v2_w[(g, a)] = shared([P, PACK, P], U32, f"v2_w{g}{a}", AT_COS01 + (PASSES * (g - 1) + a) * WORDS_BYTES)
-        v2_s_picked = shared([P, S2], U8, "v2_s_picked", AT_PICKED)
+        v2_s_picked = kept([P, S2], U8, "v2_s_picked")
         v2_s_dealt = shared([P, S2], U8, "v2_s_dealt", AT_W1_RAW1)
         v2_s = kept([P, S2], U8, "v2_s")
         nc.gpsimd.memset(v2_s[:].bitcast(I32), 0)
-        h_w = {(c, a): kept([P, HALF], U32, f"h_w{c}{a}") for c, a in [(0, 0), (0, 1), (1, 1)]}
+        h_w = {(c, a): kept([P, HALF], U32, f"h_w{c}{a}") for c, a in [(0, 1), (1, 1)]}
+        h_w[(0, 0)] = shared([P, HALF], U32, "h_w00", AT_W1_BF)
         h_w[(1, 0)] = shared([P, HALF], U32, "h_w10", AT_COS11)
         h_s = {(c, a): kept([P, HALF], U8, f"h_s{c}{a}") for c in range(2) for a in range(PASSES)}
         mu_wh = shared([P, GROUPS, PACK], F32, "mu_wh", AT_MU_WH)
         shift = kept([P, GROUPS, PACK], F32, "shift")
-        square = shared([P, QUARTER, PACK], F32, "square", AT_PICKED)
-        half_phase = kept([P, PACK], F32, "half_phase")
+        square = {
+            (1, 0): shared([P, QUARTER, PACK], F32, "square10", AT_PICKED),
+            (1, 1): shared([P, QUARTER, PACK], F32, "square11", AT_SQUARE),
+        }
+        half_phase = kept([P, PASSES, PACK], F32, "half_phase")
         y_s = kept([P, GROUPS, S], U8, "y_s")
         y_w = [kept([P, GROUPS, HALF], U32, f"y_w{c}") for c in range(2)]
         y_at = {(1, g): AT_TAB2 + g * PANEL_BYTES for g in range(GROUPS)}
-        h_bf_at = {(1, 0, 0): AT_H01, (0, 1, 1): AT_H01 + QUARTER_BF_BYTES}
+        h_bf_at = {(1, 0, 0): AT_H01, (0, 1, 1): AT_H01 + QUARTER_BF_BYTES, (0, 0, 1): AT_PICKED}
         cos_of, h_bf_of, y_of, y_bf_of = {}, {}, {}, {}
 
         def placed(shape, dtype, name, offsets, key):
@@ -230,10 +235,10 @@ def tile_list_fourier_landmark_block_kernel(
             for t in range(PACK):
                 project(c, a, t)
                 nc.scalar.activation(dist[:, t, :], scalar_banks[t][:], ACT.Abs, bias=b_sb[:, a, t : t + 1])
-            for e in range(2):
+            for e, ts in [(0, slice(0, PACK - 1)), (0, slice(PACK - 1, PACK)), (1, slice(0, PACK))]:
                 cos_of_distance(
-                    cos[:].rearrange("p t (u e n) -> p (t u) e n", e=2, n=P)[:, :, e, :],
-                    dist[:].rearrange("p t (u e n) -> p (t u) e n", e=2, n=P)[:, :, e, :],
+                    cos[:, ts, :].rearrange("p t (u e n) -> p (t u) e n", e=2, n=P)[:, :, e, :],
+                    dist[:, ts, :].rearrange("p t (u e n) -> p (t u) e n", e=2, n=P)[:, :, e, :],
                 )
 
         def mixed_cosines(c, a):
@@ -244,15 +249,16 @@ def tile_list_fourier_landmark_block_kernel(
                 project(c, a, t)
                 bank = scalar_banks[t]
                 nc.scalar.activation(
-                    first_pass[:, t, :QUARTER], bank[:, :QUARTER], ACT.Sin, bias=half_phase[:, t : t + 1], scale=0.5
+                    first_pass[:, t, :QUARTER], bank[:, :QUARTER], ACT.Sin, bias=half_phase[:, a, t : t + 1], scale=0.5
                 )
                 nc.scalar.activation(
                     first_pass[:, t, QUARTER:], bank[:, QUARTER:], ACT.Abs, bias=b_sb[:, a, t : t + 1]
                 )
-            cos_of_distance(cos[:, :, QUARTER:], first_pass[:, :, QUARTER:])
+            for ts in [slice(0, PACK - 1), slice(PACK - 1, PACK)]:
+                cos_of_distance(cos[:, ts, QUARTER:], first_pass[:, ts, QUARTER:])
             for j in range(0, QUARTER, P):
                 half_cos = first_pass[:, :, j : j + P].rearrange("p t n -> p n t")
-                nc.gpsimd.tensor_tensor(square[:, j : j + P, :], half_cos, half_cos, ALU.mult)
+                nc.gpsimd.tensor_tensor(square[(c, a)][:, j : j + P, :], half_cos, half_cos, ALU.mult)
 
         def features(c, a, quarters=(0, 1)):
             h_bf = h_bf_of.setdefault((c, a), [None, None])
@@ -261,7 +267,7 @@ def tile_list_fourier_landmark_block_kernel(
             for e in range(2):
                 for u in quarters:
                     j = u * QUARTER + e * P
-                    by_half_angle = (c, a, u) == (1, 0, 0)
+                    by_half_angle = (c, u) == (1, 0)
                     repeats = 2 if by_half_angle else 1
                     q_bank = vector_banks[2 * e + u][:].rearrange("p (t n) -> p t n", n=P)
                     for t in range(PACK):
@@ -280,7 +286,7 @@ def tile_list_fourier_landmark_block_kernel(
                     if by_half_angle:
                         nc.vector.scalar_tensor_tensor(
                             out,
-                            square[:, j : j + P, :],
+                            square[(c, a)][:, j : j + P, :],
                             0.5,
                             q_bank.rearrange("p t n -> p n t"),
                             ALU.subtract,
@@ -331,7 +337,7 @@ def tile_list_fourier_landmark_block_kernel(
 
         def round_y(c, g, u, cast):
             if (c, g) == (0, 1):
-                y_bf = shared([P, QUARTER, PACK], BF16, f"y_bf01{u}", AT_COS11 + WORDS_BYTES + u * QUARTER_BF_BYTES)
+                y_bf = shared([P, QUARTER, PACK], BF16, f"y_bf01{u}", AT_SQUARE + u * QUARTER_BF_BYTES)
             else:
                 y_bf = rounded.tile([P, QUARTER, PACK], BF16, name="y_bf", tag=f"y_bf{u}", align_bytes=64)
             y_bf_of[(c, g, u)] = y_bf
@@ -380,7 +386,7 @@ def tile_list_fourier_landmark_block_kernel(
         nc.vector.tensor_copy(v2_s_picked[:], tab2_s[:].indirect(idx2[:]))
         round_w1(1, 0, gpsimd_cast)
         nc.gpsimd.tensor_tensor(mu_wh[:], mu_sb[:], wh_sb[:], ALU.mult)
-        nc.gpsimd.tensor_scalar(half_phase[:], b_sb[:, 0, :], 0.5, math.pi / 2, ALU.mult, ALU.add)
+        nc.gpsimd.tensor_scalar(half_phase[:], b_sb[:], 0.5, math.pi / 2, ALU.mult, ALU.add)
         nc.gpsimd.tensor_scalar(shift[:], mu_wh[:], -1.0, 0.0, ALU.mult, ALU.add)
         quantize_w1(1, 1)
         deal(nc.vector.tensor_copy, v2_s_dealt[:], v2_s_picked[:])
@@ -400,7 +406,7 @@ def tile_list_fourier_landmark_block_kernel(
         for g in range(1, GROUPS):
             for a in reversed(range(PASSES)):
                 gather_v2_words(g, a)
-        cosines(1, 1)
+        mixed_cosines(1, 1)
         panel(0, 0)
         features(1, 1)
         for a in range(PASSES):

@@ -150,13 +150,12 @@ def tile_list_fourier_landmark_block_kernel(
         shift = kept([P, GROUPS, PACK], F32, "shift")
         square = {
             (1, 0): shared([P, QUARTER, PACK], F32, "square10", AT_PICKED),
-            (1, 1): shared([P, QUARTER, PACK], F32, "square11", AT_SQUARE),
         }
         half_phase = kept([P, PASSES, PACK], F32, "half_phase")
         y_s = kept([P, GROUPS, S], U8, "y_s")
         y_w = [kept([P, GROUPS, HALF], U32, f"y_w{c}") for c in range(2)]
         y_at = {(1, g): AT_TAB2 + g * PANEL_BYTES for g in range(GROUPS)}
-        h_bf_at = {(1, 0, 0): AT_H01, (0, 1, 1): AT_H01 + QUARTER_BF_BYTES, (0, 0, 1): AT_PICKED}
+        h_bf_at = {(0, 1, 0): AT_H01, (0, 1, 1): AT_H01 + QUARTER_BF_BYTES, (0, 0, 1): AT_PICKED}
         cos_of, h_bf_of, y_of, y_bf_of = {}, {}, {}, {}
 
         def placed(shape, dtype, name, offsets, key):
@@ -260,16 +259,16 @@ def tile_list_fourier_landmark_block_kernel(
                 half_cos = first_pass[:, :, j : j + P].rearrange("p t n -> p n t")
                 nc.gpsimd.tensor_tensor(square[(c, a)][:, j : j + P, :], half_cos, half_cos, ALU.mult)
 
-        def features(c, a, quarters=(0, 1)):
+        def features(c, a, quarters=(0, 1), bank_of=lambda e, u: 2 * e + u):
             h_bf = h_bf_of.setdefault((c, a), [None, None])
             for u in quarters:
                 h_bf[u] = placed([P, QUARTER, PACK], BF16, f"h_bf{c}{a}{u}", h_bf_at, (c, a, u))
             for e in range(2):
                 for u in quarters:
                     j = u * QUARTER + e * P
-                    by_half_angle = (c, u) == (1, 0)
+                    by_half_angle = (c, a, u) == (1, 0, 0)
                     repeats = 2 if by_half_angle else 1
-                    q_bank = vector_banks[2 * e + u][:].rearrange("p (t n) -> p t n", n=P)
+                    q_bank = vector_banks[bank_of(e, u)][:].rearrange("p (t n) -> p t n", n=P)
                     for t in range(PACK):
                         col = a * PASS + t * P
                         for repeat in range(repeats):
@@ -337,7 +336,7 @@ def tile_list_fourier_landmark_block_kernel(
 
         def round_y(c, g, u, cast):
             if (c, g) == (0, 1):
-                y_bf = shared([P, QUARTER, PACK], BF16, f"y_bf01{u}", AT_SQUARE + u * QUARTER_BF_BYTES)
+                y_bf = shared([P, QUARTER, PACK], BF16, f"y_bf01{u}", AT_COS11 + WORDS_BYTES + u * QUARTER_BF_BYTES)
             else:
                 y_bf = rounded.tile([P, QUARTER, PACK], BF16, name="y_bf", tag=f"y_bf{u}", align_bytes=64)
             y_bf_of[(c, g, u)] = y_bf
@@ -399,16 +398,16 @@ def tile_list_fourier_landmark_block_kernel(
         features(1, 0, [1])
         for a in range(PASSES):
             gather_v2_words(0, a)
-        features(1, 0, [0])
         cosines(0, 1)
         features(0, 1)
         quantize_h(0, 1)
+        cosines(1, 1)
+        panel(0, 0)
+        features(1, 0, [0], lambda e, u: e)
         for g in range(1, GROUPS):
             for a in reversed(range(PASSES)):
                 gather_v2_words(g, a)
-        mixed_cosines(1, 1)
-        panel(0, 0)
-        features(1, 1)
+        features(1, 1, bank_of=lambda e, u: (2 + 2 * e + u) % PACK)
         for a in range(PASSES):
             quantize_h(1, a)
 

@@ -35,12 +35,11 @@ AT_W1_RAW0 = 0
 AT_W1_RAW1 = 4 * KB
 AT_MU_WH = 6 * KB
 AT_H01 = 3 * KB
-AT_SQUARE = 5 * KB
 AT_COS11 = 12 * KB
 AT_TAB2 = 20 * KB
 AT_W1_BF = 52 * KB
-AT_PICKED = 64 * KB
 AT_COS01 = 56 * KB
+AT_SQUARE = 64 * KB
 QUARTER_BF_BYTES = QUARTER * PACK * 2
 WORDS_BYTES = PASS * 4
 PANEL_BYTES = PACK * HALF * 4
@@ -137,7 +136,8 @@ def tile_list_fourier_landmark_block_kernel(
         v2_w = {(0, a): kept([P, PACK, P], U32, f"v2_w0{a}") for a in range(PASSES)}
         for g in range(1, GROUPS):
             for a in range(PASSES):
-                v2_w[(g, a)] = shared([P, PACK, P], U32, f"v2_w{g}{a}", AT_COS01 + (PASSES * (g - 1) + a) * WORDS_BYTES)
+                at = AT_COS01 + (PASSES * (g - 1) + a) * WORDS_BYTES
+                v2_w[(g, a)] = shared([P, PACK, P], U32, f"v2_w{g}{a}", at)
         v2_s_picked = kept([P, S2], U8, "v2_s_picked")
         v2_s_dealt = shared([P, S2], U8, "v2_s_dealt", AT_W1_RAW1)
         v2_s = kept([P, S2], U8, "v2_s")
@@ -148,14 +148,12 @@ def tile_list_fourier_landmark_block_kernel(
         h_s = {(c, a): kept([P, HALF], U8, f"h_s{c}{a}") for c in range(2) for a in range(PASSES)}
         mu_wh = shared([P, GROUPS, PACK], F32, "mu_wh", AT_MU_WH)
         shift = kept([P, GROUPS, PACK], F32, "shift")
-        square = {
-            (1, 0): shared([P, QUARTER, PACK], F32, "square10", AT_PICKED),
-        }
-        half_phase = kept([P, PASSES, PACK], F32, "half_phase")
+        square = shared([P, QUARTER, PACK], F32, "square", AT_SQUARE)
+        half_phase = kept([P, PACK], F32, "half_phase")
         y_s = kept([P, GROUPS, S], U8, "y_s")
         y_w = [kept([P, GROUPS, HALF], U32, f"y_w{c}") for c in range(2)]
         y_at = {(1, g): AT_TAB2 + g * PANEL_BYTES for g in range(GROUPS)}
-        h_bf_at = {(0, 1, 0): AT_H01, (0, 1, 1): AT_H01 + QUARTER_BF_BYTES, (0, 0, 1): AT_PICKED}
+        h_bf_at = {(0, 1, 0): AT_H01, (0, 1, 1): AT_H01 + QUARTER_BF_BYTES, (0, 0, 1): AT_SQUARE}
         cos_of, h_bf_of, y_of, y_bf_of = {}, {}, {}, {}
 
         def placed(shape, dtype, name, offsets, key):
@@ -205,13 +203,14 @@ def tile_list_fourier_landmark_block_kernel(
             )
 
         def place_v2_scales():
-            moves = [(a, quad) for a in range(PASSES) for quad in range(QUADRANTS)]
-            for a, quad in moves:
-                src = BLOCKS * a + SCALE_ROWS * quad
-                dst = QUADRANT * quad + SCALE_ROWS * a
-                nc.sync.dma_start(
-                    v2_s[dst : dst + SCALE_ROWS, :].bitcast(I32), v2_s_dealt[src : src + SCALE_ROWS, :].bitcast(I32)
-                )
+            for a in range(PASSES):
+                for quad in range(QUADRANTS):
+                    src = BLOCKS * a + SCALE_ROWS * quad
+                    dst = QUADRANT * quad + SCALE_ROWS * a
+                    nc.sync.dma_start(
+                        v2_s[dst : dst + SCALE_ROWS, :].bitcast(I32),
+                        v2_s_dealt[src : src + SCALE_ROWS, :].bitcast(I32),
+                    )
 
         def project(c, a, t):
             nc.tensor.matmul_mx(
@@ -227,6 +226,8 @@ def tile_list_fourier_landmark_block_kernel(
         def cos_of_distance(out, in_):
             nc.scalar.activation(out, in_, ACT.Sin, bias=math.pi / 2, scale=-1.0)
 
+        early_t, last_t, all_t = slice(0, PACK - 1), slice(PACK - 1, PACK), slice(0, PACK)
+
         def cosines(c, a):
             dist = work.tile([P, PACK, HALF], F32, name="dist", tag="dist")
             cos = placed([P, PACK, HALF], F32, f"cos{c}{a}", cos_at, (c, a))
@@ -234,7 +235,7 @@ def tile_list_fourier_landmark_block_kernel(
             for t in range(PACK):
                 project(c, a, t)
                 nc.scalar.activation(dist[:, t, :], scalar_banks[t][:], ACT.Abs, bias=b_sb[:, a, t : t + 1])
-            for e, ts in [(0, slice(0, PACK - 1)), (0, slice(PACK - 1, PACK)), (1, slice(0, PACK))]:
+            for e, ts in [(0, early_t), (0, last_t), (1, all_t)]:
                 cos_of_distance(
                     cos[:, ts, :].rearrange("p t (u e n) -> p (t u) e n", e=2, n=P)[:, :, e, :],
                     dist[:, ts, :].rearrange("p t (u e n) -> p (t u) e n", e=2, n=P)[:, :, e, :],
@@ -242,62 +243,62 @@ def tile_list_fourier_landmark_block_kernel(
 
         def mixed_cosines(c, a):
             first_pass = work.tile([P, PACK, HALF], F32, name="dist", tag="dist")
-            cos = placed([P, PACK, HALF], F32, f"cos{c}{a}", cos_at, (c, a))
+            cos = kept([P, PACK, HALF], F32, f"cos{c}{a}")
             cos_of[(c, a)] = cos
             for t in range(PACK):
                 project(c, a, t)
                 bank = scalar_banks[t]
                 nc.scalar.activation(
-                    first_pass[:, t, :QUARTER], bank[:, :QUARTER], ACT.Sin, bias=half_phase[:, a, t : t + 1], scale=0.5
+                    first_pass[:, t, :QUARTER], bank[:, :QUARTER], ACT.Sin, bias=half_phase[:, t : t + 1], scale=0.5
                 )
                 nc.scalar.activation(
                     first_pass[:, t, QUARTER:], bank[:, QUARTER:], ACT.Abs, bias=b_sb[:, a, t : t + 1]
                 )
-            for ts in [slice(0, PACK - 1), slice(PACK - 1, PACK)]:
+            for ts in [early_t, last_t]:
                 cos_of_distance(cos[:, ts, QUARTER:], first_pass[:, ts, QUARTER:])
             for j in range(0, QUARTER, P):
                 half_cos = first_pass[:, :, j : j + P].rearrange("p t n -> p n t")
-                nc.gpsimd.tensor_tensor(square[(c, a)][:, j : j + P, :], half_cos, half_cos, ALU.mult)
+                nc.gpsimd.tensor_tensor(square[:, j : j + P, :], half_cos, half_cos, ALU.mult)
 
-        def features(c, a, quarters=(0, 1), bank_of=lambda e, u: 2 * e + u):
+        def features(c, a, quarters, q_banks):
             h_bf = h_bf_of.setdefault((c, a), [None, None])
             for u in quarters:
                 h_bf[u] = placed([P, QUARTER, PACK], BF16, f"h_bf{c}{a}{u}", h_bf_at, (c, a, u))
-            for e in range(2):
-                for u in quarters:
-                    j = u * QUARTER + e * P
-                    by_half_angle = (c, a, u) == (1, 0, 0)
-                    repeats = 2 if by_half_angle else 1
-                    q_bank = vector_banks[bank_of(e, u)][:].rearrange("p (t n) -> p t n", n=P)
-                    for t in range(PACK):
-                        col = a * PASS + t * P
-                        for repeat in range(repeats):
-                            nc.tensor.matmul_mx(
-                                out=q_bank[:, t, :],
-                                lhsT=w4_w[:, 2 * col : 2 * (col + P)].bitcast(E2M1),
-                                lhsT_scale=w4_s[:, col : col + P],
-                                rhs=v_w[c][:, j : j + P].bitcast(E4M3),
-                                rhs_scale=v_s[:, c * HALF + j : c * HALF + j + P],
-                                start=(repeat == 0),
-                                stop=(repeat == repeats - 1),
-                            )
-                    out = h_bf[u][:, e * P : (e + 1) * P, :]
-                    if by_half_angle:
-                        nc.vector.scalar_tensor_tensor(
-                            out,
-                            square[(c, a)][:, j : j + P, :],
-                            0.5,
-                            q_bank.rearrange("p t n -> p n t"),
-                            ALU.subtract,
-                            ALU.mult,
+            pieces = [(e, u) for e in range(2) for u in quarters]
+            for bank, (e, u) in zip(q_banks, pieces):
+                j = u * QUARTER + e * P
+                by_half_angle = (c, a, u) == (1, 0, 0)
+                repeats = 2 if by_half_angle else 1
+                q_bank = bank[:].rearrange("p (t n) -> p t n", n=P)
+                for t in range(PACK):
+                    col = a * PASS + t * P
+                    for repeat in range(repeats):
+                        nc.tensor.matmul_mx(
+                            out=q_bank[:, t, :],
+                            lhsT=w4_w[:, 2 * col : 2 * (col + P)].bitcast(E2M1),
+                            lhsT_scale=w4_s[:, col : col + P],
+                            rhs=v_w[c][:, j : j + P].bitcast(E4M3),
+                            rhs_scale=v_s[:, c * HALF + j : c * HALF + j + P],
+                            start=(repeat == 0),
+                            stop=(repeat == repeats - 1),
                         )
-                    else:
-                        nc.vector.tensor_tensor(
-                            out.rearrange("p (n i) t -> p n t i", i=WALK),
-                            q_bank.rearrange("p t (n i) -> p n t i", i=WALK),
-                            cos_of[(c, a)][:, :, j : j + P].rearrange("p t (n i) -> p n t i", i=WALK),
-                            ALU.mult,
-                        )
+                out = h_bf[u][:, e * P : (e + 1) * P, :]
+                if by_half_angle:
+                    nc.vector.scalar_tensor_tensor(
+                        out,
+                        square[:, j : j + P, :],
+                        0.5,
+                        q_bank.rearrange("p t n -> p n t"),
+                        ALU.subtract,
+                        ALU.mult,
+                    )
+                else:
+                    nc.vector.tensor_tensor(
+                        out.rearrange("p (n i) t -> p n t i", i=WALK),
+                        q_bank.rearrange("p t (n i) -> p n t i", i=WALK),
+                        cos_of[(c, a)][:, :, j : j + P].rearrange("p t (n i) -> p n t i", i=WALK),
+                        ALU.mult,
+                    )
 
         def quantize_h(c, a):
             for u, h_bf in enumerate(h_bf_of[(c, a)]):
@@ -385,29 +386,29 @@ def tile_list_fourier_landmark_block_kernel(
         nc.vector.tensor_copy(v2_s_picked[:], tab2_s[:].indirect(idx2[:]))
         round_w1(1, 0, gpsimd_cast)
         nc.gpsimd.tensor_tensor(mu_wh[:], mu_sb[:], wh_sb[:], ALU.mult)
-        nc.gpsimd.tensor_scalar(half_phase[:], b_sb[:], 0.5, math.pi / 2, ALU.mult, ALU.add)
+        nc.gpsimd.tensor_scalar(half_phase[:], b_sb[:, 0, :], 0.5, math.pi / 2, ALU.mult, ALU.add)
         nc.gpsimd.tensor_scalar(shift[:], mu_wh[:], -1.0, 0.0, ALU.mult, ALU.add)
         quantize_w1(1, 1)
         deal(nc.vector.tensor_copy, v2_s_dealt[:], v2_s_picked[:])
         place_v2_scales()
 
         cosines(0, 0)
-        features(0, 0)
+        features(0, 0, [0, 1], vector_banks)
         quantize_h(0, 0)
         mixed_cosines(1, 0)
-        features(1, 0, [1])
+        features(1, 0, [1], vector_banks[1::2])
         for a in range(PASSES):
             gather_v2_words(0, a)
         cosines(0, 1)
-        features(0, 1)
+        features(0, 1, [0, 1], vector_banks)
         quantize_h(0, 1)
         cosines(1, 1)
         panel(0, 0)
-        features(1, 0, [0], lambda e, u: e)
+        features(1, 0, [0], vector_banks[:2])
         for g in range(1, GROUPS):
             for a in reversed(range(PASSES)):
                 gather_v2_words(g, a)
-        features(1, 1, bank_of=lambda e, u: (2 + 2 * e + u) % PACK)
+        features(1, 1, [0, 1], vector_banks[2:] + vector_banks[:2])
         for a in range(PASSES):
             quantize_h(1, a)
 

import math
from contextlib import ExitStack

import concourse.mybir as mybir

K, H, T, S, T2, S2 = 512, 1024, 2048, 1024, 4096, 1536
FLOPS = 2 * (2 * K * H * S + H * S2 * S)

F32 = mybir.dt.float32
BF16 = mybir.dt.bfloat16
I32 = mybir.dt.int32
U32 = mybir.dt.uint32
U16 = mybir.dt.uint16
U8 = mybir.dt.uint8
E4M3 = mybir.dt.float8_e4m3fn_x4
E2M1 = mybir.dt.float4_e2m1fn_x4
ACT = mybir.ActivationFunctionType
ALU = mybir.AluOpType

P = 128
PACK = 4
PASS = P * PACK
PASSES = H // PASS
GROUPS = S2 // PASS
HALF = S // 2
QUARTER = HALF // 2
QUADRANTS = 4
QUADRANT = P // QUADRANTS
SCALE_ROWS = 4
BLOCKS = QUADRANTS * SCALE_ROWS
LIST_ROWS = 16

KB = 1024
AT_W1_RAW0 = 0
AT_W1_RAW1 = 4 * KB
AT_MU_WH = 6 * KB
AT_H01 = 3 * KB
AT_COS11 = 12 * KB
AT_TAB2 = 20 * KB
AT_W1_BF = 52 * KB
AT_COS01 = 56 * KB
AT_SQUARE = 64 * KB
QUARTER_BF_BYTES = QUARTER * PACK * 2
WORDS_BYTES = PASS * 4
PANEL_BYTES = PACK * HALF * 4
WALK = 4


def tile_list_fourier_landmark_block_kernel(
    tc, tab_words, tab_scales, tab2_words, tab2_scales, offs, offs2, w1, w4_words, w4_scales, b, mu, wh,
    out_0, out_1, out_2,
):
    nc = tc.nc
    with ExitStack() as ctx:
        lists = ctx.enter_context(tc.tile_pool(name="lists", bufs=1))
        keep = ctx.enter_context(tc.tile_pool(name="keep", bufs=1))
        work = ctx.enter_context(tc.tile_pool(name="work", bufs=3))
        rounded = ctx.enter_context(tc.tile_pool(name="rounded", bufs=3))
        reuse = ctx.enter_context(tc.tile_pool(name="reuse", bufs=1))
        psum = ctx.enter_context(tc.psum_pool(name="psum", bufs=1))

        def kept(shape, dtype, name):
            return keep.tile(shape, dtype, name=name, align_bytes=64)

        def shared(shape, dtype, name, offset):
            return reuse.tile(shape, dtype, name=name, align_bytes=64, offset=offset)

        idx = lists.tile([P, S // LIST_ROWS], U16, name="idx")
        idx2 = lists.tile([P, S2 // LIST_ROWS], U16, name="idx2")

        banks = [psum.tile([P, PASS], F32, name=f"bank{i}") for i in range(2 * PACK)]
        scalar_banks, vector_banks = banks[:PACK], banks[PACK:]

        warm = kept([P, 2], F32, "warm")
        tab_s = kept([P, T], U8, "tab_s")
        w4_s_raw = shared([P, H], U8, "w4_s_raw", AT_W1_BF)
        tab2_s = kept([P, T2], U8, "tab2_s")
        nc.gpsimd.memset(tab_s[:].bitcast(I32), 0)
        nc.vector.memset(warm[:, 0:1], 0.0)
        for plane in (w4_s_raw, tab2_s):
            nc.vector.memset(plane[:].bitcast(I32), 0)
        nc.scalar.activation(warm[:, 1:2], warm[:, 0:1], ACT.Sin)

        tab_w = kept([P, T], I32, "tab_w")
        w4_w_raw = kept([P, 2 * H], U8, "w4_w_raw")
        tab2_w = [shared([P, T2], I32, f"tab2_w{a}", AT_TAB2 + a * T2 * 4) for a in range(PASSES)]
        w1_raw = [
            [kept([P, PACK, PASS // 2], F32, "w1_raw00"), shared([P, PACK, PASS // 2], F32, "w1_raw01", AT_W1_RAW0)],
            [shared([P, PACK, PASS], F32, "w1_raw1", AT_W1_RAW1)],
        ]
        b_sb = kept([P, PASSES, PACK], F32, "b_sb")
        mu_sb = kept([P, GROUPS, PACK], F32, "mu_sb")
        wh_sb = kept([P, GROUPS, PACK], F32, "wh_sb")

        def load_w1(a, u, queue=nc.sync):
            width = PASS // len(w1_raw[a])
            c0 = a * PASS + u * width
            queue.dma_start(w1_raw[a][u][:], w1[:, c0 : c0 + width].rearrange("(p j) c -> p j c", j=PACK))

        def load_scale_rows(plane, scales):
            for quad in range(QUADRANTS):
                nc.sync.dma_start(
                    plane[QUADRANT * quad : QUADRANT * quad + SCALE_ROWS, :].bitcast(I32),
                    scales[0, SCALE_ROWS * quad : SCALE_ROWS * (quad + 1), :].bitcast(I32),
                )

        def load_words(tile, words):
            nc.sync.dma_start(tile[:], words.rearrange("p n i -> p (n i)").bitcast(I32))

        load_w1(0, 0, nc.scalar)
        nc.sync.dma_start(idx[:], offs)
        nc.sync.dma_start(idx2[:], offs2)
        load_scale_rows(tab_s, tab_scales)
        load_words(tab_w, tab_words[0])
        load_w1(0, 1)
        nc.sync.dma_start(w4_w_raw[:].bitcast(I32), w4_words[0].bitcast(I32))
        load_scale_rows(w4_s_raw, w4_scales)
        nc.sync.dma_start(
            tab2_s[0 : BLOCKS * PASSES, :].bitcast(I32), tab2_scales.rearrange("a q t -> (a q) t").bitcast(I32)
        )
        load_w1(1, 0)
        for a in range(PASSES):
            load_words(tab2_w[a], tab2_words[a])
        nc.gpsimd.dma_start(b_sb[:], b.rearrange("(a p t) -> p a t", p=P, t=PACK))
        nc.gpsimd.dma_start(mu_sb[:], mu.rearrange("(g p t) -> p g t", p=P, t=PACK))
        nc.gpsimd.dma_start(wh_sb[:], wh.rearrange("(g p t) -> p g t", p=P, t=PACK))

        w4_w = kept([P, 2 * H], U8, "w4_w")
        w4_s = kept([P, H], U8, "w4_s")
        v_w = [kept([P, HALF], U32, "v_w0"), shared([P, HALF], U32, "v_w1", AT_W1_RAW0)]
        v_s = kept([P, S], U8, "v_s")
        w1_bf = [kept([P, PACK, P, PACK], BF16, "w1_bf0"), shared([P, PACK, P, PACK], BF16, "w1_bf1", AT_W1_BF)]
        w1_w = [kept([P, PASS], U32, f"w1_w{a}") for a in range(PASSES)]
        w1_s = [kept([P, PASS], U8, f"w1_s{a}") for a in range(PASSES)]
        cos_at = {(0, 1): AT_COS01, (1, 1): AT_COS11}
        v2_w = {(0, a): kept([P, PACK, P], U32, f"v2_w0{a}") for a in range(PASSES)}
        for g in range(1, GROUPS):
            for a in range(PASSES):
                at = AT_COS01 + (PASSES * (g - 1) + a) * WORDS_BYTES
                v2_w[(g, a)] = shared([P, PACK, P], U32, f"v2_w{g}{a}", at)
        v2_s_picked = kept([P, S2], U8, "v2_s_picked")
        v2_s_dealt = shared([P, S2], U8, "v2_s_dealt", AT_W1_RAW1)
        v2_s = kept([P, S2], U8, "v2_s")
        nc.gpsimd.memset(v2_s[:].bitcast(I32), 0)
        h_w = {(c, a): kept([P, HALF], U32, f"h_w{c}{a}") for c, a in [(0, 1), (1, 1)]}
        h_w[(0, 0)] = shared([P, HALF], U32, "h_w00", AT_W1_BF)
        h_w[(1, 0)] = shared([P, HALF], U32, "h_w10", AT_COS11)
        h_s = {(c, a): kept([P, HALF], U8, f"h_s{c}{a}") for c in range(2) for a in range(PASSES)}
        mu_wh = shared([P, GROUPS, PACK], F32, "mu_wh", AT_MU_WH)
        shift = kept([P, GROUPS, PACK], F32, "shift")
        square = shared([P, QUARTER, PACK], F32, "square", AT_SQUARE)
        half_phase = kept([P, PACK], F32, "half_phase")
        y_s = kept([P, GROUPS, S], U8, "y_s")
        y_w = [kept([P, GROUPS, HALF], U32, f"y_w{c}") for c in range(2)]
        y_at = {(1, g): AT_TAB2 + g * PANEL_BYTES for g in range(GROUPS)}
        h_bf_at = {(0, 1, 0): AT_H01, (0, 1, 1): AT_H01 + QUARTER_BF_BYTES, (0, 0, 1): AT_SQUARE}
        cos_of, h_bf_of, y_of, y_bf_of = {}, {}, {}, {}

        def placed(shape, dtype, name, offsets, key):
            if key in offsets:
                return shared(shape, dtype, name, offsets[key])
            return kept(shape, dtype, name)

        def entries(lst, part):
            return lst[:, part * PASS // LIST_ROWS : (part + 1) * PASS // LIST_ROWS]

        def deal(copy, out, in_):
            copy(
                out.rearrange("p (g t m) -> p t g m", t=PACK, m=P),
                in_.rearrange("p (g m t) -> p t g m", t=PACK, m=P),
            )

        def gpsimd_cast(out, in_):
            nc.gpsimd.tensor_scalar(out, in_, 1.0, 0.0, ALU.mult, ALU.add)

        def round_w1(a, u, cast, ts=slice(0, PACK)):
            count = P // len(w1_raw[a])
            out = w1_bf[a][:, ts, u * count : (u + 1) * count, :]
            if cast is gpsimd_cast:
                cast(out, w1_raw[a][u][:].rearrange("p j (m t) -> p t m j", t=PACK)[:, ts, :, :])
            else:
                cast(
                    out.rearrange("p t m j -> p m t j"),
                    w1_raw[a][u][:].rearrange("p j (m t) -> p m t j", t=PACK)[:, :, ts, :],
                )

        def quantize_w1(a, pieces):
            width = PASS // pieces
            for c0 in range(0, PASS, width):
                nc.vector.quantize_mx(
                    out=w1_w[a][:, c0 : c0 + width].bitcast(E4M3),
                    scales=w1_s[a][:, c0 : c0 + width],
                    in_=w1_bf[a][:].rearrange("p t m j -> p (t m j)")[:, PACK * c0 : PACK * (c0 + width)],
                )

        def gather_v_words(c):
            cols = HALF // LIST_ROWS
            nc.vector.tensor_copy(v_w[c][:], tab_w[:].bitcast(U32).indirect(idx[:, c * cols : (c + 1) * cols]))

        def gather_v2_words(g, a):
            nc.vector.tensor_copy(
                v2_w[(g, a)][:].rearrange("p t m -> p m t"), tab2_w[a][:].bitcast(U32).indirect(entries(idx2, g))
            )

        def place_v2_scales():
            for a in range(PASSES):
                for quad in range(QUADRANTS):
                    src = BLOCKS * a + SCALE_ROWS * quad
                    dst = QUADRANT * quad + SCALE_ROWS * a
                    nc.sync.dma_start(
                        v2_s[dst : dst + SCALE_ROWS, :].bitcast(I32),
                        v2_s_dealt[src : src + SCALE_ROWS, :].bitcast(I32),
                    )

        def project(c, a, t):
            nc.tensor.matmul_mx(
                out=scalar_banks[t][:],
                lhsT=w1_w[a][:, t * P : (t + 1) * P].bitcast(E4M3),
                lhsT_scale=w1_s[a][:, t * P : (t + 1) * P],
                rhs=v_w[c][:].bitcast(E4M3),
                rhs_scale=v_s[:, c * HALF : (c + 1) * HALF],
                start=True,
                stop=True,
            )

        def cos_of_distance(out, in_):
            nc.scalar.activation(out, in_, ACT.Sin, bias=math.pi / 2, scale=-1.0)

        early_t, last_t, all_t = slice(0, PACK - 1), slice(PACK - 1, PACK), slice(0, PACK)

        def cosines(c, a):
            dist = work.tile([P, PACK, HALF], F32, name="dist", tag="dist")
            cos = placed([P, PACK, HALF], F32, f"cos{c}{a}", cos_at, (c, a))
            cos_of[(c, a)] = cos
            for t in range(PACK):
                project(c, a, t)
                nc.scalar.activation(dist[:, t, :], scalar_banks[t][:], ACT.Abs, bias=b_sb[:, a, t : t + 1])
            for e, ts in [(0, early_t), (0, last_t), (1, all_t)]:
                cos_of_distance(
                    cos[:, ts, :].rearrange("p t (u e n) -> p (t u) e n", e=2, n=P)[:, :, e, :],
                    dist[:, ts, :].rearrange("p t (u e n) -> p (t u) e n", e=2, n=P)[:, :, e, :],
                )

        def mixed_cosines(c, a):
            first_pass = work.tile([P, PACK, HALF], F32, name="dist", tag="dist")
            cos = kept([P, PACK, HALF], F32, f"cos{c}{a}")
            cos_of[(c, a)] = cos
            for t in range(PACK):
                project(c, a, t)
                bank = scalar_banks[t]
                nc.scalar.activation(
                    first_pass[:, t, :QUARTER], bank[:, :QUARTER], ACT.Sin, bias=half_phase[:, t : t + 1], scale=0.5
                )
                nc.scalar.activation(
                    first_pass[:, t, QUARTER:], bank[:, QUARTER:], ACT.Abs, bias=b_sb[:, a, t : t + 1]
                )
            for ts in [early_t, last_t]:
                cos_of_distance(cos[:, ts, QUARTER:], first_pass[:, ts, QUARTER:])
            for j in range(0, QUARTER, P):
                half_cos = first_pass[:, :, j : j + P].rearrange("p t n -> p n t")
                nc.gpsimd.tensor_tensor(square[:, j : j + P, :], half_cos, half_cos, ALU.mult)

        def features(c, a, quarters, q_banks):
            h_bf = h_bf_of.setdefault((c, a), [None, None])
            for u in quarters:
                h_bf[u] = placed([P, QUARTER, PACK], BF16, f"h_bf{c}{a}{u}", h_bf_at, (c, a, u))
            pieces = [(e, u) for e in range(2) for u in quarters]
            for bank, (e, u) in zip(q_banks, pieces):
                j = u * QUARTER + e * P
                by_half_angle = (c, a, u) == (1, 0, 0)
                repeats = 2 if by_half_angle else 1
                q_bank = bank[:].rearrange("p (t n) -> p t n", n=P)
                for t in range(PACK):
                    col = a * PASS + t * P
                    for repeat in range(repeats):
                        nc.tensor.matmul_mx(
                            out=q_bank[:, t, :],
                            lhsT=w4_w[:, 2 * col : 2 * (col + P)].bitcast(E2M1),
                            lhsT_scale=w4_s[:, col : col + P],
                            rhs=v_w[c][:, j : j + P].bitcast(E4M3),
                            rhs_scale=v_s[:, c * HALF + j : c * HALF + j + P],
                            start=(repeat == 0),
                            stop=(repeat == repeats - 1),
                        )
                out = h_bf[u][:, e * P : (e + 1) * P, :]
                if by_half_angle:
                    nc.vector.scalar_tensor_tensor(
                        out,
                        square[:, j : j + P, :],
                        0.5,
                        q_bank.rearrange("p t n -> p n t"),
                        ALU.subtract,
                        ALU.mult,
                    )
                else:
                    nc.vector.tensor_tensor(
                        out.rearrange("p (n i) t -> p n t i", i=WALK),
                        q_bank.rearrange("p t (n i) -> p n t i", i=WALK),
                        cos_of[(c, a)][:, :, j : j + P].rearrange("p t (n i) -> p n t i", i=WALK),
                        ALU.mult,
                    )

        def quantize_h(c, a):
            for u, h_bf in enumerate(h_bf_of[(c, a)]):
                nc.vector.quantize_mx(
                    out=h_w[(c, a)][:, u * QUARTER : (u + 1) * QUARTER].bitcast(E4M3),
                    scales=h_s[(c, a)][:, u * QUARTER : (u + 1) * QUARTER],
                    in_=h_bf[:].rearrange("p n t -> p (n t)"),
                )

        def panel(c, g):
            y = placed([P, PACK, HALF], F32, f"y{c}{g}", y_at, (c, g))
            y_of[(c, g)] = y
            passes = [0, 1] if c == 1 else [1, 0]
            rows = out_0[g * PASS : (g + 1) * PASS, c * HALF : (c + 1) * HALF].rearrange("(p t) j -> p t j", t=PACK)
            for t in range(PACK):
                col = g * PASS + t * P
                for a in passes:
                    nc.tensor.matmul_mx(
                        out=scalar_banks[t][:],
                        lhsT=v2_w[(g, a)][:, t, :].bitcast(E4M3),
                        lhsT_scale=v2_s[SCALE_ROWS * a : P, col : col + P],
                        rhs=h_w[(c, a)][:].bitcast(E4M3),
                        rhs_scale=h_s[(c, a)][:],
                        start=(a == passes[0]),
                        stop=(a == passes[-1]),
                    )
                nc.scalar.activation(
                    y[:, t, :],
                    scalar_banks[t][:],
                    ACT.Identity,
                    bias=shift[:, g, t : t + 1],
                    scale=wh_sb[:, g, t : t + 1],
                )
                if t % 2 == 1:
                    nc.sync.dma_start(rows[:, t - 1 : t + 1, :], y[:, t - 1 : t + 1, :])

        def round_y(c, g, u, cast):
            if (c, g) == (0, 1):
                y_bf = shared([P, QUARTER, PACK], BF16, f"y_bf01{u}", AT_COS11 + WORDS_BYTES + u * QUARTER_BF_BYTES)
            else:
                y_bf = rounded.tile([P, QUARTER, PACK], BF16, name="y_bf", tag=f"y_bf{u}", align_bytes=64)
            y_bf_of[(c, g, u)] = y_bf
            y = y_of[(c, g)][:, :, u * QUARTER : (u + 1) * QUARTER]
            if cast is gpsimd_cast:
                cast(y_bf[:], y.rearrange("p t n -> p n t"))
            else:
                cast(y_bf[:].rearrange("p (n i) t -> p n t i", i=WALK), y.rearrange("p t (n i) -> p n t i", i=WALK))

        def quantize_y(c, g, u):
            j0 = u * QUARTER
            nc.vector.quantize_mx(
                out=y_w[c][:, g, j0 : j0 + QUARTER].bitcast(E4M3),
                scales=y_s[:, g, c * HALF + j0 : c * HALF + j0 + QUARTER],
                in_=y_bf_of[(c, g, u)][:].rearrange("p n t -> p (n t)"),
            )

        def planes(c, g, casts):
            for u in range(2):
                round_y(c, g, u, casts[u])
            for u in range(2):
                quantize_y(c, g, u)

        def store_words(c, g):
            nc.sync.dma_start(
                out_1[g, :, c * HALF : (c + 1) * HALF, :].rearrange("p n t -> p (n t)").bitcast(I32),
                y_w[c][:, g, :].bitcast(I32),
            )

        def store_scales():
            for quad in range(QUADRANTS):
                nc.sync.dma_start(
                    out_2[:, SCALE_ROWS * quad : SCALE_ROWS * (quad + 1), :].bitcast(I32).rearrange("g r n -> r g n"),
                    y_s[QUADRANT * quad : QUADRANT * quad + SCALE_ROWS, :, :].bitcast(I32),
                )

        nc.vector.tensor_copy(v_s[:], tab_s[:].indirect(idx[:]))
        gather_v_words(0)
        round_w1(0, 0, nc.scalar.copy)
        round_w1(0, 1, nc.vector.tensor_copy, slice(0, PACK // 2))
        round_w1(0, 1, nc.scalar.copy, slice(PACK // 2, PACK))
        quantize_w1(0, 2)
        gather_v_words(1)
        deal(nc.scalar.copy, w4_w[:].bitcast(U16), w4_w_raw[:].bitcast(U16))
        deal(nc.vector.tensor_copy, w4_s[:], w4_s_raw[:])
        nc.vector.tensor_copy(v2_s_picked[:], tab2_s[:].indirect(idx2[:]))
        round_w1(1, 0, gpsimd_cast)
        nc.gpsimd.tensor_tensor(mu_wh[:], mu_sb[:], wh_sb[:], ALU.mult)
        nc.gpsimd.tensor_scalar(half_phase[:], b_sb[:, 0, :], 0.5, math.pi / 2, ALU.mult, ALU.add)
        nc.gpsimd.tensor_scalar(shift[:], mu_wh[:], -1.0, 0.0, ALU.mult, ALU.add)
        quantize_w1(1, 1)
        deal(nc.vector.tensor_copy, v2_s_dealt[:], v2_s_picked[:])
        place_v2_scales()

        cosines(0, 0)
        features(0, 0, [0, 1], vector_banks)
        quantize_h(0, 0)
        mixed_cosines(1, 0)
        features(1, 0, [1], vector_banks[1::2])
        for a in range(PASSES):
            gather_v2_words(0, a)
        cosines(0, 1)
        features(0, 1, [0, 1], vector_banks)
        quantize_h(0, 1)
        cosines(1, 1)
        panel(0, 0)
        features(1, 0, [0], vector_banks[:2])
        for g in range(1, GROUPS):
            for a in reversed(range(PASSES)):
                gather_v2_words(g, a)
        features(1, 1, [0, 1], vector_banks[2:] + vector_banks[:2])
        for a in range(PASSES):
            quantize_h(1, a)

        order = [(c, g) for c in range(2) for g in range(GROUPS)]
        panel(*order[1])
        planes(*order[0], [gpsimd_cast, gpsimd_cast])
        for n in range(2, len(order)):
            panel(*order[n])
            planes(*order[n - 1], [nc.vector.tensor_copy, nc.vector.tensor_copy])
            store_words(*order[n - 2])
        planes(*order[-1], [nc.vector.tensor_copy, nc.scalar.copy])
        for done in order[-2:]:
            store_words(*done)
        store_scales()
